import numpy as np, ml_dtypes
CORES = [66,74,82,90,194,202,210,218]
N = 8
BF = ml_dtypes.bfloat16
def gentries(a):
    return np.ascontiguousarray(a.reshape(8, 16, -1).transpose(0, 2, 1)).reshape(8, -1)
def gtable(e):
    e = np.asarray(e); return np.ascontiguousarray(e.reshape(8, -1, 16).transpose(0, 2, 1)).reshape(128, -1).astype(np.int32)
V, L, D, T, RO = 4096, 224, 4, 4, 6
def rows_of(rng, a, b):
    u = np.concatenate([a, b]); w = np.concatenate([b, a])
    return w[np.argsort(u + 0.5 * rng.random(u.size))].reshape(V, D)
def graph(rng, kind):
    i = np.arange(V)
    if kind == 2:
        m = i.reshape(-1, 2, D); a = np.repeat(m[:, 0], D, axis=1).reshape(-1); b = np.tile(m[:, 1], (1, D)).reshape(-1)
    elif kind == 1:
        s = 1 + rng.permutation(V - 1)[:D]; w = i[:, None] ^ s; keep = w > i[:, None]
        a = np.repeat(i[:, None], D, axis=1)[keep]; b = w[keep]
    else:
        s = 1 + rng.permutation(V // 2 - 1)[:D // 2]; a = np.repeat(i, D // 2); b = ((i[:, None] + s) & (V - 1)).reshape(-1)
        turn = rng.random(a.size) < 0.5; a, b = np.where(turn, b, a), np.where(turn, a, b)
        o = rng.permutation(a.size); k = a.size // 2; p, q = o[:k], o[k:2 * k]
        def key(u, w): return np.minimum(u, w) * V + np.maximum(u, w)
        new = np.concatenate([key(a[p], b[q]), key(a[q], b[p])])
        z, inv, cnt = np.unique(new, return_inverse=True, return_counts=True)
        no = np.isin(new, key(a, b)) | (cnt[inv.reshape(-1)] > 1); no = no[:k] | no[k:] | (a[p] == b[q]) | (a[q] == b[p])
        p, q = p[~no], q[~no]; bp, bq = b[p].copy(), b[q].copy(); b[p] = bq; b[q] = bp
    m = rng.permutation(V)
    return rows_of(rng, m[a], m[b])
def graphs(rng, kinds):
    return np.stack([np.stack([graph(rng, int(kinds[r, g])) for g in range(8)]) for r in range(N)])
def parts(rng):
    return (rng.integers(-15, 16, (N, 8, 16, V)), rng.integers(-15, 16, (N, 8, 16, L)), rng.integers(-15, 16, (N, 8, 16, L)), rng.integers(-255, 256, (N, 8, 16, 1)),
            rng.integers(0, V, (N, 8, L)), rng.integers(0, D + T, (N, 8, L)))
def pack(nbs, x, c, y, h, v, j):
    def bf(a): return np.ascontiguousarray(a.reshape(N, 128, -1)).astype(np.float32).astype(BF)
    return {"adj": np.ascontiguousarray(nbs.transpose(0, 1, 3, 2).reshape(N, 8 * D, V)).astype(np.int32), "x": bf(x), "c0": bf(c), "y0": bf(y), "h": bf(h),
            "v0": np.stack([gtable(a) for a in v]), "j0": np.stack([gtable(a) for a in j])}
def setup_inputs(rng):
    return pack(graphs(rng, rng.choice(np.array([0, 0, 0, 1]), (N, 8))), *parts(rng))
def setup_inputs_ties(rng):
    x, c, y, h, v, j = parts(rng); pool = rng.integers(-1, 2, (N, 8, 16, 6))
    x = np.take_along_axis(pool, np.broadcast_to(rng.integers(0, 6, (N, 8, 1, V)), (N, 8, 16, V)), 3)
    c = rng.integers(-1, 2, c.shape) * (rng.random((N, 8, 1, L)) < 0.9)
    y = rng.integers(-1, 2, y.shape)
    return pack(graphs(rng, rng.choice(np.array([0, 1, 2]), (N, 8))), x, c, y, h, v, j)
def setup_inputs_tops(rng):
    x, c, y, h, v, j = parts(rng); k = L // 2
    c[..., :k] = 0; j[..., :k] = rng.integers(D, D + T, (N, 8, k))
    h[:, :4, 0] = -1; h[:, 0, 1:6] = 128; h[:, 1, 1:6] = -128; h[:, 4:6] = 255; h[:, 6:] = -255
    y[..., 0:3] = 0; y[:, :, 0, 1] = 1; y[:, :, 0, 2] = 2; y[..., 3] = 15; y[..., 4] = -15
    y[..., 5:k:2] = np.abs(y[..., 5:k:2])
    for i in range(4):
        y[:, :2, :, 5 + i] = 0
        y[:, :2, 1:6, 5 + i] = (1, -1, 1, -1)[i] * np.clip((1, 1, 2, 2)[i] * V // 128 - 15 * np.arange(5), 0, 15)
    v[..., 9:13] = (np.add.reduce(h * y, axis=2) & (V - 1))[..., 9:13]
    nbs = graphs(rng, rng.choice(np.array([0, 1]), (N, 8)))
    for r in range(N):
        for g in range(8):
            n = int(rng.integers(0, V)); q = int(rng.integers(0, D)); w = int(nbs[r, g, n, q])
            x[r, g, :, n] = 15; x[r, g, :, w] = -15
            v[r, g, k:k + 4] = n; j[r, g, k:k + 4] = np.array([q, q, D, D]); c[r, g, :, k:k + 4] = np.array([15, -15, 15, -15])
            m = int(rng.choice(np.setdiff1d(np.arange(V), np.concatenate([np.array([n, w]), nbs[r, g, n], nbs[r, g, w]]))))
            t = rng.integers(2, 6, D); t[0] = 5; t[1] = 6; t[D - 1] = 1
            x[r, g][:, nbs[r, g, m]] = 15 - (np.argsort(rng.random((16, D)), axis=0) < t)
            p, z = ((3, 1), (10, 2))[g % 2]; x[r, g, :, m] = 15 - z * (rng.permutation(16) < p)
            v[r, g, k + 4:k + 8] = m; j[r, g, k + 4:k + 8] = np.array([D, D, 0, 0]); c[r, g, :, k + 4:k + 8] = np.array([15, -15, 15, -15])
    return pack(nbs, x, c, y, h, v, j)
def setup_inputs_deep(rng):
    x, c, y, h, v, j = parts(rng); i = np.arange(V); q = i * 3390 // V
    col = np.concatenate([(q[None, :] // 15 + np.arange(15)[:, None]) // 15, (q % 15)[None, :]])
    w = (i[:, None] + np.concatenate([np.arange(-(D // 2), 0), np.arange(1, D // 2 + 1)])) & (V - 1)
    nbs = np.zeros((N, 8, V, D), np.int64); way = np.array([15] * 15 + [1])
    for r in range(N):
        for g in range(8):
            m = rng.permutation(V); u = (w, w[:, ::-1], rng.permuted(w, axis=1), rng.permuted(w, axis=1))[g % 4]
            nbs[r, g, m] = m[u]; x[r, g][:, m] = col
            c[r, g] = way[:, None] * np.where(rng.random(L) < 0.7, 1, -1)
    return pack(nbs, x, c, y, h, v, j)
def setup_inputs_alike(rng):
    x, c, y, h, v, j = parts(rng)
    v[:, 0::4] = rng.integers(0, V, (N, 2, 1)); v[:, 1::4] = rng.choice(np.array([0, V - 1]), (N, 2, L))
    j[:, 0::4] = np.arange(L) % (D + T); c[:, 2] = c[:, 2, :, :1]
    j[:, 3::3] = rng.integers(D, D + T, (N, 2, L)); c[:, 6] = 0; j[:, 5] = 0
    for r in range(N):
        n = int(rng.integers(0, V)); x[r, 7, :, n] = 15; v[r, 7] = n
    c[:, 7] = 15; j[:, 7] = rng.integers(0, D, (N, L))
    kinds = np.tile(np.array([2, 0, 2, 1, 0, 2, 1, 2]), (N, 1))
    return pack(graphs(rng, kinds), x, c, y, h, v, j)
def setup_inputs_spread(rng):
    x, c, y, h, v, j = parts(rng)
    def size(a, top): return np.sign(a) * ((np.abs(a) * np.exp2(-top * rng.random(a.shape[:2] + (1, a.shape[3])))).astype(np.int64))
    x = size(x, 5) * (rng.random((N, 8, 1, V)) > 0.0625); c = size(c, 4); y = size(y, 4); h = size(h, 7)
    v = (V * rng.random((N, 8, L)) ** 4).astype(np.int64)
    return pack(graphs(rng, rng.choice(np.array([0, 0, 1]), (N, 8))), x, c, y, h, np.minimum(v, V - 1), j)
def check_inputs(d):
    bad = []
    for k, lo, hi in (("adj", 0, V - 1), ("x", -15, 15), ("c0", -15, 15), ("y0", -15, 15), ("h", -255, 255), ("v0", 0, V - 1), ("j0", 0, D + T - 1)):
        a = np.asarray(d[k]).astype(np.float32)
        if not (np.min(a) >= lo and np.max(a) <= hi and np.all(a == np.floor(a))): bad.append("range of " + k)
    me = np.arange(V)[:, None]; own = twice = oneway = False
    for a in np.asarray(d["adj"]).astype(np.int64).reshape(N * 8, D, V):
        w = np.ascontiguousarray(a.T); s = np.sort(w, axis=1)
        own = own or bool(np.any(w == me)); twice = twice or bool(np.any(s[:, 1:] == s[:, :-1]))
        oneway = oneway or bool(np.any(np.sort((me * V + w).reshape(-1)) != np.sort((w * V + me).reshape(-1))))
    if own: bad.append("adj: a node is its own neighbour")
    if twice: bad.append("adj: a neighbour stands twice at one node")
    if oneway: bad.append("adj: an edge goes one way only")
    return bad
def reference(adj, x, c0, y0, h, v0, j0):
    P = N * 8
    nbs = np.ascontiguousarray(adj.reshape(P, D, V).transpose(0, 2, 1)).astype(np.int64)
    def turned(a): return np.ascontiguousarray(a.astype(np.float32).reshape(P, 16, -1).transpose(0, 2, 1)).astype(np.int32)
    xs, c, y, hs = turned(x), turned(c0), turned(y0), turned(h)
    v = np.stack([gentries(a) for a in v0]).reshape(P, L).astype(np.int64); j = np.stack([gentries(a) for a in j0]).reshape(P, L).astype(np.int64)
    b = np.arange(P)[:, None]; b3 = b[:, :, None]
    def parent(e, c):
        near = nbs[b, e]
        s = np.einsum("pldi,pli->pld", xs[b3, near], c); mine = np.einsum("pli,pli->pl", xs[b, e], c)
        best = np.argmax(s, axis=2)[:, :, None]
        return np.where(np.take_along_axis(s, best, 2)[:, :, 0] > mine, np.take_along_axis(near, best, 2)[:, :, 0], e)
    for step in range(1, RO + 1):
        back = j >= D; nv = v; nj = j + T; found = np.zeros((P, L), bool); fv = v
        for t in range(T):
            ok = ~back & (j + t < D)
            w = np.where(ok, nbs[b, v, np.minimum(j + t, D - 1)], v)
            f = parent(w, c)
            if t == 0: fv = f
            hit = ok & ~found & (f == v)
            nv = np.where(hit, w, nv); nj = np.where(hit, 0, nj); found = found | hit
        at = np.argmax(nbs[b, fv] == v[:, :, None], axis=2)
        again = np.add.reduce(hs.astype(np.int64) * y, axis=2) & (V - 1)
        up = back & (fv != v); top = back & (fv == v)
        v = np.where(up, fv, np.where(top, again, nv)); j = np.where(up, 1 + at, np.where(top, 0, nj))
        if step % 2 == 0:
            xv = xs[b, v]
            y = np.roll(xv.reshape(N, 8, L, 16), 1, axis=0).reshape(P, L, 16)
            c = np.clip(c + np.sign(y - xv), -15, 15)
    return {"vo": v.reshape(N, 8, L).astype(np.float32), "jo": j.reshape(N, 8, L).astype(np.float32),
            "co": np.ascontiguousarray(c.transpose(0, 2, 1)).reshape(N, 128, L).astype(np.float32)}

@@ -1,0 +1,521 @@
+from concourse.mybir import AluOpType, ActivationFunctionType
+
+A = AluOpType
+F = ActivationFunctionType
+NV, NL, STEPS = 4096, 224, 6
+CFG = {"HS": [80, 80, 64], "CH": 2, "NENG": 8, "SPLIT": 1,
+       "cyc": 1.04, "pe": 0.52, "lat": 120.0, "rlat": 3000.0, "gat": 1.56, "fix": 50.0, "dl": 1900.0, "eps": 30.0,
+       "bias": "pidihnitrhzhadkraoonxwkoqeqazrgtoqvdclqirsneyzathiqaejnpptgnmgmlnzbinrluvopxwlljjnnrkuqbuljykrookhqkwtvkpkermvklmonyqsulmssqxtagrdiagxolcjzzgrytdofjoawtchltbuznljmlneqkqhrkaljzxwtqenrhkezgezcdqrcagyzfiitnuruqpspgymjtifgqspgfgipqocikhlkwprgrfnpiukwjqtzdppaaxftgtnrfnasdggzmqptamjcsgsdigcfujkjdnzwkuexccxavnjqhdvucnjnnlhroyibcamoodbluqgmvwlmpwsnfpogdwxkofclgmkmnzkliaaigmxrpztagspaxfldzgnpifwipzzlxwezqmbjnzrihovhzejaanmalzoriupidwphdtizxtoajajuzgaoqnjjhztgciujnnzkeynjoxtittcruiifonkazvzaukppxtunijipfgegivimtnuqlowzetucnkavmlikucaeawtwzowljuxojrtzjzxmxlzlyxsgdmdakzdqmjyrosjjayafmqsozjendamvaepttnlpmvmtaktnuajeqxvnaxjrrazwzamgaeqgfddxtkbvppxoxqspusojfgahmhzacdcdlfjqqrkqsfyssswjghzoffqnqddcmasamtlkimx"}
+HS = CFG["HS"]
+NB = len(HS)
+OFF = [sum(HS[:b]) for b in range(NB)]
+HM = max(HS)
+LW = [h + 2 * ((h // 16 + 1) // 2) for h in HS]
+LOFF = [sum(LW[:b]) for b in range(NB)]
+MATS = ["Zq", "Zq3", "Zd", "Zs", "Uw", "Vm", "Blk", "Teq", "B20", "B21", "B22", "B23",
+        "L1sg", "L1su", "L1J", "L1eq", "L2l", "L2w", "L2J", "L2c", "I"]
+NM = len(MATS)
+XW = 40 + 8 * (NM - 4)
+COLS = ["r", "a", "b", "gt", "bS", "sub", "r256", "mv", "bm3", "nb3", "a2h", "m67", "bL1", "bL2", "bq", "t0", "t1", "na0",
+        "h32", "u0", "u1", "u2", "u3"]
+BF, F32, I32, U16 = "bfloat16", "float32", "int32", "uint16"
+SCRATCH = {}
+for _d, _l in ((BF, [("xw", NV), ("win", NV), ("ahi", 1024), ("alo", 1024), ("nn", 256), ("hb", 1), ("tab", 16),
+                     ("bt", 16 * (NM + 1)), ("mt", 16 * XW), ("hbm", 128), ("l2y", 128), ("l2q", 128), ("ni", 128),
+                     ("w1", NL), ("gg", 4 * NL), ("pp", 17 * NL), ("cr", 17 * NL), ("eq", NL), ("sg", 2 * NL), ("l1o", NL),
+                     ("js", NL), ("qq", NL), ("sd", NL), ("xv0", NL), ("xv1", NL), ("xv2", NL),
+                     ("yy0", NL), ("yy1", NL), ("yy2", NL), ("yy3", NL)]),
+               (F32, [("col", len(COLS)), ("q16", 16), ("one", 16), ("ea", 4), ("eb", 4), ("le4", 4), ("e16", 16),
+                      ("lt16", 16), ("tmp", 16), ("xl", XW), ("l3v", 128), ("l3j", 128), ("scn", HM), ("t32", NL),
+                      ("vsb", NL), ("l2o", NL), ("sc", NL), ("co32", NL), ("jo32", NL)]),
+               (I32, [("a32", 1024), ("v32", 14), ("j32", 14), ("pc", 4), ("rl32", HM)]),
+               (U16, [("jl", 14), ("xu", XW), ("rl", HM), ("lst", sum(LW)), ("wq", NL // 4)])):
+    for _n, _w in _l:
+        SCRATCH[_n] = ("sbuf", [128, _w], _d)
+for _k in range(8):
+    SCRATCH["ps%d" % _k] = ("psum", [128, 512], F32)
+DRAM = ("adj", "x", "c0", "y0", "h", "v0", "j0", "vo", "jo", "co")
+
+
+def R(buf, c0, c1, st=1, p0=0, p1=128, ps=1):
+    return (buf, c0, c1, st, p0, p1, ps)
+
+
+def K(buf, i):
+    return R(buf, i, i + 1)
+
+
+def IND(win, off):
+    return ("ind", win, off)
+
+
+def C(name):
+    return K("col", COLS.index(name))
+
+
+def xo(m):
+    return 10 * m if m < 4 else 40 + 8 * (m - 4)
+
+
+def M(name, shift=0):
+    i = 16 * xo(MATS.index(name)) + shift
+    return R("mt", i, i + 128)
+
+
+def B(name, c0=0, c1=16, st=1):
+    i = 16 * (MATS.index(name) + 1)
+    return R("bt", i + c0, i + c1, st)
+
+
+def ncols(r):
+    return 16 * ncols(r[2]) if r[0] == "ind" else len(range(r[1], r[2], r[3]))
+
+
+def two(r):
+    return r[0] != "ind" and SCRATCH[r[0]][2] in (BF, U16)
+
+
+def isreg(a):
+    return isinstance(a, tuple)
+
+
+def build_ops():
+    ops = []
+    cyc, gat, fix = CFG["cyc"], CFG["gat"], CFG["fix"]
+    grp, turn = [0], [0]
+
+    def add(eng, kind, args, rd, wr, cost, same=False, **kw):
+        rr = []
+        for a in rd:
+            if isreg(a):
+                rr += [a[1], a[2]] if a[0] == "ind" else [a]
+        grp[0] += 0 if same else 1
+        d = {"eng": eng, "kind": kind, "args": args, "rd": rr, "wr": wr, "cost": cost, "id": len(ops), "grp": grp[0]}
+        d.update(kw)
+        ops.append(d)
+
+    def vcost(src, n, f):
+        return 62 + gat * n * cyc if src[0] == "ind" else fix + max(64, n * f) * cyc
+
+    def cp(o, i):
+        add("V", "cp", (o, i), [i], [o], vcost(i, ncols(o), 0.5 if two(o) and two(i) else 1))
+
+    def ts(o, i, s1, s2, op0, op1=None):
+        add("V", "ts", (o, i, s1, s2, op0, op1), [i, s1, s2], [o], vcost(i, ncols(o), 0.5 if two(o) and two(i) else 1))
+
+    def tt(o, i0, i1, op):
+        f = 1 if i0[0].startswith("ps") or i1[0].startswith("ps") else 2
+        add("V", "tt", (o, i0, i1, op), [i0, i1], [o], vcost(i0, ncols(o), f))
+
+    def ms(o, v):
+        add("V", "ms", (o, v), [], [o], vcost(o, ncols(o), 0.5 if two(o) else 1))
+
+    def act(o, i, fn, bias=0.0, scale=1.0):
+        c = 80 + gat * ncols(o) * cyc if i[0] == "ind" else fix + 30 + max(64, ncols(o)) * cyc
+        add("S", "act", (o, i, fn, bias, scale), [i, bias, scale], [o], c)
+
+    def lin(o, i, scale):
+        turn[0] += 1
+        if turn[0] % 3 < CFG["SPLIT"]:
+            act(o, i, F.Identity, 0.0, scale)
+        else:
+            ts(o, i, scale, None, A.mult)
+
+    def mm(o, pairs):
+        for k, (l, r) in enumerate(pairs):
+            f = 4 if SCRATCH[l[0]][2] == F32 else 1
+            add("P", "mm", (o, l, r, k == 0, k == len(pairs) - 1), [l, r], [o], 10 + f * max(64, ncols(r)) * CFG["pe"], k > 0)
+
+    def iota(o, pat, base, cm):
+        add("G", "iota", (o, pat, base, cm), [], [o], 160 + 2 * ncols(o) * cyc)
+
+    def sel(o, i, pat, base, cm, same=False):
+        add("G", "sel", (o, i, pat, base, cm), [i], [o], 210 + 2 * ncols(o) * cyc, same)
+
+    def dma(q, o, i, nbytes, sem=None):
+        add(q, "dma", (o, i), [i], [o], 100, done=CFG["dl"] + nbytes / 200.0, sem=sem)
+
+    for u in range(2):
+        for k in range(4):
+            dma("YS"[k % 2], R("a32", 512 * u, 512 * u + 512, 1, 32 * k, 32 * k + 32),
+                R("adj", 2048 * u, 2048 * u + 2048, 1, k, 32, 4), 200000 * (u + 1))
+    dma("S", R("v32", 0, 14), R("v0", 0, 14), 8000)
+    for b in range(NB):
+        o = 17 * OFF[b] + 16 * HS[b]
+        dma("S", R("cr", o, o + HS[b]), R("c0", OFF[b], OFF[b] + HS[b]), 30000)
+    dma("Y", R("xw", 0, NV), R("x", 0, NV), 1500000)
+    dma("Y", R("j32", 0, 14), R("j0", 0, 14), 8000)
+    dma("Y", R("yy0", 0, NL), R("y0", 0, NL), 60000)
+    dma("Y", R("hb", 0, 1), R("h", 0, 1), 8000)
+    iota(K("pc", 0), [[0, 1]], 0, 1)
+    iota(R("q16", 0, 16), [[1, 16]], 0, 0)
+    iota(R("nn", 0, 256), [[1, 256]], 0, 0)
+    ts(K("pc", 1), K("pc", 0), 15, None, A.bitwise_and)
+    ts(K("pc", 2), K("pc", 0), 2, 3, A.logical_shift_right, A.bitwise_and)
+    ts(K("pc", 3), K("pc", 0), 3, None, A.bitwise_and)
+    cp(R("col", 0, 3), R("pc", 1, 4))
+    r, a, b_ = C("r"), C("a"), C("b")
+    ts(C("r256"), r, 256.0, None, A.mult)
+    ts(R("nn", 0, 256, 1, 0, 64), R("nn", 0, 256, 1, 0, 64), 0.0, C("r256")[:5] + (64, 1), A.mult, A.add)
+    for k in range(8):
+        dma("Y", R("win", 0, NV, 1, 16 * k + 8, 16 * k + 16), R("nn", 0, 256), 100000)
+    for u in range(2):
+        c0, c1 = 512 * u, 512 * u + 512
+        cp(R("ahi", c0, c1), R("a32", c0, c1))
+        tt(R("alo", c0, c1), R("a32", c0, c1), R("ahi", c0, c1), A.subtract)
+        for j, t in enumerate(("ahi", "alo")):
+            for k in range(4):
+                dma("YS"[u * j * (k % 2)], R("win", 4 * c0, 4 * c1, 1, 4 * j + k, 128, 16),
+                    R(t, c0, c1, 1, 32 * k, 32 * k + 32), 80000)
+    for c0, n, w, base in ((0, 4, 10, 16), (40, NM - 4, 8, 80)):
+        x = R("xl", c0, c0 + n * w)
+        iota(x, [[16, n], [-16, w]], base, 1)
+        sel(x, x, [[0, n], [-16, w]], 0, 1)
+        sel(x, x, [[0, n], [16, w]], 15, -1)
+        cp(R("xu", c0, c0 + n * w), x)
+    iota(R("rl32", 0, HM), [[1, HM]], 0, 0)
+    iota(R("scn", 0, HM), [[0, HM // 16], [1, 16]], 0, 0)
+    cp(R("rl", 0, HM), R("rl32", 0, HM))
+    ms(R("one", 0, 16), 1.0)
+    ms(R("bt", 0, 16 * (NM + 1)), 0.0)
+    q4, q16, o4, o16 = R("q16", 0, 4), R("q16", 0, 16), R("one", 0, 4), R("one", 0, 16)
+    ea, eb, e16 = R("ea", 0, 4), R("eb", 0, 4), R("e16", 0, 16)
+    ts(ea, q4, a, None, A.is_equal)
+    ts(eb, q4, b_, None, A.is_equal)
+    ts(e16, q16, r, None, A.is_equal)
+    ts(R("lt16", 0, 16), q16, r, None, A.is_gt)
+    low, lt6, a0, a1, a2, e11 = K("lt16", 8), K("lt16", 6), K("ea", 0), K("ea", 1), K("ea", 2), K("e16", 11)
+    lin(B("Zq", 12, 16), eb, low)
+    lin(B("Zq3", 12, 15), R("eb", 0, 3), low)
+    lin(C("nb3"), K("eb", 3), -1.0)
+    ts(B("Zd", 12, 16), o4, C("nb3"), low, A.mult, A.mult)
+    ms(B("Zs", 15, 16), -1.0)
+    lin(B("Uw", 3, 16, 4), eb, low)
+    ts(C("mv"), K("e16", 8), K("e16", 12), None, A.add)
+    lin(B("Vm"), o16, C("mv"))
+    ms(B("Blk"), 1.0)
+    ts(R("le4", 0, 4), q4, b_, None, A.is_ge)
+    for k in range(3):
+        lin(B("Teq", k, 16, 4), ea, K("le4", k))
+    for m in range(4):
+        if m > 0:
+            lin(B("B2%d" % m, 4 * m, 5 * m), R("one", 0, m), 1.0)
+        if m < 3:
+            lin(B("B2%d" % m, 5 * m + 4, 16, 4), R("one", 0, 3 - m), -1.0)
+    ts(C("bS"), K("eb", 3), 0.5, -0.5, A.mult, A.add)
+    ts(C("gt"), a, b_, None, A.is_gt)
+    lin(C("a2h"), a2, 0.5)
+    ts(C("bm3"), b_, -3.0, None, A.add)
+    lin(B("L1sg", 0, 4), ea, 1.0)
+    lin(B("L1sg", 4, 8), ea, C("nb3"))
+    ts(B("L1sg", 8, 12), ea, C("nb3"), 8.0, A.mult, A.mult)
+    tt(R("tmp", 0, 4), ea, eb, A.subtract)
+    lin(B("L1su", 4, 8), R("tmp", 0, 4), C("gt"))
+    ts(B("L1su", 8, 12), R("tmp", 0, 4), C("gt"), 8.0, A.mult, A.mult)
+    lin(B("L1J", 0, 4), eb, C("a2h"))
+    ts(B("L1J", 4, 8), o4, e11, -0.5, A.mult, A.mult)
+    ts(B("L1J", 8, 12), o4, e11, -4.0, A.mult, A.mult)
+    lin(B("L1eq", 8, 12), ea, C("bm3"))
+    lin(C("t0"), low, -3.5)
+    ts(C("bL1"), a2, -32.0, C("t0"), A.mult, A.add)
+    lin(C("na0"), a0, -4096.0)
+    ts(R("tmp", 4, 8), q4, b_, C("na0"), A.is_gt, A.mult)
+    ts(R("tmp", 8, 12), eb, low, 4096.0, A.mult, A.mult)
+    tt(B("L2l", 0, 4), R("tmp", 4, 8), R("tmp", 8, 12), A.add)
+    lin(B("L2l", 4, 5), a0, -4096.0)
+    lin(B("L2l", 5, 6), a1, -4096.0)
+    lin(B("L2l", 6, 7), a0, -16.0)
+    lin(B("L2l", 7, 8), a2, 1.0)
+    ts(C("t1"), a0, 8.0, a2, A.mult, A.subtract)
+    lin(B("L2l", 8, 12), o4, C("t1"))
+    lin(B("L2w", 0, 4), eb, low)
+    lin(B("L2w", 4, 5), C("mv"), 1.0)
+    lin(B("L2J", 4, 5), e11, 2048.0)
+    lin(B("L2J", 5, 6), e11, -2048.0)
+    ts(B("L2J", 6, 7), e11, 8.5, C("a2h"), A.mult, A.subtract)
+    ts(B("L2J", 8, 12), o4, e11, -4.0, A.mult, A.mult)
+    ms(B("L2c", 5, 6), 1.0)
+    lin(B("I"), e16, 1.0)
+    ts(C("u0"), b_, -3.5, a2, A.add, A.mult)
+    ts(C("u1"), K("e16", 4), -2048.0, C("u0"), A.mult, A.add)
+    ts(C("u2"), K("e16", 5), 4096.0 * 192 - 2048.0, C("u1"), A.mult, A.add)
+    ts(C("u3"), K("e16", 6), -2.5, C("u2"), A.mult, A.add)
+    ts(C("bL2"), C("na0"), C("u3"), None, A.add)
+    ts(C("m67"), lt6, -1.0, low, A.mult, A.add)
+    ms(C("bq"), 192.0 - 2047.5 / 4096.0)
+    ts(C("sub"), r, -4096.0, 15 * 4096.0, A.mult, A.add)
+    ts(R("scn", 0, HM), R("scn", 0, HM), r, 135168.0, A.is_gt, A.mult)
+    ts(R("scn", 0, HM), R("scn", 0, HM), -131072.0, None, A.add)
+    ts(R("tab", 0, 16), q16, b_, 2.0, A.is_le, A.mult)
+    ts(R("tab", 0, 16), R("tab", 0, 16), -1.0, None, A.add)
+    for m0, m1 in ((0, 1), (1, 3), (3, 4), (4, 6), (6, 9), (9, 12), (12, 14), (14, 16), (16, 18), (18, NM)):
+        n = xo(m1) - xo(m0) - (1 if m1 <= 4 else 0)
+        act(R("mt", 16 * xo(m0), 16 * (xo(m0) + n)), IND(R("bt", 0, 16 * (m1 + 1)), R("xu", xo(m0), xo(m0) + n)), F.Copy)
+    cp(C("h32"), R("hb", 0, 1))
+    lin(R("hbm", 0, 128), M("Blk"), C("h32"))
+    lin(R("l2y", 0, 128), M("L2c"), C("h32"))
+    ts(R("l2q", 0, 128), M("L2c"), K("e16", 0), -4096.0, A.mult, A.mult)
+    lin(R("ni", 0, 128), M("I"), -1.0)
+    lin(R("l3v", 0, 128), M("Blk"), lt6)
+    lin(R("l3j", 0, 128), M("Blk"), C("m67"))
+    cp(R("jl", 0, 14), R("j32", 0, 14))
+    act(R("js", 0, NL), IND(R("tab", 0, 16), R("jl", 0, 14)), F.Copy)
+
+    def PS(name, b, n=None):
+        h = HS[b]
+        k, c = {"WQ": (0, 0), "U": (0, 1), "DF": (0, 2), "B2": (0, 3), "L2": (0, 4), "D3": (1, 0), "L1": (1, 1),
+                "L3": (1, 2), "LJ": (1, 3), "V0": (1, 3), "s": (2, 0), "d": (2, 1), "cn": (2, 2)}[name]
+        t, c = (2 * b + k, c * h) if k < 2 else (6 + b % 2, (c + 3 * (b // 2)) * HM)
+        return R("ps%d" % t, c, c + (h if n is None else n))
+
+    def chunks(h):
+        n = CFG["CH"]
+        e = [2 * ((h * k // n) // 2) for k in range(n)] + [h]
+        return [(e[k], e[k + 1]) for k in range(n)]
+
+    def update(b, k, last):
+        h, o = HS[b], OFF[b]
+        c, y = R("cr", 17 * o + 16 * h, 17 * o + 17 * h), R("yy%d" % (k + 1), o, o + h)
+        add("N", "recv", (k, b), [], [y], 0, after=("send", k, b))
+        mm(PS("d", b), [(R("ni", 0, 128), R("xv%d" % k, o, o + h)), (M("I"), y)])
+        act(R("sd", o, o + h), PS("d", b), F.Sign)
+        mm(PS("cn", b), [(M("I"), c), (M("I"), R("sd", o, o + h))])
+        ts(R("co32", o, o + h) if last else c, PS("cn", b), 15.0, -15.0, A.min, A.max)
+
+    for b in range(NB):
+        h = HS[b]
+        cp(R("lst", LOFF[b] + h, LOFF[b] + h + h // 16), R("v32", OFF[b] // 16, (OFF[b] + h) // 16))
+    xw, win = R("xw", 0, NV), R("win", 0, NV)
+    for s in range(STEPS):
+        for b in range(NB):
+            h, o, lo = HS[b], OFF[b], LOFF[b]
+
+            def W(buf, f=1, c0=0, st=1):
+                return R(buf, f * o + c0, f * (o + h), st)
+            vk, ul, wq = R("lst", lo + h, lo + h + h // 16), R("lst", lo, lo + h), R("wq", o // 4, (o + h) // 4)
+            p0 = 17 * o
+            c, pv = R("cr", p0 + 16 * h, p0 + 17 * h), R("pp", p0 + 16 * h, p0 + 17 * h)
+            act(W("w1"), IND(win, vk), F.Copy)
+            mm(PS("WQ", b, h // 4), [(M("Zq", 12 - 4 * k), W("w1", 1, k, 4)) for k in range(4)])
+            cp(wq, PS("WQ", b, h // 4))
+            if s == 0:
+                mm(PS("V0", b), [(M("Vm"), W("w1"))])
+                act(W("vsb"), PS("V0", b), F.Copy)
+            act(W("gg", 4), IND(win, wq), F.Copy)
+            mm(PS("U", b), [(M("Uw"), W("w1"))] + [(M("Zq3", 12 - 4 * i), W("gg", 4, i, 4)) for i in range(4)])
+            mm(PS("D3", b), [(M("Vm"), W("w1"))] + [(M("Zd", 12 - 4 * i), W("gg", 4, i, 4)) for i in range(4)])
+            tt(W("eq"), PS("U", b), W("vsb"), A.is_equal)
+            tt(W("t32"), PS("D3", b), W("eq"), A.mult)
+            tt(ul, PS("U", b), W("t32"), A.subtract)
+            if s % 2 == 0:
+                if s > 0:
+                    update(b, s // 2 - 1, False)
+                if s == 0 and b == NB - 1:
+                    for m in range(16):
+                        sel(R("cr", p0 + m, p0 + 16 * h, 16), c, [[0, h]], 0, 0, m > 0)
+                else:
+                    for l0, l1 in chunks(h):
+                        act(R("cr", p0 + 16 * l0, p0 + 16 * l1), IND(c, R("rl", l0, l1)), F.Copy)
+                mm(PS("s", b), [(R("hbm", 0, 128), W("yy%d" % (s // 2)))])
+                act(W("qq"), PS("s", b), F.Identity, C("bq"), 1.0 / 4096.0)
+            tt(pv, IND(xw, vk), c, A.mult)
+            for l0, l1 in chunks(h):
+                tt(R("pp", p0 + 16 * l0, p0 + 16 * l1), IND(xw, R("lst", lo + l0, lo + l1)),
+                   R("cr", p0 + 16 * l0, p0 + 16 * l1), A.mult)
+            mm(PS("DF", b), [(M("Blk"), pv), (M("Teq"), W("eq"))]
+               + [(M("Zs", 15 - m), R("pp", p0 + m, p0 + 16 * h, 16)) for m in range(16)])
+            mm(PS("B2", b), [(M("B2%d" % m), R("pp", p0 + 4 * m + 3, p0 + 16 * h, 16)) for m in range(4)])
+            act(W("sg", 2), PS("DF", b, 2 * h), F.Sign, C("bS"))
+            mm(PS("L1", b), [(M("L1J"), W("js")), (M("L1eq"), W("eq")), (M("L1sg"), R("sg", 2 * o, 2 * o + h)),
+                             (M("L1su"), R("sg", 2 * o + h, 2 * o + 2 * h))])
+            act(W("l1o"), PS("L1", b), F.Relu, C("bL1"))
+            mm(PS("L2", b), [(M("L2w"), W("w1")), (M("L2J"), W("js")), (R("l2y", 0, 128), W("yy%d" % (s // 2))),
+                             (R("l2q", 0, 128), W("qq")), (M("L2l"), W("l1o"))])
+            act(W("l2o"), PS("L2", b), F.Relu, C("bL2"))
+            mm(PS("L3", b), [(R("l3v", 0, 128), W("l2o"))])
+            add("V", "scan", (W("sc"), R("scn", 0, h), PS("L3", b)), [R("scn", 0, h), PS("L3", b)], [W("sc")],
+                fix + max(64, h) * cyc)
+            ts(vk, W("sc", 1, 15, 16), C("sub"), None, A.subtract)
+            if s % 2 == 1:
+                k = s // 2
+                if s < STEPS - 1:
+                    act(W("xv%d" % k), IND(xw, vk), F.Copy)
+                else:
+                    cp(W("xv%d" % k), IND(xw, vk))
+                add("G", "send", (k, b), [W("xv%d" % k)], [], 300, done=CFG["rlat"], key=("send", k, b))
+            act(W("vsb"), PS("L3", b), F.Copy)
+            if s < STEPS - 1:
+                act(W("js"), PS("L2", b), F.Sign, C("bL2"))
+            else:
+                mm(PS("LJ", b), [(R("l3j", 0, 128), W("l2o"))])
+                act(W("jo32"), PS("LJ", b), F.Copy)
+    dma("Y", R("vo", 0, NL, 1, 0, 8), R("vsb", 0, NL, 1, 0, 128, 16), 3000, "out")
+    dma("Y", R("jo", 0, NL, 1, 0, 8), R("jo32", 0, NL, 1, 0, 128, 16), 3000, "out")
+    for b in range(NB):
+        h, o = HS[b], OFF[b]
+        update(b, 2, True)
+        dma("Y", R("co", o, o + h), R("co32", o, o + h), 40000, "out")
+    return ops
+
+
+def overlap(x, y):
+    if x[1] >= y[2] or y[1] >= x[2]:
+        return False
+    if x[3] > 1 and y[3] > 1 and not set(range(*x[1:4])) & set(range(*y[1:4])):
+        return False
+    return bool(set(range(x[4], x[5], x[6])) & set(range(y[4], y[5], y[6])))
+
+
+def link(ops):
+    hist, bank, keys = {}, {}, {}
+    for d in ops:
+        deps, order = set(), set()
+        use = [(x, False) for x in d["rd"] if x[0] not in DRAM] + [(x, True) for x in d["wr"] if x[0] not in DRAM]
+        for reg, w in use:
+            for e, ereg, ew in hist.get(reg[0], []):
+                if (w or ew) and overlap(reg, ereg):
+                    (order if e["eng"] == d["eng"] == "P" else deps).add(e["id"])
+            if reg[0].startswith("ps"):
+                for en, e in bank.setdefault(reg[0], {}).items():
+                    (order if en == d["eng"] else deps).add(e["id"])
+        for reg, w in use:
+            hl = hist.setdefault(reg[0], [])
+            if w and reg[3:] == (1, 0, 128, 1):
+                hl[:] = [z for z in hl if not (z[1][1] >= reg[1] and z[1][2] <= reg[2])]
+            hl.append((d, reg, w))
+            if reg[0].startswith("ps"):
+                bank[reg[0]][d["eng"]] = d
+        if "key" in d:
+            keys[d["key"]] = d["id"]
+        d["soft"] = [keys[d["after"]]] if "after" in d else []
+        d["deps"], d["order"] = ([] if d["kind"] == "recv" else sorted(deps)), sorted(order - deps)
+
+
+def schedule(ops, bias):
+    lat, eps, n = CFG["lat"], CFG["eps"], len(ops)
+    succ = [[] for _ in range(n)]
+    for d in ops:
+        for e in d["deps"] + d["soft"]:
+            succ[e].append((d["id"], True))
+        for e in d["order"]:
+            succ[e].append((d["id"], False))
+    prio = [0.0] * n
+    for d in reversed(ops):
+        full = d["cost"] + d.get("done", 0)
+        prio[d["id"]] = max([full] + [(full + lat if h else d["cost"]) + prio[j] for j, h in succ[d["id"]]])
+    for d in ops:
+        if d["grp"] < len(bias):
+            prio[d["id"]] += 400.0 * (ord(bias[d["grp"]]) - 109)
+    left = [len(d["deps"]) + len(d["soft"]) + len(d["order"]) for d in ops]
+    rdy = [0.0] * n
+    free = {e: 0.0 for e in "VSPGYN"}
+    pool = {e: [d["id"] for d in ops if d["eng"] == e and left[d["id"]] == 0] for e in free}
+    seq = []
+    while len(seq) < n:
+        t, e = min((max(free[e], min([rdy[i] for i in pool[e]])), e) for e in pool if pool[e])
+        i = max([j for j in pool[e] if rdy[j] <= t + eps], key=lambda j: prio[j])
+        pool[e].remove(i)
+        d = ops[i]
+        d["t0"] = max(free[e], rdy[i])
+        free[e] = d["t0"] + d["cost"]
+        d["t1"] = free[e] + d.get("done", 0)
+        seq.append(d)
+        for j, h in succ[i]:
+            rdy[j] = max(rdy[j], d["t1"] + lat if h else d["t0"])
+            left[j] -= 1
+            if left[j] == 0:
+                pool[ops[j]["eng"]].append(j)
+    return seq
+
+
+def plan_waits(ops, seq):
+    cnt, known, top, nd = {}, {e: {} for e in "VSPGY"}, {}, 0
+    for d in seq:
+        if d["kind"] == "recv":
+            d["sig"], d["know"] = ("ya%d_%d" % d["args"], CFG["NENG"]), {}
+            continue
+        kn, need = known[d["eng"]], {}
+        for e in sorted(d["deps"], key=lambda j: -ops[j]["t1"]):
+            s, v = ops[e]["sig"]
+            if kn.get(s, 0) < v:
+                need[s] = max(need.get(s, 0), v)
+                kn[s] = v
+                for s2, v2 in ops[e]["know"].items():
+                    kn[s2] = max(kn.get(s2, 0), v2)
+        d["waits"] = sorted(need.items())
+        for s, v in d["waits"]:
+            top[s] = max(top.get(s, 0), v)
+        d["know"] = dict(kn)
+        if d["kind"] == "dma":
+            s, inc = d["sem"] or "d%d" % nd, 16
+            nd += 1
+        elif d["kind"] == "send":
+            s, inc = "sent", CFG["NENG"]
+        else:
+            s, inc = "e" + d["eng"], 1
+        cnt[s] = cnt.get(s, 0) + inc
+        d["sig"] = (s, cnt[s])
+    final = sorted([(s, v) for s, v in cnt.items() if top.get(s, 0) < v], key=lambda z: z[0] == "out")
+    return final, sorted(cnt) + ["ya%d_%d" % (k, b) for k in range(3) for b in range(NB)]
+
+
+OPS = build_ops()
+link(OPS)
+SEQ = schedule(OPS, CFG["bias"])
+FINAL, SEMAPHORES = plan_waits(OPS, SEQ)
+
+
+def rank_program(g, core, T, topo):
+    rank = T.rank_of(core)
+    if rank is None:
+        return
+    nxt = T.cores[(rank + 1) % len(T.cores)]
+    rid, pid = topo.addr(nxt, core)
+    mask = sum(1 << e for e in topo.engines(core, nxt)[:CFG["NENG"]])
+    queue = {"V": g.vector, "S": g.scalar, "P": g.tensor, "G": g, "Y": g.sync}
+
+    def ap(r):
+        if not isreg(r):
+            return r
+        if r[0] == "ind":
+            return ap(r[1]).indirect(ap(r[2]))
+        if r[0] == "h":
+            return T["h"][:]
+        return T[r[0]][slice(r[4], r[5], r[6] if r[6] > 1 else None), slice(r[1], r[2], r[3] if r[3] > 1 else None)]
+
+    for d in SEQ:
+        k = d["kind"]
+        if k == "recv":
+            continue
+        a = [ap(z) for z in d["args"]]
+        q = queue[d["eng"]]
+        for s, v in d["waits"]:
+            q.wait_ge(T.sem[s], v)
+        if k == "send":
+            o, h = OFF[a[1]], HS[a[1]]
+            g.remote_dma(ap(R("yy%d" % (a[0] + 1), o, o + h)), ap(R("xv%d" % a[0], o, o + h)),
+                         T.sem["ya%d_%d" % d["args"]], T.sem["sent"], pid, rid, mask)
+            continue
+        if k == "cp":
+            ins = q.tensor_copy(*a)
+        elif k == "ts":
+            ins = q.tensor_scalar(*(a[:5] if a[5] is None else a))
+        elif k == "tt":
+            ins = q.tensor_tensor(*a)
+        elif k == "ms":
+            ins = q.memset(*a)
+        elif k == "scan":
+            ins = q.tensor_tensor_scan(a[0], a[1], a[2], 0.0, A.add, A.max)
+        elif k == "act":
+            ins = q.activation(*a[:3]) if a[2] == F.Copy else q.activation(*a[:3], bias=a[3], scale=a[4])
+        elif k == "mm":
+            ins = q.matmul(*a)
+        elif k == "iota":
+            ins = q.iota(*a) if SCRATCH[d["args"][0][0]][2] == I32 else q.iota(*a, allow_small_or_imprecise_dtypes=True)
+        elif k == "sel":
+            ins = q.affine_select(a[0], a[1], a[2], A.is_ge, 0.0, a[3], a[4])
+        else:
+            ins = q.dma_start(*a)
+        ins.then_inc(T.sem[d["sig"][0]], 16 if k == "dma" else 1)
+    for s, v in FINAL:
+        g.wait_ge(T.sem[s], v)

@@ -3,9 +3,12 @@ from concourse.mybir import AluOpType, ActivationFunctionType
 A = AluOpType
 F = ActivationFunctionType
 NV, NL, STEPS = 4096, 224, 6
-CFG = {"HS": [80, 80, 64], "CH": 2, "NENG": 8, "SPLIT": 1,
-       "cyc": 1.04, "pe": 0.52, "lat": 120.0, "rlat": 3000.0, "gat": 1.56, "fix": 50.0, "dl": 1900.0, "eps": 30.0,
-       "bias": "pidihnitrhzhadkraoonxwkoqeqazrgtoqvdclqirsneyzathiqaejnpptgnmgmlnzbinrluvopxwlljjnnrkuqbuljykrookhqkwtvkpkermvklmonyqsulmssqxtagrdiagxolcjzzgrytdofjoawtchltbuznljmlneqkqhrkaljzxwtqenrhkezgezcdqrcagyzfiitnuruqpspgymjtifgqspgfgipqocikhlkwprgrfnpiukwjqtzdppaaxftgtnrfnasdggzmqptamjcsgsdigcfujkjdnzwkuexccxavnjqhdvucnjnnlhroyibcamoodbluqgmvwlmpwsnfpogdwxkofclgmkmnzkliaaigmxrpztagspaxfldzgnpifwipzzlxwezqmbjnzrihovhzejaanmalzoriupidwphdtizxtoajajuzgaoqnjjhztgciujnnzkeynjoxtittcruiifonkazvzaukppxtunijipfgegivimtnuqlowzetucnkavmlikucaeawtwzowljuxojrtzjzxmxlzlyxsgdmdakzdqmjyrosjjayafmqsozjendamvaepttnlpmvmtaktnuajeqxvnaxjrrazwzamgaeqgfddxtkbvppxoxqspusojfgahmhzacdcdlfjqqrkqsfyssswjghzoffqnqddcmasamtlkimx"}
+CFG = {"HS": [80, 64, 80], "CH": 3, "NENG": 8, "SPLIT": 1, "MOVES": 40000,
+       "cyc": 0.92, "pe": 0.46, "lat": 150.0, "rlat": 3000.0, "gat": 1.56, "fix": 50.0, "dl": 1900.0, "eps": 30.0,
+       "bias": "afjzfvnaxjtcbekeagzooyowvpdcjzfwaczrxhyrxnawuvazktoaitozkwiakhszngteuqyxogtaihqvhjdfbtcgedlxyacewqqvgzebnhazyzaiaqzkyysebmnnekmztalpcwzvethggzowdakrxumvemmidqxyvhoqawwgtsgkewnhzzkzeialatrbbqeffclaaawfelafnhquawzpwzdmzenzbxipxylyzaatphjfoyxzzhamrmtdzazednwaxipwyzxaraznnezibmwmmwagyzchkogrhglqpzgrwhzmwiafeazmwcyjfafxrdiazaaazmnfgotcwynlogjkpqyapaioczzvsisiwrzzzsdokaeczzfrwzaidrfhadfpcbniderhzazwzezusazvzxvzdzmqhinvkatfqjxgcjaazhuxcoopnbdaatzzgztazlzzltrtniegbzfancaztlwdzczvlziovistyypwsararruzdvpudzhuidhgmhiifzlgecekeddzlzgtvajkrzkzjqmekkhhyozaqqfjixhtqfhqskwaxpadizlajavdiaaheachctdwaetccjrrjabapwiaaaxmaaczjccgqmzpsdcxuqvedisxcvldvvaalzsxolzpqyaenaamczaazbnmifsnprqzizpcbznaxxemyneyoifcmxmeanqjecjqjoizkspxhjlzidlduznaaarrftxiorgzn"}
+RATES = [{"cyc": 0.83, "pe": 0.42, "lat": 150.0, "gat": 1.56, "rlat": 3000.0, "dl": 1900.0},
+         {"cyc": 0.86, "pe": 0.44, "lat": 160.0, "gat": 1.15, "rlat": 4500.0, "dl": 2300.0},
+         {"cyc": 1.2, "pe": 0.6, "lat": 120.0, "gat": 1.8, "rlat": 3500.0, "dl": 1900.0}]
 HS = CFG["HS"]
 NB = len(HS)
 OFF = [sum(HS[:b]) for b in range(NB)]
@@ -20,8 +23,9 @@ COLS = ["r", "a", "b", "gt", "bS", "sub", "r256", "mv", "bm3", "nb3", "a2h", "m6
         "h32", "u0", "u1", "u2", "u3"]
 BF, F32, I32, U16 = "bfloat16", "float32", "int32", "uint16"
 SCRATCH = {}
-for _d, _l in ((BF, [("xw", NV), ("win", NV), ("ahi", 1024), ("alo", 1024), ("nn", 256), ("hb", 1), ("tab", 16),
-                     ("bt", 16 * (NM + 1)), ("mt", 16 * XW), ("hbm", 128), ("l2y", 128), ("l2q", 128), ("ni", 128),
+for _d, _l in ((BF, [("xw", NV), ("win", NV), ("ahi", 1024), ("alo", 1024), ("nn", 256), ("nh", 256), ("cc", NL), ("clo", NL),
+                     ("chi", NL), ("hb", 1),
+                     ("tab", 16), ("bt", 16 * (NM + 1)), ("mt", 16 * XW), ("hbm", 128), ("l2y", 128), ("l2q", 128), ("ni", 128),
                      ("w1", NL), ("gg", 4 * NL), ("pp", 17 * NL), ("cr", 17 * NL), ("eq", NL), ("sg", 2 * NL), ("l1o", NL),
                      ("js", NL), ("qq", NL), ("sd", NL), ("xv0", NL), ("xv1", NL), ("xv2", NL),
                      ("yy0", NL), ("yy1", NL), ("yy2", NL), ("yy3", NL)]),
@@ -79,9 +83,9 @@ def isreg(a):
     return isinstance(a, tuple)
 
 
-def build_ops():
+def build_ops(rate):
     ops = []
-    cyc, gat, fix = CFG["cyc"], CFG["gat"], CFG["fix"]
+    cyc, gat, pe, fix = rate["cyc"], rate["gat"], rate["pe"], CFG["fix"]
     grp, turn = [0], [0]
 
     def add(eng, kind, args, rd, wr, cost, same=False, **kw):
@@ -124,7 +128,7 @@ def build_ops():
     def mm(o, pairs):
         for k, (l, r) in enumerate(pairs):
             f = 4 if SCRATCH[l[0]][2] == F32 else 1
-            add("P", "mm", (o, l, r, k == 0, k == len(pairs) - 1), [l, r], [o], 10 + f * max(64, ncols(r)) * CFG["pe"], k > 0)
+            add("P", "mm", (o, l, r, k == 0, k == len(pairs) - 1), [l, r], [o], 10 + f * max(64, ncols(r)) * pe, k > 0)
 
     def iota(o, pat, base, cm):
         add("G", "iota", (o, pat, base, cm), [], [o], 160 + 2 * ncols(o) * cyc)
@@ -132,21 +136,18 @@ def build_ops():
     def sel(o, i, pat, base, cm, same=False):
         add("G", "sel", (o, i, pat, base, cm), [i], [o], 210 + 2 * ncols(o) * cyc, same)
 
-    def dma(q, o, i, nbytes, sem=None):
-        add(q, "dma", (o, i), [i], [o], 100, done=CFG["dl"] + nbytes / 200.0, sem=sem)
+    def dma(q, o, i, nbytes, sem=None, late=(), same=False):
+        add(q, "dma", (o, i), [i] + list(late), [o], 100, same, done=rate["dl"] + nbytes / 200.0, sem=sem)
 
     for u in range(2):
         for k in range(4):
             dma("YS"[k % 2], R("a32", 512 * u, 512 * u + 512, 1, 32 * k, 32 * k + 32),
                 R("adj", 2048 * u, 2048 * u + 2048, 1, k, 32, 4), 200000 * (u + 1))
     dma("S", R("v32", 0, 14), R("v0", 0, 14), 8000)
-    for b in range(NB):
-        o = 17 * OFF[b] + 16 * HS[b]
-        dma("S", R("cr", o, o + HS[b]), R("c0", OFF[b], OFF[b] + HS[b]), 30000)
-    dma("Y", R("xw", 0, NV), R("x", 0, NV), 1500000)
-    dma("Y", R("j32", 0, 14), R("j0", 0, 14), 8000)
-    dma("Y", R("yy0", 0, NL), R("y0", 0, NL), 60000)
-    dma("Y", R("hb", 0, 1), R("h", 0, 1), 8000)
+    dma("S", R("cc", 0, NL), R("c0", 0, NL), 300000)
+    dma("Y", R("xw", 0, NV, 1, 0, 64), R("x", 0, NV, 1, 0, 64), 1000000)
+    for k in (9, 10, 11, 13, 14, 15):
+        dma("Y", R("win", 0, NV, 1, k, 128, 16), R("x", 0, NV, 1, 0, 8), 1000000)
     iota(K("pc", 0), [[0, 1]], 0, 1)
     iota(R("q16", 0, 16), [[1, 16]], 0, 0)
     iota(R("nn", 0, 256), [[1, 256]], 0, 0)
@@ -156,17 +157,21 @@ def build_ops():
     cp(R("col", 0, 3), R("pc", 1, 4))
     r, a, b_ = C("r"), C("a"), C("b")
     ts(C("r256"), r, 256.0, None, A.mult)
-    ts(R("nn", 0, 256, 1, 0, 64), R("nn", 0, 256, 1, 0, 64), 0.0, C("r256")[:5] + (64, 1), A.mult, A.add)
-    for k in range(8):
-        dma("Y", R("win", 0, NV, 1, 16 * k + 8, 16 * k + 16), R("nn", 0, 256), 100000)
+    ts(R("nh", 0, 256), R("nn", 0, 256), 0.0, C("r256"), A.mult, A.add)
+    dma("Y", R("win", 0, NV, 1, 8, 128, 16), R("nh", 0, 256), 300000)
+    dma("Y", R("win", 0, NV, 1, 12, 128, 16), R("nn", 0, 256), 300000)
     for u in range(2):
         c0, c1 = 512 * u, 512 * u + 512
         cp(R("ahi", c0, c1), R("a32", c0, c1))
-        tt(R("alo", c0, c1), R("a32", c0, c1), R("ahi", c0, c1), A.subtract)
+        act(R("ps%d" % (6 + u), 0, 512), R("ahi", c0, c1), F.Copy)
+        tt(R("alo", c0, c1), R("a32", c0, c1), R("ps%d" % (6 + u), 0, 512), A.subtract)
         for j, t in enumerate(("ahi", "alo")):
             for k in range(4):
                 dma("YS"[u * j * (k % 2)], R("win", 4 * c0, 4 * c1, 1, 4 * j + k, 128, 16),
                     R(t, c0, c1, 1, 32 * k, 32 * k + 32), 80000)
+    dma("Y", R("xw", 0, NV, 1, 64, 128), R("x", 0, NV, 1, 64, 128), 300000, late=[R("alo", 512, 1024)], same=True)
+    for o, i in ((R("j32", 0, 14), R("j0", 0, 14)), (R("yy0", 0, NL), R("y0", 0, NL)), (R("hb", 0, 1), R("h", 0, 1))):
+        dma("Y", o, i, 100000, late=[R("alo", 512, 1024)])
     for c0, n, w, base in ((0, 4, 10, 16), (40, NM - 4, 8, 80)):
         x = R("xl", c0, c0 + n * w)
         iota(x, [[16, n], [-16, w]], base, 1)
@@ -264,7 +269,7 @@ def build_ops():
     def PS(name, b, n=None):
         h = HS[b]
         k, c = {"WQ": (0, 0), "U": (0, 1), "DF": (0, 2), "B2": (0, 3), "L2": (0, 4), "D3": (1, 0), "L1": (1, 1),
-                "L3": (1, 2), "LJ": (1, 3), "V0": (1, 3), "s": (2, 0), "d": (2, 1), "cn": (2, 2)}[name]
+                "L3": (1, 2), "LJ": (1, 3), "V0": (1, 3), "s": (2, 0), "d": (2, 1)}[name]
         t, c = (2 * b + k, c * h) if k < 2 else (6 + b % 2, (c + 3 * (b // 2)) * HM)
         return R("ps%d" % t, c, c + (h if n is None else n))
 
@@ -275,12 +280,13 @@ def build_ops():
 
     def update(b, k, last):
         h, o = HS[b], OFF[b]
-        c, y = R("cr", 17 * o + 16 * h, 17 * o + 17 * h), R("yy%d" % (k + 1), o, o + h)
+        c, y = R("cc", o, o + h), R("yy%d" % (k + 1), o, o + h)
         add("N", "recv", (k, b), [], [y], 0, after=("send", k, b))
-        mm(PS("d", b), [(R("ni", 0, 128), R("xv%d" % k, o, o + h)), (M("I"), y)])
-        act(R("sd", o, o + h), PS("d", b), F.Sign)
-        mm(PS("cn", b), [(M("I"), c), (M("I"), R("sd", o, o + h))])
-        ts(R("co32", o, o + h) if last else c, PS("cn", b), 15.0, -15.0, A.min, A.max)
+        ts(R("clo", o, o + h), c, -1.0, -15.0, A.add, A.max)
+        ts(R("chi", o, o + h), c, 1.0, 15.0, A.add, A.min)
+        mm(PS("d", b), [(M("I"), c), (R("ni", 0, 128), R("xv%d" % k, o, o + h)), (M("I"), y)])
+        tt(R("sd", o, o + h), PS("d", b), R("clo", o, o + h), A.max)
+        tt(R("co32", o, o + h) if last else c, R("sd", o, o + h), R("chi", o, o + h), A.min)
 
     for b in range(NB):
         h = HS[b]
@@ -294,7 +300,7 @@ def build_ops():
                 return R(buf, f * o + c0, f * (o + h), st)
             vk, ul, wq = R("lst", lo + h, lo + h + h // 16), R("lst", lo, lo + h), R("wq", o // 4, (o + h) // 4)
             p0 = 17 * o
-            c, pv = R("cr", p0 + 16 * h, p0 + 17 * h), R("pp", p0 + 16 * h, p0 + 17 * h)
+            c, pv = W("cc"), R("pp", p0 + 16 * h, p0 + 17 * h)
             act(W("w1"), IND(win, vk), F.Copy)
             mm(PS("WQ", b, h // 4), [(M("Zq", 12 - 4 * k), W("w1", 1, k, 4)) for k in range(4)])
             cp(wq, PS("WQ", b, h // 4))
@@ -338,11 +344,8 @@ def build_ops():
             ts(vk, W("sc", 1, 15, 16), C("sub"), None, A.subtract)
             if s % 2 == 1:
                 k = s // 2
-                if s < STEPS - 1:
-                    act(W("xv%d" % k), IND(xw, vk), F.Copy)
-                else:
-                    cp(W("xv%d" % k), IND(xw, vk))
-                add("G", "send", (k, b), [W("xv%d" % k)], [], 300, done=CFG["rlat"], key=("send", k, b))
+                cp(W("xv%d" % k), IND(xw, vk))
+                add("G", "send", (k, b), [W("xv%d" % k)], [], 300, done=rate["rlat"], key=("send", k, b))
             act(W("vsb"), PS("L3", b), F.Copy)
             if s < STEPS - 1:
                 act(W("js"), PS("L2", b), F.Sign, C("bL2"))
@@ -404,7 +407,7 @@ def schedule(ops, bias):
         full = d["cost"] + d.get("done", 0)
         prio[d["id"]] = max([full] + [(full + lat if h else d["cost"]) + prio[j] for j, h in succ[d["id"]]])
     for d in ops:
-        if d["grp"] < len(bias):
+        if d["grp"] < len(bias) and d["kind"] != "dma":
             prio[d["id"]] += 400.0 * (ord(bias[d["grp"]]) - 109)
     left = [len(d["deps"]) + len(d["soft"]) + len(d["order"]) for d in ops]
     rdy = [0.0] * n
@@ -426,6 +429,52 @@ def schedule(ops, bias):
             if left[j] == 0:
                 pool[ops[j]["eng"]].append(j)
     return seq
+
+
+def polish(ops, seq):
+    n = len(ops)
+    sets = [([d["cost"] for d in o], [d.get("done", 0) for d in o], z["lat"]) for o, z in [(build_ops(z), z) for z in RATES]]
+    hard = [d["deps"] + d["soft"] for d in ops]
+    pre = [set(d["deps"] + d["soft"] + d["order"]) for d in ops]
+    eng = ["VSPGYN".index(d["eng"]) for d in ops]
+
+    def span(order):
+        tot = 0.0
+        for cost, done, lat in sets:
+            free, t1 = [0.0] * 6, [0.0] * n
+            for i in order:
+                t = free[eng[i]]
+                for e in hard[i]:
+                    if t1[e] > t:
+                        t = t1[e]
+                t += cost[i]
+                free[eng[i]] = t
+                t1[i] = t + done[i] + lat
+            tot += max(t1) / cost[-2]
+        return tot
+    order = [d["id"] for d in seq]
+    best, z = span(order), 12345
+    for _ in range(CFG["MOVES"]):
+        z = (z * 1103515245 + 12345) % 2147483648
+        i, k = (z >> 8) % n, (1, 1, 1, 2, 3)[(z >> 3) % 5]
+        d, j = order[i], i
+        if eng[d] > 2 or ops[d]["kind"] == "dma":
+            continue
+        while k and j > 0:
+            j -= 1
+            k -= 1 if eng[order[j]] == eng[d] else 0
+        need, mv = set(pre[d]), set()
+        for e in reversed(order[j:i]):
+            if e in need:
+                mv.add(e)
+                need |= pre[e]
+        if k or order[j] in mv or ops[order[j]]["kind"] == "dma":
+            continue
+        c = order[:j] + [e for e in order[j:i] if e in mv] + [d] + [e for e in order[j:i] if e not in mv] + order[i + 1:]
+        s = span(c)
+        if s <= best:
+            order, best = c, s
+    return [ops[i] for i in order]
 
 
 def plan_waits(ops, seq):
@@ -459,9 +508,9 @@ def plan_waits(ops, seq):
     return final, sorted(cnt) + ["ya%d_%d" % (k, b) for k in range(3) for b in range(NB)]
 
 
-OPS = build_ops()
+OPS = build_ops(CFG)
 link(OPS)
-SEQ = schedule(OPS, CFG["bias"])
+SEQ = polish(OPS, schedule(OPS, CFG["bias"]))
 FINAL, SEMAPHORES = plan_waits(OPS, SEQ)
 
 

@@ -3,42 +3,48 @@ from concourse.mybir import AluOpType, ActivationFunctionType
 A = AluOpType
 F = ActivationFunctionType
 NV, NL, STEPS = 4096, 224, 6
-CFG = {"HS": [80, 64, 80], "CH": 3, "NENG": 8, "SPLIT": 1, "MOVES": 40000,
-       "cyc": 0.92, "pe": 0.46, "lat": 150.0, "rlat": 3000.0, "gat": 1.56, "fix": 50.0, "dl": 1900.0, "eps": 30.0,
-       "bias": "afjzfvnaxjtcbekeagzooyowvpdcjzfwaczrxhyrxnawuvazktoaitozkwiakhszngteuqyxogtaihqvhjdfbtcgedlxyacewqqvgzebnhazyzaiaqzkyysebmnnekmztalpcwzvethggzowdakrxumvemmidqxyvhoqawwgtsgkewnhzzkzeialatrbbqeffclaaawfelafnhquawzpwzdmzenzbxipxylyzaatphjfoyxzzhamrmtdzazednwaxipwyzxaraznnezibmwmmwagyzchkogrhglqpzgrwhzmwiafeazmwcyjfafxrdiazaaazmnfgotcwynlogjkpqyapaioczzvsisiwrzzzsdokaeczzfrwzaidrfhadfpcbniderhzazwzezusazvzxvzdzmqhinvkatfqjxgcjaazhuxcoopnbdaatzzgztazlzzltrtniegbzfancaztlwdzczvlziovistyypwsararruzdvpudzhuidhgmhiifzlgecekeddzlzgtvajkrzkzjqmekkhhyozaqqfjixhtqfhqskwaxpadizlajavdiaaheachctdwaetccjrrjabapwiaaaxmaaczjccgqmzpsdcxuqvedisxcvldvvaalzsxolzpqyaenaamczaazbnmifsnprqzizpcbznaxxemyneyoifcmxmeanqjecjqjoizkspxhjlzidlduznaaarrftxiorgzn"}
-RATES = [{"cyc": 0.83, "pe": 0.42, "lat": 150.0, "gat": 1.56, "rlat": 3000.0, "dl": 1900.0},
-         {"cyc": 0.86, "pe": 0.44, "lat": 160.0, "gat": 1.15, "rlat": 4500.0, "dl": 2300.0},
-         {"cyc": 1.2, "pe": 0.6, "lat": 120.0, "gat": 1.8, "rlat": 3500.0, "dl": 1900.0}]
-HS = CFG["HS"]
+CFG = {"HS": [64, 80, 80], "NENG": 8, "WQ": "S", "VK": "S", "UL": "S", "XV": "S", "DFS": 2, "ZB": (2, 0), "LJB": (2, 1),
+       "EQ": "E", "LAY": [(0, 1), (1, 2), (2, 5), (5, 8), (8, 11), (11, 13), (13, 16), (16, 18)], "GFILL": 1024, "WL": 40,
+       "VL": 0, "SPLIT": 2, "LATE": 64, "NR": "NNRNRN", "REP0": ["VVVVV", "GGGGG", "GGGGG"], "REP": "GGG",
+       "MODE": ["V", "V", "WS", "V", "WS", "V"],
+       "eps": 30.0, "T0": 8500.0, "T3": 2700.0, "TX": 2000.0, "SHAKES": 2200, "MOVES": 15000, "HEAT": 0.003, "SEED": 12345}
+RATES = [{"cyc": 0.83, "pe": 0.42, "lat": 150.0, "gat": 1.56, "rlat": 3000.0, "d0": 1300.0, "d1": 600.0, "bw": 400.0},
+         {"cyc": 0.86, "pe": 0.44, "lat": 160.0, "gat": 1.15, "rlat": 4500.0, "d0": 1500.0, "d1": 800.0, "bw": 280.0},
+         {"cyc": 1.2, "pe": 0.6, "lat": 120.0, "gat": 1.8, "rlat": 3500.0, "d0": 1300.0, "d1": 600.0, "bw": 400.0}]
+HS, MODE = CFG["HS"], CFG["MODE"]
 NB = len(HS)
 OFF = [sum(HS[:b]) for b in range(NB)]
 HM = max(HS)
-LW = [h + 2 * ((h // 16 + 1) // 2) for h in HS]
+LW = [h + h // 4 + 2 * ((h // 16 + 1) // 2) for h in HS]
 LOFF = [sum(LW[:b]) for b in range(NB)]
-MATS = ["Zq", "Zq3", "Zd", "Zs", "Uw", "Vm", "Blk", "Teq", "B20", "B21", "B22", "B23",
-        "L1sg", "L1su", "L1J", "L1eq", "L2l", "L2w", "L2J", "L2c", "I"]
+HALF = NV // 2
+MATS = ["Zq", "Zs", "Blk", "B20", "B21", "B22", "B23", "B2v", "Teq",
+        "L1sg", "L1su", "L1eq", "L1J", "L2l", "L2w", "L2J", "L2y", "L2r"]
 NM = len(MATS)
-XW = 40 + 8 * (NM - 4)
-COLS = ["r", "a", "b", "gt", "bS", "sub", "r256", "mv", "bm3", "nb3", "a2h", "m67", "bL1", "bL2", "bq", "t0", "t1", "na0",
-        "h32", "u0", "u1", "u2", "u3"]
-BF, F32, I32, U16 = "bfloat16", "float32", "int32", "uint16"
+XW = 20 + 8 * (NM - 2)
+NP = 16 * sum(LW)
+COLS = ["r", "a", "b", "gt", "ge", "sq", "bq", "ndg", "lt8", "bL13", "bS", "sub", "r256", "mv", "bL1", "bL2", "t0", "t1",
+        "na0", "na2", "zj", "zl", "h32", "u0", "u1", "u2", "u3", "u4", "u5"]
+BF, F16, F32, I32, U16 = "bfloat16", "float16", "float32", "int32", "uint16"
 SCRATCH = {}
-for _d, _l in ((BF, [("xw", NV), ("win", NV), ("ahi", 1024), ("alo", 1024), ("nn", 256), ("nh", 256), ("cc", NL), ("clo", NL),
-                     ("chi", NL), ("hb", 1),
-                     ("tab", 16), ("bt", 16 * (NM + 1)), ("mt", 16 * XW), ("hbm", 128), ("l2y", 128), ("l2q", 128), ("ni", 128),
-                     ("w1", NL), ("gg", 4 * NL), ("pp", 17 * NL), ("cr", 17 * NL), ("eq", NL), ("sg", 2 * NL), ("l1o", NL),
-                     ("js", NL), ("qq", NL), ("sd", NL), ("xv0", NL), ("xv1", NL), ("xv2", NL),
+for _d, _l in ((BF, [("xw", NV), ("vm", 128), ("k2", 128), ("hb", 1),
+                     ("tab", 16), ("bt", 16 * (NM + 1)), ("mt", 16 * XW), ("hbm", 128), ("ni", 128),
+                     ("Zq3", 144), ("Zd", 144), ("Uw", 128), ("L1eq3", 128),
+                     ("rep", 4 * HM), ("ct", 128 * NB), ("cc", NL), ("l3v", 128), ("l3j", 128), ("lzj", 128),
+                     ("pp", NP), ("cr", 16 * NL), ("eq", NL), ("sg", 2 * NL), ("l1o", NL),
+                     ("nvm", 128), ("sd", NL), ("xx0", NP), ("xx1", NP), ("xx2", NP), ("xx3", NP), ("eye", 128),
                      ("yy0", NL), ("yy1", NL), ("yy2", NL), ("yy3", NL)]),
-               (F32, [("col", len(COLS)), ("q16", 16), ("one", 16), ("ea", 4), ("eb", 4), ("le4", 4), ("e16", 16),
-                      ("lt16", 16), ("tmp", 16), ("xl", XW), ("l3v", 128), ("l3j", 128), ("scn", HM), ("t32", NL),
-                      ("vsb", NL), ("l2o", NL), ("sc", NL), ("co32", NL), ("jo32", NL)]),
-               (I32, [("a32", 1024), ("v32", 14), ("j32", 14), ("pc", 4), ("rl32", HM)]),
-               (U16, [("jl", 14), ("xu", XW), ("rl", HM), ("lst", sum(LW)), ("wq", NL // 4)])):
+               (F32, [("col", len(COLS)), ("q16", 16), ("one", 16), ("ea", 16), ("eb", 8), ("le4", 16), ("e16", 16),
+                      ("qa", 16), ("qb", 16), ("tmp", 40), ("xl", XW), ("scn", HM), ("t32", NL),
+                      ("vsb", NL), ("zo", NL), ("sc", NL), ("co32", NL), ("jo32", NL)]),
+               (F16, [("qq", NL), ("w1", NL), ("gg", 4 * NL), ("l2o", NL)]),
+               (I32, [("win", NV), ("nn", 256), ("v32", 14), ("j32", 14), ("pc", 4)]),
+               (U16, [("jl", 14), ("xu", XW), ("lst", sum(LW))])):
     for _n, _w in _l:
         SCRATCH[_n] = ("sbuf", [128, _w], _d)
 for _k in range(8):
     SCRATCH["ps%d" % _k] = ("psum", [128, 512], F32)
-DRAM = ("adj", "x", "c0", "y0", "h", "v0", "j0", "vo", "jo", "co")
+DRAM = {"adj": 4, "x": 2, "c0": 2, "y0": 2, "h": 2, "v0": 4, "j0": 4, "vo": 4, "jo": 4, "co": 4}
 
 
 def R(buf, c0, c1, st=1, p0=0, p1=128, ps=1):
@@ -58,12 +64,14 @@ def C(name):
 
 
 def xo(m):
-    return 10 * m if m < 4 else 40 + 8 * (m - 4)
+    return 10 * m if m < 2 else 20 + 8 * (m - 2)
 
 
 def M(name, shift=0):
-    i = 16 * xo(MATS.index(name)) + shift
-    return R("mt", i, i + 128)
+    if name not in MATS:
+        return R("eye" if name == "I" else name, shift, shift + 128)
+    m = MATS.index(name)
+    return R("mt", 16 * xo(m) + shift, 16 * xo(m) + shift + 128)
 
 
 def B(name, c0=0, c1=16, st=1):
@@ -71,12 +79,20 @@ def B(name, c0=0, c1=16, st=1):
     return R("bt", i + c0, i + c1, st)
 
 
+def top(r, n):
+    return r[:5] + (n,) + r[6:]
+
+
 def ncols(r):
     return 16 * ncols(r[2]) if r[0] == "ind" else len(range(r[1], r[2], r[3]))
 
 
+def size(r):
+    return DRAM[r[0]] if r[0] in DRAM else {BF: 2, F16: 2, U16: 2, F32: 4, I32: 4}[SCRATCH[r[0]][2]]
+
+
 def two(r):
-    return r[0] != "ind" and SCRATCH[r[0]][2] in (BF, U16)
+    return r[0] != "ind" and size(r) == 2
 
 
 def isreg(a):
@@ -85,16 +101,19 @@ def isreg(a):
 
 def build_ops(rate):
     ops = []
-    cyc, gat, pe, fix = rate["cyc"], rate["gat"], rate["pe"], CFG["fix"]
-    grp, turn = [0], [0]
+    cyc, gat, pe, fix = rate["cyc"], rate["gat"], rate["pe"], 50.0
+    turn, kept, age, region, seen = [0], [True], [None], [""], {}
 
-    def add(eng, kind, args, rd, wr, cost, same=False, **kw):
+    def add(eng, kind, args, rd, wr, cost, **kw):
         rr = []
         for a in rd:
             if isreg(a):
                 rr += [a[1], a[2]] if a[0] == "ind" else [a]
-        grp[0] += 0 if same else 1
-        d = {"eng": eng, "kind": kind, "args": args, "rd": rr, "wr": wr, "cost": cost, "id": len(ops), "grp": grp[0]}
+        d = {"eng": eng, "kind": kind, "args": args, "rd": rr, "wr": wr, "cost": cost, "id": len(ops), "done": 0.0, "busy": 0.0,
+             "turn": age[0]}
+        name = eng + (region[0] if eng == "P" else wr[0][0].rstrip("0123") if wr else kind)
+        seen[age[0], name] = seen.get((age[0], name), 0) + 1
+        d["tag"] = name + str(seen[age[0], name])
         d.update(kw)
         ops.append(d)
 
@@ -118,246 +137,333 @@ def build_ops(rate):
         c = 80 + gat * ncols(o) * cyc if i[0] == "ind" else fix + 30 + max(64, ncols(o)) * cyc
         add("S", "act", (o, i, fn, bias, scale), [i, bias, scale], [o], c)
 
-    def lin(o, i, scale):
+    def lin(o, i, scale, bias=0.0, eng=None):
         turn[0] += 1
-        if turn[0] % 3 < CFG["SPLIT"]:
-            act(o, i, F.Identity, 0.0, scale)
-        else:
+        if eng == "S" or (eng is None and turn[0] % 3 < CFG["SPLIT"]):
+            act(o, i, F.Identity, bias, scale)
+        elif bias == 0.0:
             ts(o, i, scale, None, A.mult)
+        else:
+            ts(o, i, scale, bias, A.mult, A.add)
 
-    def mm(o, pairs):
-        for k, (l, r) in enumerate(pairs):
-            f = 4 if SCRATCH[l[0]][2] == F32 else 1
-            add("P", "mm", (o, l, r, k == 0, k == len(pairs) - 1), [l, r], [o], 10 + f * max(64, ncols(r)) * pe, k > 0)
+    def copy(eng, o, i):
+        if eng == "S":
+            act(o, i, F.Copy)
+        else:
+            cp(o, i)
+
+    def mm(o, *units):
+        for k, unit in enumerate(units):
+            calls = [(l, r, k == 0 and j == 0, k == len(units) - 1 and j == len(unit) - 1) for j, (l, r) in enumerate(unit)]
+            cost = sum(10 + (size(l) // 2) ** 2 * max(min(64, ncols(l)), ncols(r)) * pe for l, r in unit)
+            add("P", "mm", (o, calls), [z for lr in unit for z in lr], [o], cost)
 
     def iota(o, pat, base, cm):
         add("G", "iota", (o, pat, base, cm), [], [o], 160 + 2 * ncols(o) * cyc)
 
-    def sel(o, i, pat, base, cm, same=False):
-        add("G", "sel", (o, i, pat, base, cm), [i], [o], 210 + 2 * ncols(o) * cyc, same)
+    def sel(o, i, pat, base, cm, op=A.is_ge, fill=0.0):
+        add("G", "sel", (o, i, pat, op, base, cm, fill), [i], [o], 210 + 2 * ncols(o) * cyc)
 
-    def dma(q, o, i, nbytes, sem=None, late=(), same=False):
-        add(q, "dma", (o, i), [i] + list(late), [o], 100, same, done=rate["dl"] + nbytes / 200.0, sem=sem)
+    def dma(q, o, i, sem=None):
+        nb = len(range(o[4], o[5], o[6])) * ncols(o) * size(o)
+        rows = nb / min(ncols(o) * size(o), ncols(i) * size(i))
+        add(q, "dma", (o, i), [i], [o], 100, done=rate["d1"], busy=rows * 1.5 + nb / rate["bw"], sem=sem, kept=kept[0])
 
-    for u in range(2):
-        for k in range(4):
-            dma("YS"[k % 2], R("a32", 512 * u, 512 * u + 512, 1, 32 * k, 32 * k + 32),
-                R("adj", 2048 * u, 2048 * u + 2048, 1, k, 32, 4), 200000 * (u + 1))
-    dma("S", R("v32", 0, 14), R("v0", 0, 14), 8000)
-    dma("S", R("cc", 0, NL), R("c0", 0, NL), 300000)
-    dma("Y", R("xw", 0, NV, 1, 0, 64), R("x", 0, NV, 1, 0, 64), 1000000)
-    for k in (9, 10, 11, 13, 14, 15):
-        dma("Y", R("win", 0, NV, 1, k, 128, 16), R("x", 0, NV, 1, 0, 8), 1000000)
+    cut, early = NV - CFG["GFILL"], 128 - CFG["LATE"]
+    dma("S", R("cc", 0, NL), R("c0", 0, NL))
+    dma("S", R("v32", 0, 14), R("v0", 0, 14))
+    if early:
+        dma("Y", R("xw", 0, NV, 1, 0, early), R("x", 0, NV, 1, 0, early))
+    for c0, c1 in ((0, cut // 2), (cut // 2, cut)):
+        ms(R("win", c0, c1), 2 * HALF)
+    if cut < NV:
+        iota(R("win", cut, NV), [[0, NV - cut]], 2 * HALF, 0)
     iota(K("pc", 0), [[0, 1]], 0, 1)
     iota(R("q16", 0, 16), [[1, 16]], 0, 0)
-    iota(R("nn", 0, 256), [[1, 256]], 0, 0)
+    iota(R("nn", 0, 256), [[1, 256]], 0, 256)
+    for c0, c1 in ((0, cut // 2), (cut // 2, NV)):
+        dma("Y", R("win", c0, c1, 1, 0, 128, 4), R("adj", c0, c1, 1, 0, 32))
+    ts(R("nn", 0, 256), R("nn", 0, 256), NV - 1, None, A.bitwise_and)
+    dma("Y", R("win", 0, NV, 1, 1, 128, 16), R("nn", 0, 256))
     ts(K("pc", 1), K("pc", 0), 15, None, A.bitwise_and)
     ts(K("pc", 2), K("pc", 0), 2, 3, A.logical_shift_right, A.bitwise_and)
     ts(K("pc", 3), K("pc", 0), 3, None, A.bitwise_and)
     cp(R("col", 0, 3), R("pc", 1, 4))
     r, a, b_ = C("r"), C("a"), C("b")
-    ts(C("r256"), r, 256.0, None, A.mult)
-    ts(R("nh", 0, 256), R("nn", 0, 256), 0.0, C("r256"), A.mult, A.add)
-    dma("Y", R("win", 0, NV, 1, 8, 128, 16), R("nh", 0, 256), 300000)
-    dma("Y", R("win", 0, NV, 1, 12, 128, 16), R("nn", 0, 256), 300000)
-    for u in range(2):
-        c0, c1 = 512 * u, 512 * u + 512
-        cp(R("ahi", c0, c1), R("a32", c0, c1))
-        act(R("ps%d" % (6 + u), 0, 512), R("ahi", c0, c1), F.Copy)
-        tt(R("alo", c0, c1), R("a32", c0, c1), R("ps%d" % (6 + u), 0, 512), A.subtract)
-        for j, t in enumerate(("ahi", "alo")):
-            for k in range(4):
-                dma("YS"[u * j * (k % 2)], R("win", 4 * c0, 4 * c1, 1, 4 * j + k, 128, 16),
-                    R(t, c0, c1, 1, 32 * k, 32 * k + 32), 80000)
-    dma("Y", R("xw", 0, NV, 1, 64, 128), R("x", 0, NV, 1, 64, 128), 300000, late=[R("alo", 512, 1024)], same=True)
-    for o, i in ((R("j32", 0, 14), R("j0", 0, 14)), (R("yy0", 0, NL), R("y0", 0, NL)), (R("hb", 0, 1), R("h", 0, 1))):
-        dma("Y", o, i, 100000, late=[R("alo", 512, 1024)])
-    for c0, n, w, base in ((0, 4, 10, 16), (40, NM - 4, 8, 80)):
+    if early < 128:
+        dma("Y", R("xw", 0, NV, 1, early, 128), R("x", 0, NV, 1, early, 128))
+    for o, i in ((R("hb", 0, 1), R("h", 0, 1)), (R("j32", 0, 14), R("j0", 0, 14)), (R("yy0", 0, NL), R("y0", 0, NL))):
+        dma("Y", o, i)
+    kept[0] = False
+    for c0, n, w, base in ((0, 2, 10, 16), (20, NM - 2, 8, 48)):
         x = R("xl", c0, c0 + n * w)
         iota(x, [[16, n], [-16, w]], base, 1)
         sel(x, x, [[0, n], [-16, w]], 0, 1)
         sel(x, x, [[0, n], [16, w]], 15, -1)
         cp(R("xu", c0, c0 + n * w), x)
-    iota(R("rl32", 0, HM), [[1, HM]], 0, 0)
     iota(R("scn", 0, HM), [[0, HM // 16], [1, 16]], 0, 0)
-    cp(R("rl", 0, HM), R("rl32", 0, HM))
-    ms(R("one", 0, 16), 1.0)
-    ms(R("bt", 0, 16 * (NM + 1)), 0.0)
-    q4, q16, o4, o16 = R("q16", 0, 4), R("q16", 0, 16), R("one", 0, 4), R("one", 0, 16)
-    ea, eb, e16 = R("ea", 0, 4), R("eb", 0, 4), R("e16", 0, 16)
-    ts(ea, q4, a, None, A.is_equal)
-    ts(eb, q4, b_, None, A.is_equal)
+    iota(R("one", 0, 16), [[0, 16]], 1, 0)
+    iota(R("bt", 0, 16 * (NM + 1)), [[0, 16 * (NM + 1)]], 0, 0)
+    q4, q16, o4, o8, o16 = R("q16", 0, 4), R("q16", 0, 16), R("one", 0, 4), R("one", 0, 8), R("one", 0, 16)
+    iota(R("qa", 0, 16), [[1, 4], [0, 4]], 0, 0)
+    iota(R("qb", 0, 16), [[0, 4], [1, 4]], 0, 0)
+    ea, eb, e16 = R("ea", 0, 16, 4), R("eb", 0, 4), R("e16", 0, 16)
+    ts(R("ea", 0, 16), R("qa", 0, 16), a, None, A.is_equal)
+    ts(R("eb", 0, 8), R("qb", 0, 8), b_, None, A.is_equal)
     ts(e16, q16, r, None, A.is_equal)
-    ts(R("lt16", 0, 16), q16, r, None, A.is_gt)
-    low, lt6, a0, a1, a2, e11 = K("lt16", 8), K("lt16", 6), K("ea", 0), K("ea", 1), K("ea", 2), K("e16", 11)
-    lin(B("Zq", 12, 16), eb, low)
-    lin(B("Zq3", 12, 15), R("eb", 0, 3), low)
-    lin(C("nb3"), K("eb", 3), -1.0)
-    ts(B("Zd", 12, 16), o4, C("nb3"), low, A.mult, A.mult)
-    ms(B("Zs", 15, 16), -1.0)
-    lin(B("Uw", 3, 16, 4), eb, low)
-    ts(C("mv"), K("e16", 8), K("e16", 12), None, A.add)
-    lin(B("Vm"), o16, C("mv"))
-    ms(B("Blk"), 1.0)
-    ts(R("le4", 0, 4), q4, b_, None, A.is_ge)
-    for k in range(3):
-        lin(B("Teq", k, 16, 4), ea, K("le4", k))
+    ts(R("le4", 0, 16), R("qb", 0, 16), b_, None, A.is_ge)
+    low, lt8 = K("eb", 0), C("lt8")
+    a0, a1, a2, a3, e11 = K("ea", 0), K("ea", 4), K("ea", 8), K("ea", 12), K("e16", 11)
+    ts(lt8, r, 8.0, -8192.0, A.is_lt, A.mult)
+    lin(B("Zq", 12, 16), ea, low)
+    lin(B("Zs", 15, 16), K("one", 0), -1.0)
+    lin(C("mv"), K("e16", 1), 1.0, K("e16", 2))
+    lin(B("Blk"), o16, 1.0)
+    tt(B("Teq"), R("ea", 0, 16), R("le4", 0, 16), A.mult)
     for m in range(4):
-        if m > 0:
-            lin(B("B2%d" % m, 4 * m, 5 * m), R("one", 0, m), 1.0)
+        lin(B("B2%d" % m, 4 * m, 5 * m + 1), R("one", 0, m + 1), 1.0)
         if m < 3:
             lin(B("B2%d" % m, 5 * m + 4, 16, 4), R("one", 0, 3 - m), -1.0)
-    ts(C("bS"), K("eb", 3), 0.5, -0.5, A.mult, A.add)
+    lin(B("B2v", 0, 16, 5), o4, -1.0)
     ts(C("gt"), a, b_, None, A.is_gt)
-    lin(C("a2h"), a2, 0.5)
-    ts(C("bm3"), b_, -3.0, None, A.add)
+    ts(C("ge"), a, b_, None, A.is_ge)
+    ts(C("ndg"), a, b_, -1.0, A.is_equal, A.mult)
+    lin(C("bS"), C("gt"), -0.5)
     lin(B("L1sg", 0, 4), ea, 1.0)
-    lin(B("L1sg", 4, 8), ea, C("nb3"))
-    ts(B("L1sg", 8, 12), ea, C("nb3"), 8.0, A.mult, A.mult)
-    tt(R("tmp", 0, 4), ea, eb, A.subtract)
-    lin(B("L1su", 4, 8), R("tmp", 0, 4), C("gt"))
-    ts(B("L1su", 8, 12), R("tmp", 0, 4), C("gt"), 8.0, A.mult, A.mult)
-    lin(B("L1J", 0, 4), eb, C("a2h"))
-    ts(B("L1J", 4, 8), o4, e11, -0.5, A.mult, A.mult)
-    ts(B("L1J", 8, 12), o4, e11, -4.0, A.mult, A.mult)
-    lin(B("L1eq", 8, 12), ea, C("bm3"))
-    lin(C("t0"), low, -3.5)
-    ts(C("bL1"), a2, -32.0, C("t0"), A.mult, A.add)
-    lin(C("na0"), a0, -4096.0)
-    ts(R("tmp", 4, 8), q4, b_, C("na0"), A.is_gt, A.mult)
-    ts(R("tmp", 8, 12), eb, low, 4096.0, A.mult, A.mult)
-    tt(B("L2l", 0, 4), R("tmp", 4, 8), R("tmp", 8, 12), A.add)
-    lin(B("L2l", 4, 5), a0, -4096.0)
-    lin(B("L2l", 5, 6), a1, -4096.0)
-    lin(B("L2l", 6, 7), a0, -16.0)
-    lin(B("L2l", 7, 8), a2, 1.0)
-    ts(C("t1"), a0, 8.0, a2, A.mult, A.subtract)
+    lin(B("L1su", 0, 4), ea, C("ndg"))
+    lin(R("tmp", 0, 4), ea, C("ge"))
+    lin(R("tmp", 12, 16), eb, C("gt"))
+    tt(B("L1su", 4, 8), R("tmp", 0, 4), R("tmp", 12, 16), A.subtract)
+    lin(B("L1su", 8, 12), B("L1su", 4, 8), 8.0)
+    ts(B("L1J", 0, 4), eb, a2, -8.0, A.mult, A.mult)
+    ts(B("L1J", 4, 12), o8, e11, 8.0, A.mult, A.mult)
+    lin(B("L1eq", 8, 12), ea, b_)
+    lin(C("t0"), a1, -7.0, -4.0)
+    lin(C("bL1"), a2, -35.0, C("t0"))
+    lin(C("bL13"), a2, -32.0, C("t0"))
+    o2 = R("one", 0, 2)
+    lin(C("na0"), a0, -8192.0)
+    ts(R("tmp", 32, 40), R("qb", 0, 8), b_, C("na0"), A.is_gt, A.mult)
+    lin(R("tmp", 4, 12), R("eb", 0, 8), lt8)
+    tt(B("L2l", 0, 8), R("tmp", 32, 40), R("tmp", 4, 12), A.subtract)
+    lin(C("t1"), a0, -4.0, a2)
     lin(B("L2l", 8, 12), o4, C("t1"))
-    lin(B("L2w", 0, 4), eb, low)
-    lin(B("L2w", 4, 5), C("mv"), 1.0)
-    lin(B("L2J", 4, 5), e11, 2048.0)
-    lin(B("L2J", 5, 6), e11, -2048.0)
-    ts(B("L2J", 6, 7), e11, 8.5, C("a2h"), A.mult, A.subtract)
+    lin(B("L2l", 12, 16, 2), o2, C("na0"))
+    ts(B("L2l", 13, 16, 2), o2, a1, -8192.0, A.mult, A.mult)
+    lin(B("L2w", 0, 4), ea, low)
+    lin(B("L2w", 4, 8), B("L2w", 0, 4), -1.0)
+    lin(B("L2w", 12, 13), K("e16", 1), 1.0)
+    lin(B("L2w", 14, 15), K("e16", 1), -1.0)
     ts(B("L2J", 8, 12), o4, e11, -4.0, A.mult, A.mult)
-    ms(B("L2c", 5, 6), 1.0)
-    lin(B("I"), e16, 1.0)
-    ts(C("u0"), b_, -3.5, a2, A.add, A.mult)
-    ts(C("u1"), K("e16", 4), -2048.0, C("u0"), A.mult, A.add)
-    ts(C("u2"), K("e16", 5), 4096.0 * 192 - 2048.0, C("u1"), A.mult, A.add)
-    ts(C("u3"), K("e16", 6), -2.5, C("u2"), A.mult, A.add)
-    ts(C("bL2"), C("na0"), C("u3"), None, A.add)
-    ts(C("m67"), lt6, -1.0, low, A.mult, A.add)
-    ms(C("bq"), 192.0 - 2047.5 / 4096.0)
-    ts(C("sub"), r, -4096.0, 15 * 4096.0, A.mult, A.add)
-    ts(R("scn", 0, HM), R("scn", 0, HM), r, 135168.0, A.is_gt, A.mult)
-    ts(R("scn", 0, HM), R("scn", 0, HM), -131072.0, None, A.add)
-    ts(R("tab", 0, 16), q16, b_, 2.0, A.is_le, A.mult)
-    ts(R("tab", 0, 16), R("tab", 0, 16), -1.0, None, A.add)
-    for m0, m1 in ((0, 1), (1, 3), (3, 4), (4, 6), (6, 9), (9, 12), (12, 14), (14, 16), (16, 18), (18, NM)):
-        n = xo(m1) - xo(m0) - (1 if m1 <= 4 else 0)
-        act(R("mt", 16 * xo(m0), 16 * (xo(m0) + n)), IND(R("bt", 0, 16 * (m1 + 1)), R("xu", xo(m0), xo(m0) + n)), F.Copy)
+    ts(B("L2J", 12, 16, 2), o2, e11, -8192.0, A.mult, A.mult)
+    ts(B("L2J", 13, 16, 2), o2, e11, 8192.0, A.mult, A.mult)
+    lin(B("L2r", 15, 16), K("e16", 1), 128.0)
+    lin(B("L2r", 13, 14), K("e16", 0), -4096.0, B("L2r", 15, 16))
+    lin(C("sq"), K("e16", 0), 1.0 / 4096 - 1.0 / 128, 1.0 / 128)
+    lin(C("bq"), K("e16", 0), 1.0 / 8192 - 1.0 / 256, 1535.5 + 1.0 / 256)
     cp(C("h32"), R("hb", 0, 1))
+    lin(B("L2y", 15, 16), C("h32"), -1.0)
+    lin(C("u0"), b_, -1.0, 4.0)
+    lin(C("u2"), C("u0"), a2, lt8)
+    lin(C("u3"), K("e16", 13), 1536.0 * (4096 - 128) - 8192, C("u2"))
+    lin(C("bL2"), K("e16", 15), HALF - 1536.0 * 128 - 8192, C("u3"))
+    lin(C("u4"), K("le4", 1), 2.0, -1.0)
+    ts(C("u5"), a0, a1, None, A.subtract)
+    lin(C("na2"), C("u4"), a3, C("u5"))
+    lin(C("sub"), r, 4096.0, -15 * 4096.0)
+    ts(R("scn", 0, HM), R("scn", 0, HM), r, 135168.0, A.is_gt, A.mult)
+    lin(R("scn", 0, HM), R("scn", 0, HM), 1.0, -131072.0)
+    ts(R("tmp", 16, 32), q16, 4.0, b_, A.min, A.subtract)
+    ts(R("tab", 0, 16), R("tmp", 16, 32), 0.0, a2, A.max, A.mult)
+    for m0, m1 in CFG["LAY"]:
+        n = xo(m1) - xo(m0) - (1 if m1 <= 2 else 0)
+        act(R("mt", 16 * xo(m0), 16 * (xo(m0) + n)), IND(R("bt", 0, 16 * (m1 + 1)), R("xu", xo(m0), xo(m0) + n)), F.Copy)
     lin(R("hbm", 0, 128), M("Blk"), C("h32"))
-    lin(R("l2y", 0, 128), M("L2c"), C("h32"))
-    ts(R("l2q", 0, 128), M("L2c"), K("e16", 0), -4096.0, A.mult, A.mult)
-    lin(R("ni", 0, 128), M("I"), -1.0)
-    lin(R("l3v", 0, 128), M("Blk"), lt6)
-    lin(R("l3j", 0, 128), M("Blk"), C("m67"))
+    for t, col in (("vm", C("mv")), ("l3v", C("na2"))):
+        lin(R(t, 0, 128), M("Blk"), col)
+    if CFG["EQ"] == "E":
+        lin(R("nvm", 0, 128), R("vm", 0, 128), -1.0)
+    eye, ni, slot = R("eye", 0, 128), R("ni", 0, 128), [[-16, 8], [0, 16]]
+    iota(eye, [[-1, 128]], 1, 1)
+    sel(eye, eye, [[-1, 128]], 0, 1, A.is_equal)
+    sel(ni, eye, [[-1, 128]], 0, 1, A.not_equal, -1.0)
+    sel(R("k2", 0, 128), M("Blk"), slot, -2, 1, A.is_equal)
+    zq, z3, zd, uw, q3 = R("mt", 0, 144), R("Zq3", 0, 144), R("Zd", 0, 144), R("Uw", 0, 128), R("L1eq3", 0, 128)
+    sel(z3, zq, [[0, 9], [1, 16]], -15, 0, A.not_equal)
+    sel(zd, z3, [[-16, 9], [256, 4], [0, 4]], -12 - 768, 1, A.not_equal, -1.0)
+    sel(uw, R("k2", 0, 128), [[-16, 8], [-4, 4], [256, 4]], -768, 1, A.not_equal, 1.0)
+    iota(q3, [[-16, 8], [0, 4], [-4, 4]], -3, 1)
+    sel(q3, q3, [[-16, 8], [256, 4], [-4, 4]], -512, 1)
+    sel(q3, q3, [[16, 8], [-256, 4], [4, 4]], 512 + 3, -1)
+    sel(R("l3j", 0, 128), M("Blk"), slot, -8, 1, A.is_equal)
+    sel(R("lzj", 0, 128), R("l3j", 0, 128), slot, -11, 1, A.not_equal, -256.0)
     cp(R("jl", 0, 14), R("j32", 0, 14))
-    act(R("js", 0, NL), IND(R("tab", 0, 16), R("jl", 0, 14)), F.Copy)
+    act(R("l2o", 0, NL), IND(R("tab", 0, 16), R("jl", 0, 14)), F.Copy)
+    rep = R("rep", 0, 4 * HM)
+    iota(rep, [[1, HM], [0, 4]], 1, -1)
+    sel(rep, rep, [[1, HM], [0, 4]], 0, -1, A.is_equal)
 
     def PS(name, b, n=None):
-        h = HS[b]
-        k, c = {"WQ": (0, 0), "U": (0, 1), "DF": (0, 2), "B2": (0, 3), "L2": (0, 4), "D3": (1, 0), "L1": (1, 1),
-                "L3": (1, 2), "LJ": (1, 3), "V0": (1, 3), "s": (2, 0), "d": (2, 1)}[name]
-        t, c = (2 * b + k, c * h) if k < 2 else (6 + b % 2, (c + 3 * (b // 2)) * HM)
-        return R("ps%d" % t, c, c + (h if n is None else n))
+        h, region[0] = HS[b], name
+        if name == "zT":
+            return top(R("ps%d" % (2 * b + 1), 384, 512), h)
+        k, c = {"WQ": (0, 0), "U": (0, 1), "DF": (0, 2), "B3": (2, 0), "L2": (0, 4), "B2": (1, 1), "D3": (1, 1), "U2": (1, 2), "L1": (1, 2),
+                "L3": (1, 0), "d": (1, 3), "c4": (1, 1), "c": (2, 1), "s": (0, 0), "r": (0, 5), "z": (1, 4), "Z": CFG["ZB"], "LJ": CFG["LJB"]}[name]
+        return R("ps%d" % (2 * b + k if k < 2 else 6 + b % 2), c * h, c * h + (h if n is None else n))
 
-    def chunks(h):
-        n = CFG["CH"]
-        e = [2 * ((h * k // n) // 2) for k in range(n)] + [h]
+    def chunks(h, n, first=0):
+        if first:
+            return [(0, first)] + [(first + l0, first + l1) for l0, l1 in chunks(h - first, n - 1)]
+        e = [2 * ((h * k // n + 1) // 2) for k in range(n)] + [h]
         return [(e[k], e[k + 1]) for k in range(n)]
 
-    def update(b, k, last):
+    def crep(b, st=1, at=0, l0=0, l1=None):
+        return R("cr", 16 * (OFF[b] + l0) + at, 16 * (OFF[b] + (HS[b] if l1 is None else l1)), st)
+
+    def move(eng, o, i):
+        if eng == "G":
+            sel(o, i, [[0, ncols(o)]], 0, 0)
+        else:
+            copy(eng, o, i)
+
+    def repeat(b, engs, st):
+        for eng in engs:
+            move(eng, crep(b, st, st // 2), crep(b, st))
+            st //= 2
+
+    def sign_of_change(b, k):
         h, o = HS[b], OFF[b]
-        c, y = R("cc", o, o + h), R("yy%d" % (k + 1), o, o + h)
+        y = R("yy%d" % (k + 1), o, o + h)
         add("N", "recv", (k, b), [], [y], 0, after=("send", k, b))
-        ts(R("clo", o, o + h), c, -1.0, -15.0, A.add, A.max)
-        ts(R("chi", o, o + h), c, 1.0, 15.0, A.add, A.min)
-        mm(PS("d", b), [(M("I"), c), (R("ni", 0, 128), R("xv%d" % k, o, o + h)), (M("I"), y)])
-        tt(R("sd", o, o + h), PS("d", b), R("clo", o, o + h), A.max)
-        tt(R("co32", o, o + h) if last else c, R("sd", o, o + h), R("chi", o, o + h), A.min)
+        mm(PS("d", b), [(R("ni", 0, 128), R("xx%d" % k, 16 * (LOFF[b] + h), 16 * (LOFF[b] + h) + h))], [(M("I"), y)])
+        act(R("sd", o, o + h), PS("d", b), F.Sign)
+
+    def vlist(b):
+        at = LOFF[b] + HS[b]
+        return R("lst", at, at + HS[b] // 16)
 
     for b in range(NB):
-        h = HS[b]
-        cp(R("lst", LOFF[b] + h, LOFF[b] + h + h // 16), R("v32", OFF[b] // 16, (OFF[b] + h) // 16))
+        cp(vlist(b), R("v32", OFF[b] // 16, (OFF[b] + HS[b]) // 16))
+    for b in range(NB):
+        move(CFG["REP0"][b][0], crep(b, 16), R("cc", OFF[b], OFF[b] + HS[b]))
+        repeat(b, CFG["REP0"][b][1:], 16)
     xw, win = R("xw", 0, NV), R("win", 0, NV)
     for s in range(STEPS):
         for b in range(NB):
             h, o, lo = HS[b], OFF[b], LOFF[b]
+            age[0] = (s, b)
 
             def W(buf, f=1, c0=0, st=1):
                 return R(buf, f * o + c0, f * (o + h), st)
-            vk, ul, wq = R("lst", lo + h, lo + h + h // 16), R("lst", lo, lo + h), R("wq", o // 4, (o + h) // 4)
-            p0 = 17 * o
-            c, pv = W("cc"), R("pp", p0 + 16 * h, p0 + 17 * h)
-            act(W("w1"), IND(win, vk), F.Copy)
+            wat, end, mode = LW[b] - h // 4, LW[b], (MODE[s].split("/") * NB)[b]
+            vk, ul, wq = vlist(b), R("lst", lo, lo + h), R("lst", lo + wat, lo + end)
+            p0, fresh, keep = 16 * lo, s in (2, 4), CFG["NR"][s] == "N"
+            pv, y = R("pp", p0 + 16 * h, p0 + 17 * h), W("yy%d" % (s // 2))
+            sg, su = R("sg", 2 * o, 2 * o + h), R("sg", 2 * o + h, 2 * o + 2 * h)
+            xx, ct = "xx%d" % (s // 2 - 1 if fresh else 3), top(R("ct", 128 * b, 128 * b + 128), h)
+            ident = top(R("eye", 0, h), h)
+
+            def weigh(l0, l1, weights):
+                tt(R("pp", p0 + 16 * l0, p0 + 16 * l1), IND(xw, R("lst", lo + l0, lo + l1)), weights, A.mult)
+
+            def second(name, first, st):
+                mm(PS(name, b), [(M("B2%d" % m), R("pp", first(m), first(m) + st * h, st)) for m in range(4)] + [(M("B2v"), pv)])
+                act(su, PS(name, b), F.Sign, C("bS"))
+            act(W("w1"), IND(win, vk), F.Identity, -float(HALF))
             mm(PS("WQ", b, h // 4), [(M("Zq", 12 - 4 * k), W("w1", 1, k, 4)) for k in range(4)])
-            cp(wq, PS("WQ", b, h // 4))
+            lin(wq, PS("WQ", b, h // 4), 1.0, float(HALF), eng=(CFG["WQ"] * 6)[s])
+            act(W("gg", 4), IND(win, wq), F.Identity, -float(HALF))
             if s == 0:
-                mm(PS("V0", b), [(M("Vm"), W("w1"))])
-                act(W("vsb"), PS("V0", b), F.Copy)
-            act(W("gg", 4), IND(win, wq), F.Copy)
-            mm(PS("U", b), [(M("Uw"), W("w1"))] + [(M("Zq3", 12 - 4 * i), W("gg", 4, i, 4)) for i in range(4)])
-            mm(PS("D3", b), [(M("Vm"), W("w1"))] + [(M("Zd", 12 - 4 * i), W("gg", 4, i, 4)) for i in range(4)])
-            tt(W("eq"), PS("U", b), W("vsb"), A.is_equal)
-            tt(W("t32"), PS("D3", b), W("eq"), A.mult)
-            tt(ul, PS("U", b), W("t32"), A.subtract)
-            if s % 2 == 0:
-                if s > 0:
-                    update(b, s // 2 - 1, False)
-                if s == 0 and b == NB - 1:
-                    for m in range(16):
-                        sel(R("cr", p0 + m, p0 + 16 * h, 16), c, [[0, h]], 0, 0, m > 0)
+                mm(PS("L3", b), [(R("vm", 0, 128), W("w1"))])
+                if set(MODE[0] + MODE[1]) & set("SW"):
+                    mm(PS("zT", b), [(R("cc", o, o + h), M("I"))])
+                    act(ct, PS("zT", b), F.Copy)
+            if not fresh:
+                weigh(h, h + h // 16, crep(b, 16))
+                weigh(wat, end, crep(b, 4))
+                second("B2", lambda m: p0 + 16 * wat + m, 4)
+                mm(PS("U", b), [(M("Zq", 12 - 4 * i), W("gg", 4, i, 4)) for i in range(4)])
+                lin(ul, PS("U", b), 1.0, float(HALF), eng=(CFG["UL"] * 6)[s])
+                tt(W("eq"), PS("L3", b), ul, A.is_equal)
+            else:
+                three = [(M("Zq3", 12 - 4 * i), W("gg", 4, i, 4)) for i in range(4)]
+                un = "U" if CFG["EQ"] != "E" else "U2"
+                if CFG["EQ"] == "E":
+                    mm(PS("U", b), [(M("Uw"), W("w1")), (R("nvm", 0, 128), W("w1"))], three)
+                    ts(W("eq"), PS("U", b), 0.0, None, A.is_equal)
+                    mm(PS("D3", b), [(M("Zd", 12 - 4 * i), W("gg", 4, i, 4)) for i in range(4)])
+                    mm(PS("U2", b), [(M("Uw"), W("w1"))] + three)
                 else:
-                    for l0, l1 in chunks(h):
-                        act(R("cr", p0 + 16 * l0, p0 + 16 * l1), IND(c, R("rl", l0, l1)), F.Copy)
-                mm(PS("s", b), [(R("hbm", 0, 128), W("yy%d" % (s // 2)))])
-                act(W("qq"), PS("s", b), F.Identity, C("bq"), 1.0 / 4096.0)
-            tt(pv, IND(xw, vk), c, A.mult)
-            for l0, l1 in chunks(h):
-                tt(R("pp", p0 + 16 * l0, p0 + 16 * l1), IND(xw, R("lst", lo + l0, lo + l1)),
-                   R("cr", p0 + 16 * l0, p0 + 16 * l1), A.mult)
-            mm(PS("DF", b), [(M("Blk"), pv), (M("Teq"), W("eq"))]
-               + [(M("Zs", 15 - m), R("pp", p0 + m, p0 + 16 * h, 16)) for m in range(16)])
-            mm(PS("B2", b), [(M("B2%d" % m), R("pp", p0 + 4 * m + 3, p0 + 16 * h, 16)) for m in range(4)])
-            act(W("sg", 2), PS("DF", b, 2 * h), F.Sign, C("bS"))
-            mm(PS("L1", b), [(M("L1J"), W("js")), (M("L1eq"), W("eq")), (M("L1sg"), R("sg", 2 * o, 2 * o + h)),
-                             (M("L1su"), R("sg", 2 * o + h, 2 * o + 2 * h))])
-            act(W("l1o"), PS("L1", b), F.Relu, C("bL1"))
-            mm(PS("L2", b), [(M("L2w"), W("w1")), (M("L2J"), W("js")), (R("l2y", 0, 128), W("yy%d" % (s // 2))),
-                             (R("l2q", 0, 128), W("qq")), (M("L2l"), W("l1o"))])
+                    mm(PS("U", b), [(M("Uw"), W("w1"))], three)
+                    mm(PS("D3", b), [(M("Zd", 12 - 4 * i), W("gg", 4, i, 4)) for i in range(4)])
+                    tt(W("eq"), PS("U", b), W("vsb"), A.is_equal)
+                tt(W("t32"), PS("D3", b), W("eq"), A.mult)
+                tt(ul, PS(un, b), W("t32"), A.subtract)
+            late = h
+            for (l0, l1), m in zip(chunks(h, len(mode), CFG["WL" if fresh else "VL"]), mode):
+                if m == "V":
+                    weigh(l0, l1, crep(b, 1, 0, l0, l1))
+                else:
+                    late = min(late, l0)
+                    copy("S" if m == "S" else "V", R(xx, p0 + 16 * l0, p0 + 16 * l1), IND(xw, R("lst", lo + l0, lo + l1)))
+            if fresh:
+                sign_of_change(b, s // 2 - 1)
+                mm(PS("zT", b), [(W("cc"), M("I")) if s == 2 else (ident, ct)], [(W("sd"), M("I"))])
+                ts(ct, PS("zT", b), -15.0, 15.0, A.max, A.min)
+            if late < h:
+                c4 = PS("c4", b, 4 * (h - late))
+                mm(c4, [(ct, top(R("rep", 4 * late, 4 * h), h))])
+            if fresh:
+                st = 2 ** len(CFG["REP"])
+                mm(PS("c", b, 16 * h // st), [(ct, top(R("rep", 0, 4 * h, st // 4), h))])
+                act(crep(b, st), PS("c", b, 16 * h // st), F.Copy)
+                repeat(b, CFG["REP"], st)
+                tt(pv, c4[:3] + (4,) + c4[4:], R(xx, p0 + 16 * h, p0 + 17 * h), A.mult)
+            if late < h:
+                for k in (3, 0, 1, 2):
+                    tt(R("pp", p0 + 16 * late + k, p0 + 16 * h, 4), c4, R(xx, p0 + 16 * late + k, p0 + 16 * h, 4), A.mult)
+                    if fresh and k == 3:
+                        second("B3", lambda m: p0 + 4 * m + 3, 16)
+            if s % 2 == 0:
+                mm(PS("s", b), [(R("hbm", 0, 128), y)])
+                act(W("qq"), PS("s", b), F.Identity, C("bq"), C("sq"))
+            sums = [(M("Zs", 15 - m), R("pp", p0 + m, p0 + 16 * h, 16)) for m in range(16)]
+            units = [sums[k::4] for k in (3, 0, 1, 2)] if late < h else [sums[k::CFG["DFS"]] for k in range(CFG["DFS"])]
+            mm(PS("DF", b), [(M("Teq"), W("eq")), (M("Blk"), pv)], *units)
+            act(sg, PS("DF", b), F.Sign, -0.5)
+            mm(PS("L1", b), [(M("L1J"), W("l2o")), (M("L1eq3" if fresh else "L1eq"), W("eq")), (M("L1su"), su)],
+               [(M("L1sg"), sg)])
+            act(W("l1o"), PS("L1", b), F.Relu, C("bL1" if keep else "bL13"))
+            mm(PS("L2", b), [(M("L2w"), W("w1")), (M("L2J"), W("l2o")), (M("L2y"), y), (M("L2r"), W("qq"))],
+               [(M("L2l"), W("l1o"))])
+            if s == STEPS - 1:
+                mm(PS("Z", b), [(R("lzj", 0, 128), W("l2o"))], [(M("L2l"), W("l1o"))])
+                act(W("zo"), PS("Z", b), F.Relu)
             act(W("l2o"), PS("L2", b), F.Relu, C("bL2"))
-            mm(PS("L3", b), [(R("l3v", 0, 128), W("l2o"))])
+            mm(PS("L3", b), [(R("k2", 0, 128), W("w1"))], [(R("l3v", 0, 128), W("l2o"))])
             add("V", "scan", (W("sc"), R("scn", 0, h), PS("L3", b)), [R("scn", 0, h), PS("L3", b)], [W("sc")],
                 fix + max(64, h) * cyc)
-            ts(vk, W("sc", 1, 15, 16), C("sub"), None, A.subtract)
+            lin(vk, W("sc", 1, 15, 16), 1.0, C("sub"), eng=(CFG["VK"] * 6)[s])
             if s % 2 == 1:
                 k = s // 2
-                cp(W("xv%d" % k), IND(xw, vk))
-                add("G", "send", (k, b), [W("xv%d" % k)], [], 300, done=rate["rlat"], key=("send", k, b))
-            act(W("vsb"), PS("L3", b), F.Copy)
-            if s < STEPS - 1:
-                act(W("js"), PS("L2", b), F.Sign, C("bL2"))
-            else:
+                xv = R("xx%d" % k, p0 + 16 * h, p0 + 17 * h)
+                copy(CFG["XV"], xv, IND(xw, vk))
+                add("G", "send", (k, b), [xv], [], 300, done=rate["rlat"], key=("send", k, b))
+            if s < STEPS - 1 and CFG["NR"][s + 1] == "R" and CFG["EQ"] != "E":
+                act(W("vsb"), PS("L3", b), F.Copy)
+            if s == STEPS - 1:
+                act(W("vsb"), PS("L3", b), F.Copy)
                 mm(PS("LJ", b), [(R("l3j", 0, 128), W("l2o"))])
-                act(W("jo32"), PS("LJ", b), F.Copy)
-    dma("Y", R("vo", 0, NL, 1, 0, 8), R("vsb", 0, NL, 1, 0, 128, 16), 3000, "out")
-    dma("Y", R("jo", 0, NL, 1, 0, 8), R("jo32", 0, NL, 1, 0, 128, 16), 3000, "out")
+                tt(W("jo32"), PS("LJ", b), W("zo"), A.add)
+    dma("Y", R("vo", 0, NL, 1, 0, 8), R("vsb", 0, NL, 1, 0, 128, 16), "out")
+    dma("Y", R("jo", 0, NL, 1, 0, 8), R("jo32", 0, NL, 1, 12, 128, 16), "out")
     for b in range(NB):
         h, o = HS[b], OFF[b]
-        update(b, 2, True)
-        dma("Y", R("co", o, o + h), R("co32", o, o + h), 40000, "out")
+        age[0] = (STEPS, b)
+        sign_of_change(b, 2)
+        mm(PS("z", b), [(M("I"), crep(b, 16))], [(M("I"), R("sd", o, o + h))])
+        ts(R("co32", o, o + h), PS("z", b), -15.0, 15.0, A.max, A.min)
+        dma("Y", R("co", o, o + h), R("co32", o, o + h), "out")
     return ops
 
 
@@ -388,14 +494,17 @@ def link(ops):
             hl.append((d, reg, w))
             if reg[0].startswith("ps"):
                 bank[reg[0]][d["eng"]] = d
+        if d.get("kept"):
+            order |= {keys[d["eng"]]} if d["eng"] in keys else set()
+            keys[d["eng"]] = d["id"]
         if "key" in d:
             keys[d["key"]] = d["id"]
         d["soft"] = [keys[d["after"]]] if "after" in d else []
         d["deps"], d["order"] = ([] if d["kind"] == "recv" else sorted(deps)), sorted(order - deps)
 
 
-def schedule(ops, bias):
-    lat, eps, n = CFG["lat"], CFG["eps"], len(ops)
+def schedule(ops, rate):
+    lat, eps, n = rate["lat"], CFG["eps"], len(ops)
     succ = [[] for _ in range(n)]
     for d in ops:
         for e in d["deps"] + d["soft"]:
@@ -404,14 +513,11 @@ def schedule(ops, bias):
             succ[e].append((d["id"], False))
     prio = [0.0] * n
     for d in reversed(ops):
-        full = d["cost"] + d.get("done", 0)
+        full = d["cost"] + d["done"] + (d["busy"] + rate["d0"] if d["busy"] else 0)
         prio[d["id"]] = max([full] + [(full + lat if h else d["cost"]) + prio[j] for j, h in succ[d["id"]]])
-    for d in ops:
-        if d["grp"] < len(bias) and d["kind"] != "dma":
-            prio[d["id"]] += 400.0 * (ord(bias[d["grp"]]) - 109)
     left = [len(d["deps"]) + len(d["soft"]) + len(d["order"]) for d in ops]
     rdy = [0.0] * n
-    free = {e: 0.0 for e in "VSPGYN"}
+    free, pipe = {e: 0.0 for e in "VSPGYN"}, 0.0
     pool = {e: [d["id"] for d in ops if d["eng"] == e and left[d["id"]] == 0] for e in free}
     seq = []
     while len(seq) < n:
@@ -419,46 +525,193 @@ def schedule(ops, bias):
         i = max([j for j in pool[e] if rdy[j] <= t + eps], key=lambda j: prio[j])
         pool[e].remove(i)
         d = ops[i]
-        d["t0"] = max(free[e], rdy[i])
-        free[e] = d["t0"] + d["cost"]
-        d["t1"] = free[e] + d.get("done", 0)
+        t0 = max(free[e], rdy[i])
+        free[e] = t1 = t0 + d["cost"]
+        if d["busy"]:
+            pipe = t1 = max(pipe, t1 + rate["d0"]) + d["busy"]
         seq.append(d)
+        d["t0"], d["t1"] = t0, t1 + d["done"] + lat
         for j, h in succ[i]:
-            rdy[j] = max(rdy[j], d["t1"] + lat if h else d["t0"])
+            rdy[j] = max(rdy[j], t1 + d["done"] + lat if h else t0)
             left[j] -= 1
             if left[j] == 0:
                 pool[ops[j]["eng"]].append(j)
     return seq
 
 
-def polish(ops, seq):
-    n = len(ops)
-    sets = [([d["cost"] for d in o], [d.get("done", 0) for d in o], z["lat"]) for o, z in [(build_ops(z), z) for z in RATES]]
-    hard = [d["deps"] + d["soft"] for d in ops]
-    pre = [set(d["deps"] + d["soft"] + d["order"]) for d in ops]
-    eng = ["VSPGYN".index(d["eng"]) for d in ops]
+def stagger(ops, rate):
+    schedule(ops, rate)
+    free, t0, t1, off = {}, {}, {}, {}
 
-    def span(order):
-        tot = 0.0
-        for cost, done, lat in sets:
-            free, t1 = [0.0] * 6, [0.0] * n
-            for i in order:
+    def start(turn):
+        return CFG["T0"] + CFG["T3"] * (NB * turn[0] + turn[1]) + CFG["TX"] * (turn[0] // 2)
+    for d in ops:
+        i = d["id"]
+        if d["turn"] is None:
+            t0[i], t1[i] = d["t0"], d["t1"]
+            continue
+        s, b = d["turn"]
+        t = max([free.get((d["eng"], b), 0.0)] + [t1[e] for e in d["deps"] + d["soft"]] + [t0[e] + 1 for e in d["order"]])
+        if d["tag"] == ("PU1" if CFG["NR"][min(s, STEPS - 1)] == "N" else "PU2"):
+            t = max(t, start(d["turn"]))
+        t0[i], free[d["eng"], b] = t, t + d["cost"]
+        t1[i] = t + d["cost"] + d["done"] + rate["lat"] + (d["busy"] + rate["d0"] if d["busy"] else 0)
+        if b == 0:
+            off[s, d["tag"]] = t - start(d["turn"])
+    at = []
+    for d in ops:
+        t = t0[d["id"]] if d["turn"] is None else start(d["turn"]) + off.get((d["turn"][0], d["tag"]), 0.0)
+        at.append(max([t] + [at[e] + 1 for e in d["deps"] + d["soft"] + d["order"]]))
+    return [ops[i] for i in sorted(range(len(ops)), key=lambda i: at[i])]
+
+
+def draws(seed):
+    z = [seed]
+
+    def rnd():
+        z[0] = (z[0] * 1103515245 + 12345) % 2147483648
+        return (z[0] >> 7) / 16777216.0
+    return rnd
+
+
+def justify(ops, seq, rate):
+    n, span, rnd = len(ops), timer(ops)[0], draws(CFG["SEED"])
+    cost, eng = [d["cost"] for d in ops], ["VSPGYN".index(d["eng"]) for d in ops]
+    lag = [d["done"] + rate["lat"] + (d["busy"] + rate["d0"] if d["busy"] else 0) for d in ops]
+    order = [d["id"] for d in seq]
+    t1, free, key = span(order)[1][0], [0.0] * 6, [0.0] * n
+    for i in order:
+        key[i] = max([free[eng[i]]] + [t1[e] for e in ops[i]["deps"] + ops[i]["soft"]])
+        free[eng[i]] = key[i] + cost[i]
+        if ops[i].get("kept"):
+            lag[i] = t1[i] - free[eng[i]]
+    pre = [[(e, lag[e]) for e in d["deps"] + d["soft"]] + [(e, 0.0) for e in d["order"]] for d in ops]
+    suc = [[] for _ in ops]
+    for i in range(n):
+        for e, g in pre[i]:
+            suc[e].append((i, g))
+
+    def rank(key, edges):
+        at = [0.0] * n
+        for i in (range(n) if edges is pre else range(n - 1, -1, -1)):
+            t = key[i]
+            for e, g in edges[i]:
+                if at[e] >= t:
+                    t = at[e] + 1e-3
+            at[i] = t
+        return sorted(range(n), key=lambda i: at[i])
+
+    def pack(key, edges, first):
+        st, en, end = [[] for _ in range(6)], [[] for _ in range(6)], [0.0] * n
+        for i in rank(key, edges):
+            t, c = first[i], cost[i]
+            for e, g in edges[i]:
+                if end[e] + g > t:
+                    t = end[e] + g
+            if c > 0:
+                a, b = st[eng[i]], en[eng[i]]
+                k = m = len(a)
+                while k and b[k - 1] > t:
+                    k -= 1
+                while k < m and a[k] < t + c - 1e-6:
+                    t = b[k]
+                    k += 1
+                a.insert(k, t)
+                b.insert(k, t + c)
+            end[i] = t + c
+        return end
+
+    def both(key):
+        zero, best = [0.0] * n, None
+        end = pack(key, pre, zero)
+        while True:
+            whole = max([e + g for e, g in zip(end, lag)])
+            if best is not None and whole >= best[0] - 5:
+                return best
+            best = (whole, [e - c for e, c in zip(end, cost)])
+            end = pack([-e for e in pack([-e for e in end], suc, lag)], pre, zero)
+    whole, st = both(key)
+    keep = rank(st, pre)
+    base = span(keep)[0]
+    now = best = len(base)
+    for it in range(CFG["SHAKES"]):
+        c, w = rnd() * whole, (3000.0, 8000.0, 20000.0)[it % 3]
+        whole, new = both([x + ((rnd() + rnd() - 1) * 1200 if abs(x - c) < w and rnd() < 1000 / w else 0) for x in st])
+        order = rank(new, pre)
+        s = sum(t / t0 for t, t0 in zip(span(order)[0], base))
+        if s <= now + 0.004 * rnd():
+            now, st = s, new
+            if s < best:
+                best, keep = s, order
+    return [ops[i] for i in keep]
+
+
+def timer(ops):
+    sets = [([d["cost"] for d in o], [d["done"] + z["lat"] for d in o], [d["busy"] for d in o], z["d0"])
+            for o, z in [(build_ops(z), z) for z in RATES]]
+    hard = [d["deps"] + d["soft"] for d in ops]
+    eng, n = ["VSPGYN".index(d["eng"]) for d in ops], len(ops)
+
+    def span(order, at=0, old=None):
+        ends, all_t1 = [], []
+        for k, (cost, done, busy, d0) in enumerate(sets):
+            free, t1, pipe = [0.0] * 6, (list(old[k]) if at else [0.0] * (2 * len(ops))), 0.0
+            seen, j = set(), at - 1
+            while j >= 0 and len(seen) < 7:
+                i = order[j]
+                if eng[i] not in seen:
+                    seen.add(eng[i])
+                    free[eng[i]] = t1[n + i]
+                if busy[i] and 6 not in seen:
+                    seen.add(6)
+                    pipe = t1[i] - done[i]
+                j -= 1
+            for i in order[at:]:
                 t = free[eng[i]]
                 for e in hard[i]:
                     if t1[e] > t:
                         t = t1[e]
                 t += cost[i]
-                free[eng[i]] = t
-                t1[i] = t + done[i] + lat
-            tot += max(t1) / cost[-2]
-        return tot
+                free[eng[i]] = t1[n + i] = t
+                if busy[i]:
+                    pipe = t = max(pipe, t + d0) + busy[i]
+                t1[i] = t + done[i]
+            ends.append(max(t1))
+            all_t1.append(t1)
+        return ends, all_t1
+
+    def held(order, all_t1):
+        before, last, out = {}, {}, []
+        for i in order:
+            before[i] = last.get(eng[i])
+            last[eng[i]] = i
+        for (cost, done, busy, d0), t1 in zip(sets, all_t1):
+            i = t1.index(max(t1))
+            while i is not None:
+                e = max(hard[i], key=lambda j: t1[j]) if hard[i] else None
+                p = before[i]
+                if p is not None and (e is None or t1[n + p] >= t1[e]):
+                    out.append(i)
+                    e = p
+                i = e
+        return out
+    return span, held
+
+
+def polish(ops, seq):
+    span, held = timer(ops)
+    pre = [set(d["deps"] + d["soft"] + d["order"]) for d in ops]
+    eng = [d["eng"] for d in ops]
     order = [d["id"] for d in seq]
-    best, z = span(order), 12345
-    for _ in range(CFG["MOVES"]):
-        z = (z * 1103515245 + 12345) % 2147483648
-        i, k = (z >> 8) % n, (1, 1, 1, 2, 3)[(z >> 3) % 5]
-        d, j = order[i], i
-        if eng[d] > 2 or ops[d]["kind"] == "dma":
+    base, t1 = span(order)
+    now = best = len(base)
+    keep, rnd, moves = order, draws(CFG["SEED"]), CFG["MOVES"]
+    pick = held(order, t1)
+    for it in range(moves):
+        d = pick[int(rnd() * len(pick))] if it % 5 else order[int(rnd() * len(order))]
+        k = (1, 1, 1, 2, 2, 3)[int(rnd() * 6)]
+        i = j = order.index(d)
+        if eng[d] == "N" or ops[d].get("kept"):
             continue
         while k and j > 0:
             j -= 1
@@ -468,23 +721,27 @@ def polish(ops, seq):
             if e in need:
                 mv.add(e)
                 need |= pre[e]
-        if k or order[j] in mv or ops[order[j]]["kind"] == "dma":
+        if k or order[j] in mv or ops[order[j]].get("kept"):
             continue
         c = order[:j] + [e for e in order[j:i] if e in mv] + [d] + [e for e in order[j:i] if e not in mv] + order[i + 1:]
-        s = span(c)
-        if s <= best:
-            order, best = c, s
-    return [ops[i] for i in order]
+        ends, new = span(c, j, t1)
+        s = sum(t / t0 for t, t0 in zip(ends, base))
+        if s <= now + CFG["HEAT"] * (1 - it / moves) * rnd() ** 2:
+            order, now, t1, pick = c, s, new, held(c, new)
+            if s < best:
+                best, keep = s, c
+    return [ops[i] for i in keep]
 
 
 def plan_waits(ops, seq):
-    cnt, known, top, nd = {}, {e: {} for e in "VSPGY"}, {}, 0
+    cnt, known, most, nd = {}, {e: {} for e in "VSPGY"}, {}, 0
+    place = {d["id"]: i for i, d in enumerate(seq)}
     for d in seq:
         if d["kind"] == "recv":
             d["sig"], d["know"] = ("ya%d_%d" % d["args"], CFG["NENG"]), {}
             continue
         kn, need = known[d["eng"]], {}
-        for e in sorted(d["deps"], key=lambda j: -ops[j]["t1"]):
+        for e in sorted(d["deps"], key=lambda j: -place[j]):
             s, v = ops[e]["sig"]
             if kn.get(s, 0) < v:
                 need[s] = max(need.get(s, 0), v)
@@ -493,7 +750,7 @@ def plan_waits(ops, seq):
                     kn[s2] = max(kn.get(s2, 0), v2)
         d["waits"] = sorted(need.items())
         for s, v in d["waits"]:
-            top[s] = max(top.get(s, 0), v)
+            most[s] = max(most.get(s, 0), v)
         d["know"] = dict(kn)
         if d["kind"] == "dma":
             s, inc = d["sem"] or "d%d" % nd, 16
@@ -501,16 +758,16 @@ def plan_waits(ops, seq):
         elif d["kind"] == "send":
             s, inc = "sent", CFG["NENG"]
         else:
-            s, inc = "e" + d["eng"], 1
+            s, inc = "e" + d["eng"], len(d["args"][1]) if d["kind"] == "mm" else 1
         cnt[s] = cnt.get(s, 0) + inc
         d["sig"] = (s, cnt[s])
-    final = sorted([(s, v) for s, v in cnt.items() if top.get(s, 0) < v], key=lambda z: z[0] == "out")
+    final = sorted([(s, v) for s, v in cnt.items() if most.get(s, 0) < v], key=lambda z: z[0] == "out")
     return final, sorted(cnt) + ["ya%d_%d" % (k, b) for k in range(3) for b in range(NB)]
 
 
-OPS = build_ops(CFG)
+OPS = build_ops(RATES[0])
 link(OPS)
-SEQ = polish(OPS, schedule(OPS, CFG["bias"]))
+SEQ = polish(OPS, justify(OPS, stagger(OPS, RATES[0]), RATES[0]))
 FINAL, SEMAPHORES = plan_waits(OPS, SEQ)
 
 
@@ -530,7 +787,7 @@ def rank_program(g, core, T, topo):
             return ap(r[1]).indirect(ap(r[2]))
         if r[0] == "h":
             return T["h"][:]
-        return T[r[0]][slice(r[4], r[5], r[6] if r[6] > 1 else None), slice(r[1], r[2], r[3] if r[3] > 1 else None)]
+        return T[r[0]][slice(r[4], r[5], r[6] if r[6] > 1 else None), slice(r[1], r[1] + (ncols(r) - 1) * r[3] + 1, r[3] if r[3] > 1 else None)]
 
     for d in SEQ:
         k = d["kind"]
@@ -542,7 +799,7 @@ def rank_program(g, core, T, topo):
             q.wait_ge(T.sem[s], v)
         if k == "send":
             o, h = OFF[a[1]], HS[a[1]]
-            g.remote_dma(ap(R("yy%d" % (a[0] + 1), o, o + h)), ap(R("xv%d" % a[0], o, o + h)),
+            g.remote_dma(ap(R("yy%d" % (a[0] + 1), o, o + h)), ap(d["rd"][0]),
                          T.sem["ya%d_%d" % d["args"]], T.sem["sent"], pid, rid, mask)
             continue
         if k == "cp":
@@ -558,11 +815,13 @@ def rank_program(g, core, T, topo):
         elif k == "act":
             ins = q.activation(*a[:3]) if a[2] == F.Copy else q.activation(*a[:3], bias=a[3], scale=a[4])
         elif k == "mm":
-            ins = q.matmul(*a)
+            for l, r, start, stop in a[1]:
+                q.matmul(a[0], ap(l), ap(r), start, stop).then_inc(T.sem["eP"], 1)
+            continue
         elif k == "iota":
             ins = q.iota(*a) if SCRATCH[d["args"][0][0]][2] == I32 else q.iota(*a, allow_small_or_imprecise_dtypes=True)
         elif k == "sel":
-            ins = q.affine_select(a[0], a[1], a[2], A.is_ge, 0.0, a[3], a[4])
+            ins = q.affine_select(a[0], a[1], a[2], a[3], a[6], a[4], a[5])
         else:
             ins = q.dma_start(*a)
         ins.then_inc(T.sem[d["sig"][0]], 16 if k == "dma" else 1)

@@ -4,13 +4,15 @@ A = AluOpType
 F = ActivationFunctionType
 NV, NL, STEPS = 4096, 224, 6
 CFG = {"HS": [64, 80, 80], "NENG": 8, "WQ": "S", "VK": "S", "UL": "S", "XV": "S", "DFS": 2, "ZB": (2, 0), "LJB": (2, 1),
-       "EQ": "E", "LAY": [(0, 1), (1, 2), (2, 5), (5, 8), (8, 11), (11, 13), (13, 16), (16, 18)], "GFILL": 1024, "WL": 40,
-       "VL": 0, "SPLIT": 2, "LATE": 64, "NR": "NNRNRN", "REP0": ["VVVVV", "GGGGG", "GGGGG"], "REP": "GGG",
-       "MODE": ["V", "V", "WS", "V", "WS", "V"],
-       "eps": 30.0, "T0": 8500.0, "T3": 2700.0, "TX": 2000.0, "SHAKES": 2200, "MOVES": 15000, "HEAT": 0.003, "SEED": 12345}
-RATES = [{"cyc": 0.83, "pe": 0.42, "lat": 150.0, "gat": 1.56, "rlat": 3000.0, "d0": 1300.0, "d1": 600.0, "bw": 400.0},
-         {"cyc": 0.86, "pe": 0.44, "lat": 160.0, "gat": 1.15, "rlat": 4500.0, "d0": 1500.0, "d1": 800.0, "bw": 280.0},
-         {"cyc": 1.2, "pe": 0.6, "lat": 120.0, "gat": 1.8, "rlat": 3500.0, "d0": 1300.0, "d1": 600.0, "bw": 400.0}]
+       "EQN": "SSVSVS", "LAY": [(0, 1), (1, 2), (2, 5), (5, 8), (8, 11), (11, 13), (13, 16), (16, 18)],
+       "FILL": [("V", 1024), ("S", 1024), ("S", 1024), ("V", 1024)], "CUT": 2048, "NN": 0, "B2G": 0, "ONE": "SGG", "WL": [0],
+       "VL": 48, "LATE": 16, "NR": "NNRNRN", "REP0": ["VVVVV", "GGGGG", "GGGGG"], "REP": "GGGGG",
+       "MODE": ["V", "V", "WWS/WWS/WSS", "V", "WWS/WWS/WSS", "V/V/VS"],
+       "eps": 30.0, "T0": 7500.0, "T3": 2500.0, "TX": 1500.0, "SHAKES": 4500, "MOVES": 25000, "HEAT": 0.005,
+       "AMP": 2500, "DEN": 600, "FLIPS": [0, 0, 1, 2], "TH": 0.006, "SEED": 23}
+RATES = [{"cyc": 0.83, "pe": 0.42, "lat": 150.0, "gat": 1.56, "rlat": 3000.0, "d0": 1300.0, "d1": 600.0, "bw": 400.0, "scale": 72e3},
+         {"cyc": 0.86, "pe": 0.44, "lat": 160.0, "gat": 1.15, "rlat": 4500.0, "d0": 1500.0, "d1": 800.0, "bw": 280.0, "scale": 79e3},
+         {"cyc": 1.2, "pe": 0.6, "lat": 120.0, "gat": 1.8, "rlat": 3500.0, "d0": 1300.0, "d1": 600.0, "bw": 400.0, "scale": 96e3}]
 HS, MODE = CFG["HS"], CFG["MODE"]
 NB = len(HS)
 OFF = [sum(HS[:b]) for b in range(NB)]
@@ -23,15 +25,15 @@ MATS = ["Zq", "Zs", "Blk", "B20", "B21", "B22", "B23", "B2v", "Teq",
 NM = len(MATS)
 XW = 20 + 8 * (NM - 2)
 NP = 16 * sum(LW)
-COLS = ["r", "a", "b", "gt", "ge", "sq", "bq", "ndg", "lt8", "bL13", "bS", "sub", "r256", "mv", "bL1", "bL2", "t0", "t1",
+COLS = ["r", "a", "b", "gt", "ge", "sq", "bq", "ndg", "lt8", "nv", "bL13", "bS", "sub", "r256", "mv", "bL1", "bL2", "t0", "t1",
         "na0", "na2", "zj", "zl", "h32", "u0", "u1", "u2", "u3", "u4", "u5"]
 BF, F16, F32, I32, U16 = "bfloat16", "float16", "float32", "int32", "uint16"
 SCRATCH = {}
-for _d, _l in ((BF, [("xw", NV), ("vm", 128), ("k2", 128), ("hb", 1),
+for _d, _l in ((BF, [("xw", NV), ("vm", 128), ("k2", 128), ("nv1", 128), ("ab", NL), ("hb", 1),
                      ("tab", 16), ("bt", 16 * (NM + 1)), ("mt", 16 * XW), ("hbm", 128), ("ni", 128),
                      ("Zq3", 144), ("Zd", 144), ("Uw", 128), ("L1eq3", 128),
                      ("rep", 4 * HM), ("ct", 128 * NB), ("cc", NL), ("l3v", 128), ("l3j", 128), ("lzj", 128),
-                     ("pp", NP), ("cr", 16 * NL), ("eq", NL), ("sg", 2 * NL), ("l1o", NL),
+                     ("pp", NP), ("cr", 20 * NL), ("eq", NL), ("sg", 2 * NL), ("l1o", NL),
                      ("nvm", 128), ("sd", NL), ("xx0", NP), ("xx1", NP), ("xx2", NP), ("xx3", NP), ("eye", 128),
                      ("yy0", NL), ("yy1", NL), ("yy2", NL), ("yy3", NL)]),
                (F32, [("col", len(COLS)), ("q16", 16), ("one", 16), ("ea", 16), ("eb", 8), ("le4", 16), ("e16", 16),
@@ -139,18 +141,21 @@ def build_ops(rate):
 
     def lin(o, i, scale, bias=0.0, eng=None):
         turn[0] += 1
-        if eng == "S" or (eng is None and turn[0] % 3 < CFG["SPLIT"]):
-            act(o, i, F.Identity, bias, scale)
-        elif bias == 0.0:
-            ts(o, i, scale, None, A.mult)
-        else:
-            ts(o, i, scale, bias, A.mult, A.add)
+        either(eng or "SSV"[turn[0] % 3], lambda: act(o, i, F.Identity, bias, scale),
+               lambda: ts(o, i, scale, None, A.mult) if bias == 0.0 else ts(o, i, scale, bias, A.mult, A.add))
 
     def copy(eng, o, i):
-        if eng == "S":
-            act(o, i, F.Copy)
-        else:
-            cp(o, i)
+        either(eng, lambda: act(o, i, F.Copy), lambda: cp(o, i))
+
+    def relu(o, i, bias=0.0):
+        either("S", lambda: act(o, i, F.Relu, bias), lambda: ts(o, i, bias, 0.0, A.add, A.max))
+
+    def either(eng, on_scalar, on_vector):
+        first, other = (on_vector, on_scalar) if eng == "S" else (on_scalar, on_vector)
+        first()
+        d = ops.pop()
+        other()
+        ops[-1]["alt"] = {z["eng"]: (z["kind"], z["args"], z["cost"]) for z in (d, ops[-1])}
 
     def mm(o, *units):
         for k, unit in enumerate(units):
@@ -169,22 +174,31 @@ def build_ops(rate):
         rows = nb / min(ncols(o) * size(o), ncols(i) * size(i))
         add(q, "dma", (o, i), [i], [o], 100, done=rate["d1"], busy=rows * 1.5 + nb / rate["bw"], sem=sem, kept=kept[0])
 
-    cut, early = NV - CFG["GFILL"], 128 - CFG["LATE"]
+    early = 128 - CFG["LATE"]
     dma("S", R("cc", 0, NL), R("c0", 0, NL))
     dma("S", R("v32", 0, 14), R("v0", 0, 14))
     if early:
         dma("Y", R("xw", 0, NV, 1, 0, early), R("x", 0, NV, 1, 0, early))
-    for c0, c1 in ((0, cut // 2), (cut // 2, cut)):
-        ms(R("win", c0, c1), 2 * HALF)
-    if cut < NV:
-        iota(R("win", cut, NV), [[0, NV - cut]], 2 * HALF, 0)
+    at = 0
+    for eng, n in CFG["FILL"]:
+        if eng == "V":
+            ms(R("win", at, at + n), 2 * HALF)
+        elif eng == "G":
+            iota(R("win", at, at + n), [[0, n]], 2 * HALF, 0)
+        else:
+            act(R("win", at, at + n), R("win", 0, n), F.Copy)
+        at += n
     iota(K("pc", 0), [[0, 1]], 0, 1)
     iota(R("q16", 0, 16), [[1, 16]], 0, 0)
     iota(R("nn", 0, 256), [[1, 256]], 0, 256)
-    for c0, c1 in ((0, cut // 2), (cut // 2, NV)):
+    for c0, c1 in ((0, CFG["CUT"]), (CFG["CUT"], NV)):
         dma("Y", R("win", c0, c1, 1, 0, 128, 4), R("adj", c0, c1, 1, 0, 32))
-    ts(R("nn", 0, 256), R("nn", 0, 256), NV - 1, None, A.bitwise_and)
-    dma("Y", R("win", 0, NV, 1, 1, 128, 16), R("nn", 0, 256))
+    if CFG["NN"]:
+        for k in range(8):
+            dma("Y", R("win", 0, NV, 1, 16 * k + 1, 16 * k + 2), R("nn", 0, 256, 1, 0, 16), "nn")
+    else:
+        ts(R("nn", 0, 256), R("nn", 0, 256), NV - 1, None, A.bitwise_and)
+        dma("Y", R("win", 0, NV, 1, 1, 128, 16), R("nn", 0, 256))
     ts(K("pc", 1), K("pc", 0), 15, None, A.bitwise_and)
     ts(K("pc", 2), K("pc", 0), 2, 3, A.logical_shift_right, A.bitwise_and)
     ts(K("pc", 3), K("pc", 0), 3, None, A.bitwise_and)
@@ -200,7 +214,7 @@ def build_ops(rate):
         iota(x, [[16, n], [-16, w]], base, 1)
         sel(x, x, [[0, n], [-16, w]], 0, 1)
         sel(x, x, [[0, n], [16, w]], 15, -1)
-        cp(R("xu", c0, c0 + n * w), x)
+        copy("V", R("xu", c0, c0 + n * w), x)
     iota(R("scn", 0, HM), [[0, HM // 16], [1, 16]], 0, 0)
     iota(R("one", 0, 16), [[0, 16]], 1, 0)
     iota(R("bt", 0, 16 * (NM + 1)), [[0, 16 * (NM + 1)]], 0, 0)
@@ -217,10 +231,16 @@ def build_ops(rate):
     ts(lt8, r, 8.0, -8192.0, A.is_lt, A.mult)
     lin(B("Zq", 12, 16), ea, low)
     lin(B("Zs", 15, 16), K("one", 0), -1.0)
-    lin(C("mv"), K("e16", 1), 1.0, K("e16", 2))
+    lin(C("nv"), K("e16", 1), -1.0)
     lin(B("Blk"), o16, 1.0)
     tt(B("Teq"), R("ea", 0, 16), R("le4", 0, 16), A.mult)
-    for m in range(4):
+    if CFG["B2G"]:
+        b2 = R("bt", B("B20")[1], B("B23")[2])
+        sel(b2, b2, [[-1, 4], [0, 4], [1, 4]], 0, 0, A.not_equal, -1.0)
+        sel(b2, b2, [[-1, 4], [1, 4], [0, 4]], 0, 0, A.is_gt)
+        sel(b2, b2, [[-1, 4], [1, 4], [0, 4]], 0, 0, A.not_equal, 1.0)
+        sel(b2, b2, [[1, 4], [0, 4], [-1, 4]], 0, 0)
+    for m in range(0 if CFG["B2G"] else 4):
         lin(B("B2%d" % m, 4 * m, 5 * m + 1), R("one", 0, m + 1), 1.0)
         if m < 3:
             lin(B("B2%d" % m, 5 * m + 4, 16, 4), R("one", 0, 3 - m), -1.0)
@@ -240,7 +260,6 @@ def build_ops(rate):
     lin(B("L1eq", 8, 12), ea, b_)
     lin(C("t0"), a1, -7.0, -4.0)
     lin(C("bL1"), a2, -35.0, C("t0"))
-    lin(C("bL13"), a2, -32.0, C("t0"))
     o2 = R("one", 0, 2)
     lin(C("na0"), a0, -8192.0)
     ts(R("tmp", 32, 40), R("qb", 0, 8), b_, C("na0"), A.is_gt, A.mult)
@@ -270,55 +289,51 @@ def build_ops(rate):
     lin(C("u4"), K("le4", 1), 2.0, -1.0)
     ts(C("u5"), a0, a1, None, A.subtract)
     lin(C("na2"), C("u4"), a3, C("u5"))
-    lin(C("sub"), r, 4096.0, -15 * 4096.0)
+    lin(C("sub"), r, 4096.0, HALF - 15 * 4096.0)
     ts(R("scn", 0, HM), R("scn", 0, HM), r, 135168.0, A.is_gt, A.mult)
     lin(R("scn", 0, HM), R("scn", 0, HM), 1.0, -131072.0)
     ts(R("tmp", 16, 32), q16, 4.0, b_, A.min, A.subtract)
     ts(R("tab", 0, 16), R("tmp", 16, 32), 0.0, a2, A.max, A.mult)
     for m0, m1 in CFG["LAY"]:
         n = xo(m1) - xo(m0) - (1 if m1 <= 2 else 0)
-        act(R("mt", 16 * xo(m0), 16 * (xo(m0) + n)), IND(R("bt", 0, 16 * (m1 + 1)), R("xu", xo(m0), xo(m0) + n)), F.Copy)
+        copy("S", R("mt", 16 * xo(m0), 16 * (xo(m0) + n)), IND(R("bt", 0, 16 * (m1 + 1)), R("xu", xo(m0), xo(m0) + n)))
     lin(R("hbm", 0, 128), M("Blk"), C("h32"))
-    for t, col in (("vm", C("mv")), ("l3v", C("na2"))):
+    for t, col in (("l3v", C("na2")), ("nv1", C("nv"))):
         lin(R(t, 0, 128), M("Blk"), col)
-    if CFG["EQ"] == "E":
-        lin(R("nvm", 0, 128), R("vm", 0, 128), -1.0)
     eye, ni, slot = R("eye", 0, 128), R("ni", 0, 128), [[-16, 8], [0, 16]]
     iota(eye, [[-1, 128]], 1, 1)
     sel(eye, eye, [[-1, 128]], 0, 1, A.is_equal)
     sel(ni, eye, [[-1, 128]], 0, 1, A.not_equal, -1.0)
     sel(R("k2", 0, 128), M("Blk"), slot, -2, 1, A.is_equal)
-    zq, z3, zd, uw, q3 = R("mt", 0, 144), R("Zq3", 0, 144), R("Zd", 0, 144), R("Uw", 0, 128), R("L1eq3", 0, 128)
+    zq, z3, zd, uw = R("mt", 0, 144), R("Zq3", 0, 144), R("Zd", 0, 144), R("Uw", 0, 128)
     sel(z3, zq, [[0, 9], [1, 16]], -15, 0, A.not_equal)
     sel(zd, z3, [[-16, 9], [256, 4], [0, 4]], -12 - 768, 1, A.not_equal, -1.0)
     sel(uw, R("k2", 0, 128), [[-16, 8], [-4, 4], [256, 4]], -768, 1, A.not_equal, 1.0)
-    iota(q3, [[-16, 8], [0, 4], [-4, 4]], -3, 1)
-    sel(q3, q3, [[-16, 8], [256, 4], [-4, 4]], -512, 1)
-    sel(q3, q3, [[16, 8], [-256, 4], [4, 4]], 512 + 3, -1)
+    sel(zd, zd, [[0, 9], [1, 16]], -15, 0, A.not_equal)
     sel(R("l3j", 0, 128), M("Blk"), slot, -8, 1, A.is_equal)
     sel(R("lzj", 0, 128), R("l3j", 0, 128), slot, -11, 1, A.not_equal, -256.0)
     cp(R("jl", 0, 14), R("j32", 0, 14))
-    act(R("l2o", 0, NL), IND(R("tab", 0, 16), R("jl", 0, 14)), F.Copy)
-    rep = R("rep", 0, 4 * HM)
-    iota(rep, [[1, HM], [0, 4]], 1, -1)
-    sel(rep, rep, [[1, HM], [0, 4]], 0, -1, A.is_equal)
+    copy("S", R("l2o", 0, NL), IND(R("tab", 0, 16), R("jl", 0, 14)))
 
     def PS(name, b, n=None):
         h, region[0] = HS[b], name
         if name == "zT":
             return top(R("ps%d" % (2 * b + 1), 384, 512), h)
-        k, c = {"WQ": (0, 0), "U": (0, 1), "DF": (0, 2), "B3": (2, 0), "L2": (0, 4), "B2": (1, 1), "D3": (1, 1), "U2": (1, 2), "L1": (1, 2),
-                "L3": (1, 0), "d": (1, 3), "c4": (1, 1), "c": (2, 1), "s": (0, 0), "r": (0, 5), "z": (1, 4), "Z": CFG["ZB"], "LJ": CFG["LJB"]}[name]
+        k, c = {"WQ": (0, 0), "U": (0, 1), "DF": (0, 2), "B3": (2, 0), "E": (2, 2), "L2": (0, 4), "B2": (1, 1), "D3": (1, 1), "U2": (1, 2), "L1": (1, 2),
+                "L3": (1, 0), "d": (1, 3), "c4": (1, 1), "c": (2, 1), "s": (0, 0), "r": (0, 5), "z": (1, 5), "Z": CFG["ZB"], "LJ": CFG["LJB"]}[name]
         return R("ps%d" % (2 * b + k if k < 2 else 6 + b % 2), c * h, c * h + (h if n is None else n))
 
     def chunks(h, n, first=0):
-        if first:
+        if first and n > 1:
             return [(0, first)] + [(first + l0, first + l1) for l0, l1 in chunks(h - first, n - 1)]
         e = [2 * ((h * k // n + 1) // 2) for k in range(n)] + [h]
         return [(e[k], e[k + 1]) for k in range(n)]
 
     def crep(b, st=1, at=0, l0=0, l1=None):
-        return R("cr", 16 * (OFF[b] + l0) + at, 16 * (OFF[b] + (HS[b] if l1 is None else l1)), st)
+        return R("cr", 20 * OFF[b] + 16 * l0 + at, 20 * OFF[b] + 16 * (HS[b] if l1 is None else l1), st)
+
+    def cone(b, l0=0):
+        return R("cr", 20 * OFF[b] + 16 * HS[b] + 4 * l0, 20 * (OFF[b] + HS[b]), 4)
 
     def move(eng, o, i):
         if eng == "G":
@@ -336,10 +351,11 @@ def build_ops(rate):
         y = R("yy%d" % (k + 1), o, o + h)
         add("N", "recv", (k, b), [], [y], 0, after=("send", k, b))
         mm(PS("d", b), [(R("ni", 0, 128), R("xx%d" % k, 16 * (LOFF[b] + h), 16 * (LOFF[b] + h) + h))], [(M("I"), y)])
-        act(R("sd", o, o + h), PS("d", b), F.Sign)
+        either("S", lambda: act(R("sd", o, o + h), PS("d", b), F.Sign),
+               lambda: ts(R("sd", o, o + h), PS("d", b), -1.0, 1.0, A.max, A.min))
 
     def vlist(b):
-        at = LOFF[b] + HS[b]
+        at = LOFF[b] + HS[b] + HS[b] // 4
         return R("lst", at, at + HS[b] // 16)
 
     for b in range(NB):
@@ -347,6 +363,7 @@ def build_ops(rate):
     for b in range(NB):
         move(CFG["REP0"][b][0], crep(b, 16), R("cc", OFF[b], OFF[b] + HS[b]))
         repeat(b, CFG["REP0"][b][1:], 16)
+        move(CFG["ONE"][b], cone(b), R("cc", OFF[b], OFF[b] + HS[b]))
     xw, win = R("xw", 0, NV), R("win", 0, NV)
     for s in range(STEPS):
         for b in range(NB):
@@ -356,9 +373,9 @@ def build_ops(rate):
             def W(buf, f=1, c0=0, st=1):
                 return R(buf, f * o + c0, f * (o + h), st)
             wat, end, mode = LW[b] - h // 4, LW[b], (MODE[s].split("/") * NB)[b]
-            vk, ul, wq = vlist(b), R("lst", lo, lo + h), R("lst", lo + wat, lo + end)
+            vk, ul, wq = vlist(b), R("lst", lo, lo + h), R("lst", lo + h, lo + h + h // 4)
             p0, fresh, keep = 16 * lo, s in (2, 4), CFG["NR"][s] == "N"
-            pv, y = R("pp", p0 + 16 * h, p0 + 17 * h), W("yy%d" % (s // 2))
+            pv, y = R("pp", p0 + 20 * h, p0 + 21 * h), W("yy%d" % (s // 2))
             sg, su = R("sg", 2 * o, 2 * o + h), R("sg", 2 * o + h, 2 * o + 2 * h)
             xx, ct = "xx%d" % (s // 2 - 1 if fresh else 3), top(R("ct", 128 * b, 128 * b + 128), h)
             ident = top(R("eye", 0, h), h)
@@ -369,38 +386,29 @@ def build_ops(rate):
             def second(name, first, st):
                 mm(PS(name, b), [(M("B2%d" % m), R("pp", first(m), first(m) + st * h, st)) for m in range(4)] + [(M("B2v"), pv)])
                 act(su, PS(name, b), F.Sign, C("bS"))
-            act(W("w1"), IND(win, vk), F.Identity, -float(HALF))
+            lin(W("w1"), IND(win, vk), 1.0, -float(HALF), "S")
             mm(PS("WQ", b, h // 4), [(M("Zq", 12 - 4 * k), W("w1", 1, k, 4)) for k in range(4)])
             lin(wq, PS("WQ", b, h // 4), 1.0, float(HALF), eng=(CFG["WQ"] * 6)[s])
-            act(W("gg", 4), IND(win, wq), F.Identity, -float(HALF))
-            if s == 0:
-                mm(PS("L3", b), [(R("vm", 0, 128), W("w1"))])
-                if set(MODE[0] + MODE[1]) & set("SW"):
-                    mm(PS("zT", b), [(R("cc", o, o + h), M("I"))])
-                    act(ct, PS("zT", b), F.Copy)
+            lin(W("gg", 4), IND(win, wq), 1.0, -float(HALF), "S")
             if not fresh:
-                weigh(h, h + h // 16, crep(b, 16))
-                weigh(wat, end, crep(b, 4))
-                second("B2", lambda m: p0 + 16 * wat + m, 4)
+                weigh(h, h + 5 * h // 16, R("cr", 20 * o, 20 * (o + h), 4))
+                second("B2", lambda m: p0 + 16 * h + m, 4)
                 mm(PS("U", b), [(M("Zq", 12 - 4 * i), W("gg", 4, i, 4)) for i in range(4)])
                 lin(ul, PS("U", b), 1.0, float(HALF), eng=(CFG["UL"] * 6)[s])
-                tt(W("eq"), PS("L3", b), ul, A.is_equal)
+            mm(PS("E", b), [(R("nv1", 0, 128), W("w1"))], [(M("Zq", 12 - 4 * i), W("gg", 4, i, 4)) for i in range(4)])
+            if (CFG["EQN"][s] * NB)[b] == "V":
+                ts(W("eq"), PS("E", b), 0.0, None, A.is_equal)
             else:
-                three = [(M("Zq3", 12 - 4 * i), W("gg", 4, i, 4)) for i in range(4)]
-                un = "U" if CFG["EQ"] != "E" else "U2"
-                if CFG["EQ"] == "E":
-                    mm(PS("U", b), [(M("Uw"), W("w1")), (R("nvm", 0, 128), W("w1"))], three)
-                    ts(W("eq"), PS("U", b), 0.0, None, A.is_equal)
-                    mm(PS("D3", b), [(M("Zd", 12 - 4 * i), W("gg", 4, i, 4)) for i in range(4)])
-                    mm(PS("U2", b), [(M("Uw"), W("w1"))] + three)
-                else:
-                    mm(PS("U", b), [(M("Uw"), W("w1"))], three)
-                    mm(PS("D3", b), [(M("Zd", 12 - 4 * i), W("gg", 4, i, 4)) for i in range(4)])
-                    tt(W("eq"), PS("U", b), W("vsb"), A.is_equal)
+                act(W("ab"), PS("E", b), F.Abs)
+                either("S", lambda: act(W("eq"), W("ab"), F.Relu, 1.0, -1.0),
+                       lambda: ts(W("eq"), W("ab"), 0.0, None, A.is_equal))
+            if fresh:
+                mm(PS("D3", b), [(M("Zd", 12 - 4 * i), W("gg", 4, i, 4)) for i in range(4)])
+                mm(PS("U", b), [(M("Uw"), W("w1"))], [(M("Zq3", 12 - 4 * i), W("gg", 4, i, 4)) for i in range(4)])
                 tt(W("t32"), PS("D3", b), W("eq"), A.mult)
-                tt(ul, PS(un, b), W("t32"), A.subtract)
+                tt(ul, PS("U", b), W("t32"), A.subtract)
             late = h
-            for (l0, l1), m in zip(chunks(h, len(mode), CFG["WL" if fresh else "VL"]), mode):
+            for (l0, l1), m in zip(chunks(h, len(mode), (CFG["WL"] * NB)[b] if fresh else CFG["VL"]), mode):
                 if m == "V":
                     weigh(l0, l1, crep(b, 1, 0, l0, l1))
                 else:
@@ -408,16 +416,15 @@ def build_ops(rate):
                     copy("S" if m == "S" else "V", R(xx, p0 + 16 * l0, p0 + 16 * l1), IND(xw, R("lst", lo + l0, lo + l1)))
             if fresh:
                 sign_of_change(b, s // 2 - 1)
-                mm(PS("zT", b), [(W("cc"), M("I")) if s == 2 else (ident, ct)], [(W("sd"), M("I"))])
-                ts(ct, PS("zT", b), -15.0, 15.0, A.max, A.min)
+                mm(PS("z", b), [(M("I"), cone(b))], [(M("I"), W("sd"))])
+                ts(cone(b), PS("z", b), -15.0, 15.0, A.max, A.min)
             if late < h:
                 c4 = PS("c4", b, 4 * (h - late))
-                mm(c4, [(ct, top(R("rep", 4 * late, 4 * h), h))])
+                add("P", "mm", (c4, [(M("I"), cone(b, late), True, True, R(c4[0], c4[1] + k, c4[2], 4)) for k in range(4)]),
+                    [M("I"), cone(b, late)], [c4], 4 * (10 + max(64, h - late) * pe))
             if fresh:
-                st = 2 ** len(CFG["REP"])
-                mm(PS("c", b, 16 * h // st), [(ct, top(R("rep", 0, 4 * h, st // 4), h))])
-                act(crep(b, st), PS("c", b, 16 * h // st), F.Copy)
-                repeat(b, CFG["REP"], st)
+                move(CFG["REP"][0], crep(b, 16), cone(b))
+                repeat(b, CFG["REP"][1:], 16)
                 tt(pv, c4[:3] + (4,) + c4[4:], R(xx, p0 + 16 * h, p0 + 17 * h), A.mult)
             if late < h:
                 for k in (3, 0, 1, 2):
@@ -426,33 +433,31 @@ def build_ops(rate):
                         second("B3", lambda m: p0 + 4 * m + 3, 16)
             if s % 2 == 0:
                 mm(PS("s", b), [(R("hbm", 0, 128), y)])
-                act(W("qq"), PS("s", b), F.Identity, C("bq"), C("sq"))
+                lin(W("qq"), PS("s", b), C("sq"), C("bq"), "S")
             sums = [(M("Zs", 15 - m), R("pp", p0 + m, p0 + 16 * h, 16)) for m in range(16)]
             units = [sums[k::4] for k in (3, 0, 1, 2)] if late < h else [sums[k::CFG["DFS"]] for k in range(CFG["DFS"])]
             mm(PS("DF", b), [(M("Teq"), W("eq")), (M("Blk"), pv)], *units)
             act(sg, PS("DF", b), F.Sign, -0.5)
-            mm(PS("L1", b), [(M("L1J"), W("l2o")), (M("L1eq3" if fresh else "L1eq"), W("eq")), (M("L1su"), su)],
+            mm(PS("L1", b), [(M("L1J"), W("l2o")), (M("L1eq"), W("eq")), (M("L1su"), su)],
                [(M("L1sg"), sg)])
-            act(W("l1o"), PS("L1", b), F.Relu, C("bL1" if keep else "bL13"))
+            relu(W("l1o"), PS("L1", b), C("bL1"))
             mm(PS("L2", b), [(M("L2w"), W("w1")), (M("L2J"), W("l2o")), (M("L2y"), y), (M("L2r"), W("qq"))],
                [(M("L2l"), W("l1o"))])
             if s == STEPS - 1:
                 mm(PS("Z", b), [(R("lzj", 0, 128), W("l2o"))], [(M("L2l"), W("l1o"))])
-                act(W("zo"), PS("Z", b), F.Relu)
-            act(W("l2o"), PS("L2", b), F.Relu, C("bL2"))
-            mm(PS("L3", b), [(R("k2", 0, 128), W("w1"))], [(R("l3v", 0, 128), W("l2o"))])
+                relu(W("zo"), PS("Z", b))
+            relu(W("l2o"), PS("L2", b), C("bL2"))
+            mm(PS("L3", b), [(R("l3v", 0, 128), W("l2o"))])
             add("V", "scan", (W("sc"), R("scn", 0, h), PS("L3", b)), [R("scn", 0, h), PS("L3", b)], [W("sc")],
                 fix + max(64, h) * cyc)
-            lin(vk, W("sc", 1, 15, 16), 1.0, C("sub"), eng=(CFG["VK"] * 6)[s])
+            lin(vk, W("sc", 1, 15, 16), 1.0, C("sub"), eng="V" if (s, b) == (STEPS - 1, NB - 1) else (CFG["VK"] * 6)[s])
             if s % 2 == 1:
                 k = s // 2
                 xv = R("xx%d" % k, p0 + 16 * h, p0 + 17 * h)
-                copy(CFG["XV"], xv, IND(xw, vk))
+                copy("V" if (s, b) == (STEPS - 1, NB - 1) else (CFG["XV"] * 3)[k], xv, IND(xw, vk))
                 add("G", "send", (k, b), [xv], [], 300, done=rate["rlat"], key=("send", k, b))
-            if s < STEPS - 1 and CFG["NR"][s + 1] == "R" and CFG["EQ"] != "E":
-                act(W("vsb"), PS("L3", b), F.Copy)
             if s == STEPS - 1:
-                act(W("vsb"), PS("L3", b), F.Copy)
+                lin(W("vsb"), PS("L3", b), 1.0, float(HALF), "S")
                 mm(PS("LJ", b), [(R("l3j", 0, 128), W("l2o"))])
                 tt(W("jo32"), PS("LJ", b), W("zo"), A.add)
     dma("Y", R("vo", 0, NL, 1, 0, 8), R("vsb", 0, NL, 1, 0, 128, 16), "out")
@@ -460,9 +465,19 @@ def build_ops(rate):
     for b in range(NB):
         h, o = HS[b], OFF[b]
         age[0] = (STEPS, b)
-        sign_of_change(b, 2)
-        mm(PS("z", b), [(M("I"), crep(b, 16))], [(M("I"), R("sd", o, o + h))])
-        ts(R("co32", o, o + h), PS("z", b), -15.0, 15.0, A.max, A.min)
+        if b < NB - 1:
+            sign_of_change(b, 2)
+            mm(PS("z", b), [(M("I"), cone(b))], [(M("I"), R("sd", o, o + h))])
+            ts(R("co32", o, o + h), PS("z", b), -15.0, 15.0, A.max, A.min)
+        else:
+            y, hi = R("yy3", o, o + h), R("ps7", 256, 256 + h)
+            add("N", "recv", (2, b), [], [y], 0, after=("send", 2, b))
+            ts(R("eq", o, o + h), cone(b), -1.0, -15.0, A.add, A.max)
+            ts(hi, cone(b), 1.0, 15.0, A.add, A.min)
+            mm(PS("d", b), [(M("I"), cone(b)), (R("ni", 0, 128), R("xx2", 16 * (LOFF[b] + h), 16 * (LOFF[b] + h) + h))],
+               [(M("I"), y)])
+            tt(R("sd", o, o + h), PS("d", b), R("eq", o, o + h), A.max)
+            tt(R("co32", o, o + h), hi, R("sd", o, o + h), A.min)
         dma("Y", R("co", o, o + h), R("co32", o, o + h), "out")
     return ops
 
@@ -486,14 +501,14 @@ def link(ops):
                     (order if e["eng"] == d["eng"] == "P" else deps).add(e["id"])
             if reg[0].startswith("ps"):
                 for en, e in bank.setdefault(reg[0], {}).items():
-                    (order if en == d["eng"] else deps).add(e["id"])
+                    (order if en == d["eng"] and "alt" not in d else deps).add(e["id"])
         for reg, w in use:
             hl = hist.setdefault(reg[0], [])
             if w and reg[3:] == (1, 0, 128, 1):
                 hl[:] = [z for z in hl if not (z[1][1] >= reg[1] and z[1][2] <= reg[2])]
             hl.append((d, reg, w))
             if reg[0].startswith("ps"):
-                bank[reg[0]][d["eng"]] = d
+                bank[reg[0]]["either" if "alt" in d else d["eng"]] = d
         if d.get("kept"):
             order |= {keys[d["eng"]]} if d["eng"] in keys else set()
             keys[d["eng"]] = d["id"]
@@ -565,6 +580,10 @@ def stagger(ops, rate):
     return [ops[i] for i in sorted(range(len(ops)), key=lambda i: at[i])]
 
 
+def worth(ends):
+    return 3 * (sum((t / z["scale"]) ** 8 for t, z in zip(ends, RATES)) / len(RATES)) ** 0.125
+
+
 def draws(seed):
     z = [seed]
 
@@ -575,7 +594,9 @@ def draws(seed):
 
 
 def justify(ops, seq, rate):
-    n, span, rnd = len(ops), timer(ops)[0], draws(CFG["SEED"])
+    n, rnd = len(ops), draws(CFG["SEED"])
+    span, held, put = timer(ops)
+
     cost, eng = [d["cost"] for d in ops], ["VSPGYN".index(d["eng"]) for d in ops]
     lag = [d["done"] + rate["lat"] + (d["busy"] + rate["d0"] if d["busy"] else 0) for d in ops]
     order = [d["id"] for d in seq]
@@ -630,27 +651,51 @@ def justify(ops, seq, rate):
                 return best
             best = (whole, [e - c for e, c in zip(end, cost)])
             end = pack([-e for e in pack([-e for e in end], suc, lag)], pre, zero)
+
+    def swap(calls):
+        for i in calls:
+            eng[i] = 1 - eng[i]
+            put(i, "VS"[eng[i]])
+            cost[i] = ops[i]["cost"]
     whole, st = both(key)
-    keep = rank(st, pre)
-    base = span(keep)[0]
-    now = best = len(base)
+    keep, where, free_to_move, late = rank(st, pre), list(eng), [d["id"] for d in ops if "alt" in d], []
+    now = best = worth(span(keep)[0])
     for it in range(CFG["SHAKES"]):
         c, w = rnd() * whole, (3000.0, 8000.0, 20000.0)[it % 3]
-        whole, new = both([x + ((rnd() + rnd() - 1) * 1200 if abs(x - c) < w and rnd() < 1000 / w else 0) for x in st])
+        pool = free_to_move if it % 3 == 0 else (late or free_to_move)
+        moved = {pool[int(rnd() * len(pool))] for _ in range(CFG["FLIPS"][it % len(CFG["FLIPS"])])}
+        swap(moved)
+        shake = CFG["DEN"] / w if not moved or it % 2 else 0.0
+        whole, new = both([x + ((rnd() + rnd() - 1) * CFG["AMP"] if abs(x - c) < w and rnd() < shake else 0) for x in st])
         order = rank(new, pre)
-        s = sum(t / t0 for t, t0 in zip(span(order)[0], base))
-        if s <= now + 0.004 * rnd():
-            now, st = s, new
+        ends, t1 = span(order)
+        s = worth(ends)
+        if s <= now + CFG["TH"] * (1 - it / CFG["SHAKES"]) * rnd():
+            now, st, late = s, new, [i for i in held(order, t1, True) if "alt" in ops[i]]
             if s < best:
-                best, keep = s, order
+                best, keep, where = s, order, list(eng)
+        else:
+            swap(moved)
+    swap([i for i in free_to_move if eng[i] != where[i]])
     return [ops[i] for i in keep]
 
 
 def timer(ops):
+    built = [build_ops(z) for z in RATES]
     sets = [([d["cost"] for d in o], [d["done"] + z["lat"] for d in o], [d["busy"] for d in o], z["d0"])
-            for o, z in [(build_ops(z), z) for z in RATES]]
+            for o, z in zip(built, RATES)]
     hard = [d["deps"] + d["soft"] for d in ops]
     eng, n = ["VSPGYN".index(d["eng"]) for d in ops], len(ops)
+
+    def put(i, e):
+        d = ops[i]
+        eng[i], d["eng"] = "VS".index(e), e
+        d["kind"], d["args"], d["cost"] = d["alt"][e]
+        for o, z in zip(built, sets):
+            z[0][i] = o[i]["alt"][e][2]
+    for d in ops:
+        if "alt" in d:
+            put(d["id"], d["eng"])
 
     def span(order, at=0, old=None):
         ends, all_t1 = [], []
@@ -680,7 +725,7 @@ def timer(ops):
             all_t1.append(t1)
         return ends, all_t1
 
-    def held(order, all_t1):
+    def held(order, all_t1, both=False):
         before, last, out = {}, {}, []
         for i in order:
             before[i] = last.get(eng[i])
@@ -691,27 +736,38 @@ def timer(ops):
                 e = max(hard[i], key=lambda j: t1[j]) if hard[i] else None
                 p = before[i]
                 if p is not None and (e is None or t1[n + p] >= t1[e]):
-                    out.append(i)
+                    out += [i, p] if both else [i]
                     e = p
                 i = e
         return out
-    return span, held
+    return span, held, put
 
 
 def polish(ops, seq):
-    span, held = timer(ops)
+    span, held, put = timer(ops)
     pre = [set(d["deps"] + d["soft"] + d["order"]) for d in ops]
     eng = [d["eng"] for d in ops]
     order = [d["id"] for d in seq]
-    base, t1 = span(order)
-    now = best = len(base)
-    keep, rnd, moves = order, draws(CFG["SEED"]), CFG["MOVES"]
+    ends, t1 = span(order)
+    now = best = worth(ends)
+    keep, where, rnd, moves = order, list(eng), draws(CFG["SEED"]), CFG["MOVES"]
     pick = held(order, t1)
     for it in range(moves):
         d = pick[int(rnd() * len(pick))] if it % 5 else order[int(rnd() * len(order))]
         k = (1, 1, 1, 2, 2, 3)[int(rnd() * 6)]
         i = j = order.index(d)
         if eng[d] == "N" or ops[d].get("kept"):
+            continue
+        if "alt" in ops[d] and it % 4 == 0:
+            put(d, "VS"[eng[d] == "V"])
+            ends, new = span(order, i, t1)
+            s = worth(ends)
+            if s <= now + CFG["HEAT"] * (1 - it / moves) * rnd() ** 2:
+                now, t1, pick, eng[d] = s, new, held(order, new), ops[d]["eng"]
+                if s < best:
+                    best, keep, where = s, order, list(eng)
+            else:
+                put(d, eng[d])
             continue
         while k and j > 0:
             j -= 1
@@ -725,11 +781,14 @@ def polish(ops, seq):
             continue
         c = order[:j] + [e for e in order[j:i] if e in mv] + [d] + [e for e in order[j:i] if e not in mv] + order[i + 1:]
         ends, new = span(c, j, t1)
-        s = sum(t / t0 for t, t0 in zip(ends, base))
+        s = worth(ends)
         if s <= now + CFG["HEAT"] * (1 - it / moves) * rnd() ** 2:
             order, now, t1, pick = c, s, new, held(c, new)
             if s < best:
-                best, keep = s, c
+                best, keep, where = s, c, list(eng)
+    for d in ops:
+        if "alt" in d:
+            put(d["id"], where[d["id"]])
     return [ops[i] for i in keep]
 
 
@@ -815,8 +874,8 @@ def rank_program(g, core, T, topo):
         elif k == "act":
             ins = q.activation(*a[:3]) if a[2] == F.Copy else q.activation(*a[:3], bias=a[3], scale=a[4])
         elif k == "mm":
-            for l, r, start, stop in a[1]:
-                q.matmul(a[0], ap(l), ap(r), start, stop).then_inc(T.sem["eP"], 1)
+            for z in a[1]:
+                q.matmul(ap(z[4]) if len(z) > 4 else a[0], ap(z[0]), ap(z[1]), z[2], z[3]).then_inc(T.sem["eP"], 1)
             continue
         elif k == "iota":
             ins = q.iota(*a) if SCRATCH[d["args"][0][0]][2] == I32 else q.iota(*a, allow_small_or_imprecise_dtypes=True)

from concourse.mybir import AluOpType, ActivationFunctionType

A = AluOpType
F = ActivationFunctionType
NV, NL, STEPS = 4096, 224, 6
CFG = {"HS": [64, 80, 80], "NENG": 8, "WQ": "S", "VK": "S", "UL": "S", "XV": "S", "DFS": 2, "ZB": (2, 0), "LJB": (2, 1),
       "EQN": "SSVSVS", "LAY": [(0, 1), (1, 2), (2, 5), (5, 8), (8, 11), (11, 13), (13, 16), (16, 18)],
       "FILL": [("V", 1024), ("S", 1024), ("S", 1024), ("V", 1024)], "CUT": 2048, "NN": 0, "B2G": 0, "ONE": "SGG", "WL": [0],
       "VL": 48, "LATE": 16, "NR": "NNRNRN", "REP0": ["VVVVV", "GGGGG", "GGGGG"], "REP": "GGGGG",
       "MODE": ["V", "V", "WWS/WWS/WSS", "V", "WWS/WWS/WSS", "V/V/VS"],
       "eps": 30.0, "T0": 7500.0, "T3": 2500.0, "TX": 1500.0, "SHAKES": 4500, "MOVES": 25000, "HEAT": 0.005,
       "AMP": 2500, "DEN": 600, "FLIPS": [0, 0, 1, 2], "TH": 0.006, "SEED": 23}
RATES = [{"cyc": 0.83, "pe": 0.42, "lat": 150.0, "gat": 1.56, "rlat": 3000.0, "d0": 1300.0, "d1": 600.0, "bw": 400.0, "scale": 72e3},
         {"cyc": 0.86, "pe": 0.44, "lat": 160.0, "gat": 1.15, "rlat": 4500.0, "d0": 1500.0, "d1": 800.0, "bw": 280.0, "scale": 79e3},
         {"cyc": 1.2, "pe": 0.6, "lat": 120.0, "gat": 1.8, "rlat": 3500.0, "d0": 1300.0, "d1": 600.0, "bw": 400.0, "scale": 96e3}]
HS, MODE = CFG["HS"], CFG["MODE"]
NB = len(HS)
OFF = [sum(HS[:b]) for b in range(NB)]
HM = max(HS)
LW = [h + h // 4 + 2 * ((h // 16 + 1) // 2) for h in HS]
LOFF = [sum(LW[:b]) for b in range(NB)]
HALF = NV // 2
MATS = ["Zq", "Zs", "Blk", "B20", "B21", "B22", "B23", "B2v", "Teq",
        "L1sg", "L1su", "L1eq", "L1J", "L2l", "L2w", "L2J", "L2y", "L2r"]
NM = len(MATS)
XW = 20 + 8 * (NM - 2)
NP = 16 * sum(LW)
COLS = ["r", "a", "b", "gt", "ge", "sq", "bq", "ndg", "lt8", "nv", "bL13", "bS", "sub", "r256", "mv", "bL1", "bL2", "t0", "t1",
        "na0", "na2", "zj", "zl", "h32", "u0", "u1", "u2", "u3", "u4", "u5"]
BF, F16, F32, I32, U16 = "bfloat16", "float16", "float32", "int32", "uint16"
SCRATCH = {}
for _d, _l in ((BF, [("xw", NV), ("vm", 128), ("k2", 128), ("nv1", 128), ("ab", NL), ("hb", 1),
                     ("tab", 16), ("bt", 16 * (NM + 1)), ("mt", 16 * XW), ("hbm", 128), ("ni", 128),
                     ("Zq3", 144), ("Zd", 144), ("Uw", 128), ("L1eq3", 128),
                     ("rep", 4 * HM), ("ct", 128 * NB), ("cc", NL), ("l3v", 128), ("l3j", 128), ("lzj", 128),
                     ("pp", NP), ("cr", 20 * NL), ("eq", NL), ("sg", 2 * NL), ("l1o", NL),
                     ("nvm", 128), ("sd", NL), ("xx0", NP), ("xx1", NP), ("xx2", NP), ("xx3", NP), ("eye", 128),
                     ("yy0", NL), ("yy1", NL), ("yy2", NL), ("yy3", NL)]),
               (F32, [("col", len(COLS)), ("q16", 16), ("one", 16), ("ea", 16), ("eb", 8), ("le4", 16), ("e16", 16),
                      ("qa", 16), ("qb", 16), ("tmp", 40), ("xl", XW), ("scn", HM), ("t32", NL),
                      ("vsb", NL), ("zo", NL), ("sc", NL), ("co32", NL), ("jo32", NL)]),
               (F16, [("qq", NL), ("w1", NL), ("gg", 4 * NL), ("l2o", NL)]),
               (I32, [("win", NV), ("nn", 256), ("v32", 14), ("j32", 14), ("pc", 4)]),
               (U16, [("jl", 14), ("xu", XW), ("lst", sum(LW))])):
    for _n, _w in _l:
        SCRATCH[_n] = ("sbuf", [128, _w], _d)
for _k in range(8):
    SCRATCH["ps%d" % _k] = ("psum", [128, 512], F32)
DRAM = {"adj": 4, "x": 2, "c0": 2, "y0": 2, "h": 2, "v0": 4, "j0": 4, "vo": 4, "jo": 4, "co": 4}


def R(buf, c0, c1, st=1, p0=0, p1=128, ps=1):
    return (buf, c0, c1, st, p0, p1, ps)


def K(buf, i):
    return R(buf, i, i + 1)


def IND(win, off):
    return ("ind", win, off)


def C(name):
    return K("col", COLS.index(name))


def xo(m):
    return 10 * m if m < 2 else 20 + 8 * (m - 2)


def M(name, shift=0):
    if name not in MATS:
        return R("eye" if name == "I" else name, shift, shift + 128)
    m = MATS.index(name)
    return R("mt", 16 * xo(m) + shift, 16 * xo(m) + shift + 128)


def B(name, c0=0, c1=16, st=1):
    i = 16 * (MATS.index(name) + 1)
    return R("bt", i + c0, i + c1, st)


def top(r, n):
    return r[:5] + (n,) + r[6:]


def ncols(r):
    return 16 * ncols(r[2]) if r[0] == "ind" else len(range(r[1], r[2], r[3]))


def size(r):
    return DRAM[r[0]] if r[0] in DRAM else {BF: 2, F16: 2, U16: 2, F32: 4, I32: 4}[SCRATCH[r[0]][2]]


def two(r):
    return r[0] != "ind" and size(r) == 2


def isreg(a):
    return isinstance(a, tuple)


def build_ops(rate):
    ops = []
    cyc, gat, pe, fix = rate["cyc"], rate["gat"], rate["pe"], 50.0
    turn, kept, age, region, seen = [0], [True], [None], [""], {}

    def add(eng, kind, args, rd, wr, cost, **kw):
        rr = []
        for a in rd:
            if isreg(a):
                rr += [a[1], a[2]] if a[0] == "ind" else [a]
        d = {"eng": eng, "kind": kind, "args": args, "rd": rr, "wr": wr, "cost": cost, "id": len(ops), "done": 0.0, "busy": 0.0,
             "turn": age[0]}
        name = eng + (region[0] if eng == "P" else wr[0][0].rstrip("0123") if wr else kind)
        seen[age[0], name] = seen.get((age[0], name), 0) + 1
        d["tag"] = name + str(seen[age[0], name])
        d.update(kw)
        ops.append(d)

    def vcost(src, n, f):
        return 62 + gat * n * cyc if src[0] == "ind" else fix + max(64, n * f) * cyc

    def cp(o, i):
        add("V", "cp", (o, i), [i], [o], vcost(i, ncols(o), 0.5 if two(o) and two(i) else 1))

    def ts(o, i, s1, s2, op0, op1=None):
        add("V", "ts", (o, i, s1, s2, op0, op1), [i, s1, s2], [o], vcost(i, ncols(o), 0.5 if two(o) and two(i) else 1))

    def tt(o, i0, i1, op):
        f = 1 if i0[0].startswith("ps") or i1[0].startswith("ps") else 2
        add("V", "tt", (o, i0, i1, op), [i0, i1], [o], vcost(i0, ncols(o), f))

    def ms(o, v):
        add("V", "ms", (o, v), [], [o], vcost(o, ncols(o), 0.5 if two(o) else 1))

    def act(o, i, fn, bias=0.0, scale=1.0):
        c = 80 + gat * ncols(o) * cyc if i[0] == "ind" else fix + 30 + max(64, ncols(o)) * cyc
        add("S", "act", (o, i, fn, bias, scale), [i, bias, scale], [o], c)

    def lin(o, i, scale, bias=0.0, eng=None):
        turn[0] += 1
        either(eng or "SSV"[turn[0] % 3], lambda: act(o, i, F.Identity, bias, scale),
               lambda: ts(o, i, scale, None, A.mult) if bias == 0.0 else ts(o, i, scale, bias, A.mult, A.add))

    def copy(eng, o, i):
        either(eng, lambda: act(o, i, F.Copy), lambda: cp(o, i))

    def relu(o, i, bias=0.0):
        either("S", lambda: act(o, i, F.Relu, bias), lambda: ts(o, i, bias, 0.0, A.add, A.max))

    def either(eng, on_scalar, on_vector):
        first, other = (on_vector, on_scalar) if eng == "S" else (on_scalar, on_vector)
        first()
        d = ops.pop()
        other()
        ops[-1]["alt"] = {z["eng"]: (z["kind"], z["args"], z["cost"]) for z in (d, ops[-1])}

    def mm(o, *units):
        for k, unit in enumerate(units):
            calls = [(l, r, k == 0 and j == 0, k == len(units) - 1 and j == len(unit) - 1) for j, (l, r) in enumerate(unit)]
            cost = sum(10 + (size(l) // 2) ** 2 * max(min(64, ncols(l)), ncols(r)) * pe for l, r in unit)
            add("P", "mm", (o, calls), [z for lr in unit for z in lr], [o], cost)

    def iota(o, pat, base, cm):
        add("G", "iota", (o, pat, base, cm), [], [o], 160 + 2 * ncols(o) * cyc)

    def sel(o, i, pat, base, cm, op=A.is_ge, fill=0.0):
        add("G", "sel", (o, i, pat, op, base, cm, fill), [i], [o], 210 + 2 * ncols(o) * cyc)

    def dma(q, o, i, sem=None):
        nb = len(range(o[4], o[5], o[6])) * ncols(o) * size(o)
        rows = nb / min(ncols(o) * size(o), ncols(i) * size(i))
        add(q, "dma", (o, i), [i], [o], 100, done=rate["d1"], busy=rows * 1.5 + nb / rate["bw"], sem=sem, kept=kept[0])

    early = 128 - CFG["LATE"]
    dma("S", R("cc", 0, NL), R("c0", 0, NL))
    dma("S", R("v32", 0, 14), R("v0", 0, 14))
    if early:
        dma("Y", R("xw", 0, NV, 1, 0, early), R("x", 0, NV, 1, 0, early))
    at = 0
    for eng, n in CFG["FILL"]:
        if eng == "V":
            ms(R("win", at, at + n), 2 * HALF)
        elif eng == "G":
            iota(R("win", at, at + n), [[0, n]], 2 * HALF, 0)
        else:
            act(R("win", at, at + n), R("win", 0, n), F.Copy)
        at += n
    iota(K("pc", 0), [[0, 1]], 0, 1)
    iota(R("q16", 0, 16), [[1, 16]], 0, 0)
    iota(R("nn", 0, 256), [[1, 256]], 0, 256)
    for c0, c1 in ((0, CFG["CUT"]), (CFG["CUT"], NV)):
        dma("Y", R("win", c0, c1, 1, 0, 128, 4), R("adj", c0, c1, 1, 0, 32))
    if CFG["NN"]:
        for k in range(8):
            dma("Y", R("win", 0, NV, 1, 16 * k + 1, 16 * k + 2), R("nn", 0, 256, 1, 0, 16), "nn")
    else:
        ts(R("nn", 0, 256), R("nn", 0, 256), NV - 1, None, A.bitwise_and)
        dma("Y", R("win", 0, NV, 1, 1, 128, 16), R("nn", 0, 256))
    ts(K("pc", 1), K("pc", 0), 15, None, A.bitwise_and)
    ts(K("pc", 2), K("pc", 0), 2, 3, A.logical_shift_right, A.bitwise_and)
    ts(K("pc", 3), K("pc", 0), 3, None, A.bitwise_and)
    cp(R("col", 0, 3), R("pc", 1, 4))
    r, a, b_ = C("r"), C("a"), C("b")
    if early < 128:
        dma("Y", R("xw", 0, NV, 1, early, 128), R("x", 0, NV, 1, early, 128))
    for o, i in ((R("hb", 0, 1), R("h", 0, 1)), (R("j32", 0, 14), R("j0", 0, 14)), (R("yy0", 0, NL), R("y0", 0, NL))):
        dma("Y", o, i)
    kept[0] = False
    for c0, n, w, base in ((0, 2, 10, 16), (20, NM - 2, 8, 48)):
        x = R("xl", c0, c0 + n * w)
        iota(x, [[16, n], [-16, w]], base, 1)
        sel(x, x, [[0, n], [-16, w]], 0, 1)
        sel(x, x, [[0, n], [16, w]], 15, -1)
        copy("V", R("xu", c0, c0 + n * w), x)
    iota(R("scn", 0, HM), [[0, HM // 16], [1, 16]], 0, 0)
    iota(R("one", 0, 16), [[0, 16]], 1, 0)
    iota(R("bt", 0, 16 * (NM + 1)), [[0, 16 * (NM + 1)]], 0, 0)
    q4, q16, o4, o8, o16 = R("q16", 0, 4), R("q16", 0, 16), R("one", 0, 4), R("one", 0, 8), R("one", 0, 16)
    iota(R("qa", 0, 16), [[1, 4], [0, 4]], 0, 0)
    iota(R("qb", 0, 16), [[0, 4], [1, 4]], 0, 0)
    ea, eb, e16 = R("ea", 0, 16, 4), R("eb", 0, 4), R("e16", 0, 16)
    ts(R("ea", 0, 16), R("qa", 0, 16), a, None, A.is_equal)
    ts(R("eb", 0, 8), R("qb", 0, 8), b_, None, A.is_equal)
    ts(e16, q16, r, None, A.is_equal)
    ts(R("le4", 0, 16), R("qb", 0, 16), b_, None, A.is_ge)
    low, lt8 = K("eb", 0), C("lt8")
    a0, a1, a2, a3, e11 = K("ea", 0), K("ea", 4), K("ea", 8), K("ea", 12), K("e16", 11)
    ts(lt8, r, 8.0, -8192.0, A.is_lt, A.mult)
    lin(B("Zq", 12, 16), ea, low)
    lin(B("Zs", 15, 16), K("one", 0), -1.0)
    lin(C("nv"), K("e16", 1), -1.0)
    lin(B("Blk"), o16, 1.0)
    tt(B("Teq"), R("ea", 0, 16), R("le4", 0, 16), A.mult)
    if CFG["B2G"]:
        b2 = R("bt", B("B20")[1], B("B23")[2])
        sel(b2, b2, [[-1, 4], [0, 4], [1, 4]], 0, 0, A.not_equal, -1.0)
        sel(b2, b2, [[-1, 4], [1, 4], [0, 4]], 0, 0, A.is_gt)
        sel(b2, b2, [[-1, 4], [1, 4], [0, 4]], 0, 0, A.not_equal, 1.0)
        sel(b2, b2, [[1, 4], [0, 4], [-1, 4]], 0, 0)
    for m in range(0 if CFG["B2G"] else 4):
        lin(B("B2%d" % m, 4 * m, 5 * m + 1), R("one", 0, m + 1), 1.0)
        if m < 3:
            lin(B("B2%d" % m, 5 * m + 4, 16, 4), R("one", 0, 3 - m), -1.0)
    lin(B("B2v", 0, 16, 5), o4, -1.0)
    ts(C("gt"), a, b_, None, A.is_gt)
    ts(C("ge"), a, b_, None, A.is_ge)
    ts(C("ndg"), a, b_, -1.0, A.is_equal, A.mult)
    lin(C("bS"), C("gt"), -0.5)
    lin(B("L1sg", 0, 4), ea, 1.0)
    lin(B("L1su", 0, 4), ea, C("ndg"))
    lin(R("tmp", 0, 4), ea, C("ge"))
    lin(R("tmp", 12, 16), eb, C("gt"))
    tt(B("L1su", 4, 8), R("tmp", 0, 4), R("tmp", 12, 16), A.subtract)
    lin(B("L1su", 8, 12), B("L1su", 4, 8), 8.0)
    ts(B("L1J", 0, 4), eb, a2, -8.0, A.mult, A.mult)
    ts(B("L1J", 4, 12), o8, e11, 8.0, A.mult, A.mult)
    lin(B("L1eq", 8, 12), ea, b_)
    lin(C("t0"), a1, -7.0, -4.0)
    lin(C("bL1"), a2, -35.0, C("t0"))
    o2 = R("one", 0, 2)
    lin(C("na0"), a0, -8192.0)
    ts(R("tmp", 32, 40), R("qb", 0, 8), b_, C("na0"), A.is_gt, A.mult)
    lin(R("tmp", 4, 12), R("eb", 0, 8), lt8)
    tt(B("L2l", 0, 8), R("tmp", 32, 40), R("tmp", 4, 12), A.subtract)
    lin(C("t1"), a0, -4.0, a2)
    lin(B("L2l", 8, 12), o4, C("t1"))
    lin(B("L2l", 12, 16, 2), o2, C("na0"))
    ts(B("L2l", 13, 16, 2), o2, a1, -8192.0, A.mult, A.mult)
    lin(B("L2w", 0, 4), ea, low)
    lin(B("L2w", 4, 8), B("L2w", 0, 4), -1.0)
    lin(B("L2w", 12, 13), K("e16", 1), 1.0)
    lin(B("L2w", 14, 15), K("e16", 1), -1.0)
    ts(B("L2J", 8, 12), o4, e11, -4.0, A.mult, A.mult)
    ts(B("L2J", 12, 16, 2), o2, e11, -8192.0, A.mult, A.mult)
    ts(B("L2J", 13, 16, 2), o2, e11, 8192.0, A.mult, A.mult)
    lin(B("L2r", 15, 16), K("e16", 1), 128.0)
    lin(B("L2r", 13, 14), K("e16", 0), -4096.0, B("L2r", 15, 16))
    lin(C("sq"), K("e16", 0), 1.0 / 4096 - 1.0 / 128, 1.0 / 128)
    lin(C("bq"), K("e16", 0), 1.0 / 8192 - 1.0 / 256, 1535.5 + 1.0 / 256)
    cp(C("h32"), R("hb", 0, 1))
    lin(B("L2y", 15, 16), C("h32"), -1.0)
    lin(C("u0"), b_, -1.0, 4.0)
    lin(C("u2"), C("u0"), a2, lt8)
    lin(C("u3"), K("e16", 13), 1536.0 * (4096 - 128) - 8192, C("u2"))
    lin(C("bL2"), K("e16", 15), HALF - 1536.0 * 128 - 8192, C("u3"))
    lin(C("u4"), K("le4", 1), 2.0, -1.0)
    ts(C("u5"), a0, a1, None, A.subtract)
    lin(C("na2"), C("u4"), a3, C("u5"))
    lin(C("sub"), r, 4096.0, HALF - 15 * 4096.0)
    ts(R("scn", 0, HM), R("scn", 0, HM), r, 135168.0, A.is_gt, A.mult)
    lin(R("scn", 0, HM), R("scn", 0, HM), 1.0, -131072.0)
    ts(R("tmp", 16, 32), q16, 4.0, b_, A.min, A.subtract)
    ts(R("tab", 0, 16), R("tmp", 16, 32), 0.0, a2, A.max, A.mult)
    for m0, m1 in CFG["LAY"]:
        n = xo(m1) - xo(m0) - (1 if m1 <= 2 else 0)
        copy("S", R("mt", 16 * xo(m0), 16 * (xo(m0) + n)), IND(R("bt", 0, 16 * (m1 + 1)), R("xu", xo(m0), xo(m0) + n)))
    lin(R("hbm", 0, 128), M("Blk"), C("h32"))
    for t, col in (("l3v", C("na2")), ("nv1", C("nv"))):
        lin(R(t, 0, 128), M("Blk"), col)
    eye, ni, slot = R("eye", 0, 128), R("ni", 0, 128), [[-16, 8], [0, 16]]
    iota(eye, [[-1, 128]], 1, 1)
    sel(eye, eye, [[-1, 128]], 0, 1, A.is_equal)
    sel(ni, eye, [[-1, 128]], 0, 1, A.not_equal, -1.0)
    sel(R("k2", 0, 128), M("Blk"), slot, -2, 1, A.is_equal)
    zq, z3, zd, uw = R("mt", 0, 144), R("Zq3", 0, 144), R("Zd", 0, 144), R("Uw", 0, 128)
    sel(z3, zq, [[0, 9], [1, 16]], -15, 0, A.not_equal)
    sel(zd, z3, [[-16, 9], [256, 4], [0, 4]], -12 - 768, 1, A.not_equal, -1.0)
    sel(uw, R("k2", 0, 128), [[-16, 8], [-4, 4], [256, 4]], -768, 1, A.not_equal, 1.0)
    sel(zd, zd, [[0, 9], [1, 16]], -15, 0, A.not_equal)
    sel(R("l3j", 0, 128), M("Blk"), slot, -8, 1, A.is_equal)
    sel(R("lzj", 0, 128), R("l3j", 0, 128), slot, -11, 1, A.not_equal, -256.0)
    cp(R("jl", 0, 14), R("j32", 0, 14))
    copy("S", R("l2o", 0, NL), IND(R("tab", 0, 16), R("jl", 0, 14)))

    def PS(name, b, n=None):
        h, region[0] = HS[b], name
        if name == "zT":
            return top(R("ps%d" % (2 * b + 1), 384, 512), h)
        k, c = {"WQ": (0, 0), "U": (0, 1), "DF": (0, 2), "B3": (2, 0), "E": (2, 2), "L2": (0, 4), "B2": (1, 1), "D3": (1, 1), "U2": (1, 2), "L1": (1, 2),
                "L3": (1, 0), "d": (1, 3), "c4": (1, 1), "c": (2, 1), "s": (0, 0), "r": (0, 5), "z": (1, 5), "Z": CFG["ZB"], "LJ": CFG["LJB"]}[name]
        return R("ps%d" % (2 * b + k if k < 2 else 6 + b % 2), c * h, c * h + (h if n is None else n))

    def chunks(h, n, first=0):
        if first and n > 1:
            return [(0, first)] + [(first + l0, first + l1) for l0, l1 in chunks(h - first, n - 1)]
        e = [2 * ((h * k // n + 1) // 2) for k in range(n)] + [h]
        return [(e[k], e[k + 1]) for k in range(n)]

    def crep(b, st=1, at=0, l0=0, l1=None):
        return R("cr", 20 * OFF[b] + 16 * l0 + at, 20 * OFF[b] + 16 * (HS[b] if l1 is None else l1), st)

    def cone(b, l0=0):
        return R("cr", 20 * OFF[b] + 16 * HS[b] + 4 * l0, 20 * (OFF[b] + HS[b]), 4)

    def move(eng, o, i):
        if eng == "G":
            sel(o, i, [[0, ncols(o)]], 0, 0)
        else:
            copy(eng, o, i)

    def repeat(b, engs, st):
        for eng in engs:
            move(eng, crep(b, st, st // 2), crep(b, st))
            st //= 2

    def sign_of_change(b, k):
        h, o = HS[b], OFF[b]
        y = R("yy%d" % (k + 1), o, o + h)
        add("N", "recv", (k, b), [], [y], 0, after=("send", k, b))
        mm(PS("d", b), [(R("ni", 0, 128), R("xx%d" % k, 16 * (LOFF[b] + h), 16 * (LOFF[b] + h) + h))], [(M("I"), y)])
        either("S", lambda: act(R("sd", o, o + h), PS("d", b), F.Sign),
               lambda: ts(R("sd", o, o + h), PS("d", b), -1.0, 1.0, A.max, A.min))

    def vlist(b):
        at = LOFF[b] + HS[b] + HS[b] // 4
        return R("lst", at, at + HS[b] // 16)

    for b in range(NB):
        cp(vlist(b), R("v32", OFF[b] // 16, (OFF[b] + HS[b]) // 16))
    for b in range(NB):
        move(CFG["REP0"][b][0], crep(b, 16), R("cc", OFF[b], OFF[b] + HS[b]))
        repeat(b, CFG["REP0"][b][1:], 16)
        move(CFG["ONE"][b], cone(b), R("cc", OFF[b], OFF[b] + HS[b]))
    xw, win = R("xw", 0, NV), R("win", 0, NV)
    for s in range(STEPS):
        for b in range(NB):
            h, o, lo = HS[b], OFF[b], LOFF[b]
            age[0] = (s, b)

            def W(buf, f=1, c0=0, st=1):
                return R(buf, f * o + c0, f * (o + h), st)
            wat, end, mode = LW[b] - h // 4, LW[b], (MODE[s].split("/") * NB)[b]
            vk, ul, wq = vlist(b), R("lst", lo, lo + h), R("lst", lo + h, lo + h + h // 4)
            p0, fresh, keep = 16 * lo, s in (2, 4), CFG["NR"][s] == "N"
            pv, y = R("pp", p0 + 20 * h, p0 + 21 * h), W("yy%d" % (s // 2))
            sg, su = R("sg", 2 * o, 2 * o + h), R("sg", 2 * o + h, 2 * o + 2 * h)
            xx, ct = "xx%d" % (s // 2 - 1 if fresh else 3), top(R("ct", 128 * b, 128 * b + 128), h)
            ident = top(R("eye", 0, h), h)

            def weigh(l0, l1, weights):
                tt(R("pp", p0 + 16 * l0, p0 + 16 * l1), IND(xw, R("lst", lo + l0, lo + l1)), weights, A.mult)

            def second(name, first, st):
                mm(PS(name, b), [(M("B2%d" % m), R("pp", first(m), first(m) + st * h, st)) for m in range(4)] + [(M("B2v"), pv)])
                act(su, PS(name, b), F.Sign, C("bS"))
            lin(W("w1"), IND(win, vk), 1.0, -float(HALF), "S")
            mm(PS("WQ", b, h // 4), [(M("Zq", 12 - 4 * k), W("w1", 1, k, 4)) for k in range(4)])
            lin(wq, PS("WQ", b, h // 4), 1.0, float(HALF), eng=(CFG["WQ"] * 6)[s])
            lin(W("gg", 4), IND(win, wq), 1.0, -float(HALF), "S")
            if not fresh:
                weigh(h, h + 5 * h // 16, R("cr", 20 * o, 20 * (o + h), 4))
                second("B2", lambda m: p0 + 16 * h + m, 4)
                mm(PS("U", b), [(M("Zq", 12 - 4 * i), W("gg", 4, i, 4)) for i in range(4)])
                lin(ul, PS("U", b), 1.0, float(HALF), eng=(CFG["UL"] * 6)[s])
            mm(PS("E", b), [(R("nv1", 0, 128), W("w1"))], [(M("Zq", 12 - 4 * i), W("gg", 4, i, 4)) for i in range(4)])
            if (CFG["EQN"][s] * NB)[b] == "V":
                ts(W("eq"), PS("E", b), 0.0, None, A.is_equal)
            else:
                act(W("ab"), PS("E", b), F.Abs)
                either("S", lambda: act(W("eq"), W("ab"), F.Relu, 1.0, -1.0),
                       lambda: ts(W("eq"), W("ab"), 0.0, None, A.is_equal))
            if fresh:
                mm(PS("D3", b), [(M("Zd", 12 - 4 * i), W("gg", 4, i, 4)) for i in range(4)])
                mm(PS("U", b), [(M("Uw"), W("w1"))], [(M("Zq3", 12 - 4 * i), W("gg", 4, i, 4)) for i in range(4)])
                tt(W("t32"), PS("D3", b), W("eq"), A.mult)
                tt(ul, PS("U", b), W("t32"), A.subtract)
            late = h
            for (l0, l1), m in zip(chunks(h, len(mode), (CFG["WL"] * NB)[b] if fresh else CFG["VL"]), mode):
                if m == "V":
                    weigh(l0, l1, crep(b, 1, 0, l0, l1))
                else:
                    late = min(late, l0)
                    copy("S" if m == "S" else "V", R(xx, p0 + 16 * l0, p0 + 16 * l1), IND(xw, R("lst", lo + l0, lo + l1)))
            if fresh:
                sign_of_change(b, s // 2 - 1)
                mm(PS("z", b), [(M("I"), cone(b))], [(M("I"), W("sd"))])
                ts(cone(b), PS("z", b), -15.0, 15.0, A.max, A.min)
            if late < h:
                c4 = PS("c4", b, 4 * (h - late))
                add("P", "mm", (c4, [(M("I"), cone(b, late), True, True, R(c4[0], c4[1] + k, c4[2], 4)) for k in range(4)]),
                    [M("I"), cone(b, late)], [c4], 4 * (10 + max(64, h - late) * pe))
            if fresh:
                move(CFG["REP"][0], crep(b, 16), cone(b))
                repeat(b, CFG["REP"][1:], 16)
                tt(pv, c4[:3] + (4,) + c4[4:], R(xx, p0 + 16 * h, p0 + 17 * h), A.mult)
            if late < h:
                for k in (3, 0, 1, 2):
                    tt(R("pp", p0 + 16 * late + k, p0 + 16 * h, 4), c4, R(xx, p0 + 16 * late + k, p0 + 16 * h, 4), A.mult)
                    if fresh and k == 3:
                        second("B3", lambda m: p0 + 4 * m + 3, 16)
            if s % 2 == 0:
                mm(PS("s", b), [(R("hbm", 0, 128), y)])
                lin(W("qq"), PS("s", b), C("sq"), C("bq"), "S")
            sums = [(M("Zs", 15 - m), R("pp", p0 + m, p0 + 16 * h, 16)) for m in range(16)]
            units = [sums[k::4] for k in (3, 0, 1, 2)] if late < h else [sums[k::CFG["DFS"]] for k in range(CFG["DFS"])]
            mm(PS("DF", b), [(M("Teq"), W("eq")), (M("Blk"), pv)], *units)
            act(sg, PS("DF", b), F.Sign, -0.5)
            mm(PS("L1", b), [(M("L1J"), W("l2o")), (M("L1eq"), W("eq")), (M("L1su"), su)],
               [(M("L1sg"), sg)])
            relu(W("l1o"), PS("L1", b), C("bL1"))
            mm(PS("L2", b), [(M("L2w"), W("w1")), (M("L2J"), W("l2o")), (M("L2y"), y), (M("L2r"), W("qq"))],
               [(M("L2l"), W("l1o"))])
            if s == STEPS - 1:
                mm(PS("Z", b), [(R("lzj", 0, 128), W("l2o"))], [(M("L2l"), W("l1o"))])
                relu(W("zo"), PS("Z", b))
            relu(W("l2o"), PS("L2", b), C("bL2"))
            mm(PS("L3", b), [(R("l3v", 0, 128), W("l2o"))])
            add("V", "scan", (W("sc"), R("scn", 0, h), PS("L3", b)), [R("scn", 0, h), PS("L3", b)], [W("sc")],
                fix + max(64, h) * cyc)
            lin(vk, W("sc", 1, 15, 16), 1.0, C("sub"), eng="V" if (s, b) == (STEPS - 1, NB - 1) else (CFG["VK"] * 6)[s])
            if s % 2 == 1:
                k = s // 2
                xv = R("xx%d" % k, p0 + 16 * h, p0 + 17 * h)
                copy("V" if (s, b) == (STEPS - 1, NB - 1) else (CFG["XV"] * 3)[k], xv, IND(xw, vk))
                add("G", "send", (k, b), [xv], [], 300, done=rate["rlat"], key=("send", k, b))
            if s == STEPS - 1:
                lin(W("vsb"), PS("L3", b), 1.0, float(HALF), "S")
                mm(PS("LJ", b), [(R("l3j", 0, 128), W("l2o"))])
                tt(W("jo32"), PS("LJ", b), W("zo"), A.add)
    dma("Y", R("vo", 0, NL, 1, 0, 8), R("vsb", 0, NL, 1, 0, 128, 16), "out")
    dma("Y", R("jo", 0, NL, 1, 0, 8), R("jo32", 0, NL, 1, 12, 128, 16), "out")
    for b in range(NB):
        h, o = HS[b], OFF[b]
        age[0] = (STEPS, b)
        if b < NB - 1:
            sign_of_change(b, 2)
            mm(PS("z", b), [(M("I"), cone(b))], [(M("I"), R("sd", o, o + h))])
            ts(R("co32", o, o + h), PS("z", b), -15.0, 15.0, A.max, A.min)
        else:
            y, hi = R("yy3", o, o + h), R("ps7", 256, 256 + h)
            add("N", "recv", (2, b), [], [y], 0, after=("send", 2, b))
            ts(R("eq", o, o + h), cone(b), -1.0, -15.0, A.add, A.max)
            ts(hi, cone(b), 1.0, 15.0, A.add, A.min)
            mm(PS("d", b), [(M("I"), cone(b)), (R("ni", 0, 128), R("xx2", 16 * (LOFF[b] + h), 16 * (LOFF[b] + h) + h))],
               [(M("I"), y)])
            tt(R("sd", o, o + h), PS("d", b), R("eq", o, o + h), A.max)
            tt(R("co32", o, o + h), hi, R("sd", o, o + h), A.min)
        dma("Y", R("co", o, o + h), R("co32", o, o + h), "out")
    return ops


def overlap(x, y):
    if x[1] >= y[2] or y[1] >= x[2]:
        return False
    if x[3] > 1 and y[3] > 1 and not set(range(*x[1:4])) & set(range(*y[1:4])):
        return False
    return bool(set(range(x[4], x[5], x[6])) & set(range(y[4], y[5], y[6])))


def link(ops):
    hist, bank, keys = {}, {}, {}
    for d in ops:
        deps, order = set(), set()
        use = [(x, False) for x in d["rd"] if x[0] not in DRAM] + [(x, True) for x in d["wr"] if x[0] not in DRAM]
        for reg, w in use:
            for e, ereg, ew in hist.get(reg[0], []):
                if (w or ew) and overlap(reg, ereg):
                    (order if e["eng"] == d["eng"] == "P" else deps).add(e["id"])
            if reg[0].startswith("ps"):
                for en, e in bank.setdefault(reg[0], {}).items():
                    (order if en == d["eng"] and "alt" not in d else deps).add(e["id"])
        for reg, w in use:
            hl = hist.setdefault(reg[0], [])
            if w and reg[3:] == (1, 0, 128, 1):
                hl[:] = [z for z in hl if not (z[1][1] >= reg[1] and z[1][2] <= reg[2])]
            hl.append((d, reg, w))
            if reg[0].startswith("ps"):
                bank[reg[0]]["either" if "alt" in d else d["eng"]] = d
        if d.get("kept"):
            order |= {keys[d["eng"]]} if d["eng"] in keys else set()
            keys[d["eng"]] = d["id"]
        if "key" in d:
            keys[d["key"]] = d["id"]
        d["soft"] = [keys[d["after"]]] if "after" in d else []
        d["deps"], d["order"] = ([] if d["kind"] == "recv" else sorted(deps)), sorted(order - deps)


def schedule(ops, rate):
    lat, eps, n = rate["lat"], CFG["eps"], len(ops)
    succ = [[] for _ in range(n)]
    for d in ops:
        for e in d["deps"] + d["soft"]:
            succ[e].append((d["id"], True))
        for e in d["order"]:
            succ[e].append((d["id"], False))
    prio = [0.0] * n
    for d in reversed(ops):
        full = d["cost"] + d["done"] + (d["busy"] + rate["d0"] if d["busy"] else 0)
        prio[d["id"]] = max([full] + [(full + lat if h else d["cost"]) + prio[j] for j, h in succ[d["id"]]])
    left = [len(d["deps"]) + len(d["soft"]) + len(d["order"]) for d in ops]
    rdy = [0.0] * n
    free, pipe = {e: 0.0 for e in "VSPGYN"}, 0.0
    pool = {e: [d["id"] for d in ops if d["eng"] == e and left[d["id"]] == 0] for e in free}
    seq = []
    while len(seq) < n:
        t, e = min((max(free[e], min([rdy[i] for i in pool[e]])), e) for e in pool if pool[e])
        i = max([j for j in pool[e] if rdy[j] <= t + eps], key=lambda j: prio[j])
        pool[e].remove(i)
        d = ops[i]
        t0 = max(free[e], rdy[i])
        free[e] = t1 = t0 + d["cost"]
        if d["busy"]:
            pipe = t1 = max(pipe, t1 + rate["d0"]) + d["busy"]
        seq.append(d)
        d["t0"], d["t1"] = t0, t1 + d["done"] + lat
        for j, h in succ[i]:
            rdy[j] = max(rdy[j], t1 + d["done"] + lat if h else t0)
            left[j] -= 1
            if left[j] == 0:
                pool[ops[j]["eng"]].append(j)
    return seq


def stagger(ops, rate):
    schedule(ops, rate)
    free, t0, t1, off = {}, {}, {}, {}

    def start(turn):
        return CFG["T0"] + CFG["T3"] * (NB * turn[0] + turn[1]) + CFG["TX"] * (turn[0] // 2)
    for d in ops:
        i = d["id"]
        if d["turn"] is None:
            t0[i], t1[i] = d["t0"], d["t1"]
            continue
        s, b = d["turn"]
        t = max([free.get((d["eng"], b), 0.0)] + [t1[e] for e in d["deps"] + d["soft"]] + [t0[e] + 1 for e in d["order"]])
        if d["tag"] == ("PU1" if CFG["NR"][min(s, STEPS - 1)] == "N" else "PU2"):
            t = max(t, start(d["turn"]))
        t0[i], free[d["eng"], b] = t, t + d["cost"]
        t1[i] = t + d["cost"] + d["done"] + rate["lat"] + (d["busy"] + rate["d0"] if d["busy"] else 0)
        if b == 0:
            off[s, d["tag"]] = t - start(d["turn"])
    at = []
    for d in ops:
        t = t0[d["id"]] if d["turn"] is None else start(d["turn"]) + off.get((d["turn"][0], d["tag"]), 0.0)
        at.append(max([t] + [at[e] + 1 for e in d["deps"] + d["soft"] + d["order"]]))
    return [ops[i] for i in sorted(range(len(ops)), key=lambda i: at[i])]


def worth(ends):
    return 3 * (sum((t / z["scale"]) ** 8 for t, z in zip(ends, RATES)) / len(RATES)) ** 0.125


def draws(seed):
    z = [seed]

    def rnd():
        z[0] = (z[0] * 1103515245 + 12345) % 2147483648
        return (z[0] >> 7) / 16777216.0
    return rnd


def justify(ops, seq, rate):
    n, rnd = len(ops), draws(CFG["SEED"])
    span, held, put = timer(ops)

    cost, eng = [d["cost"] for d in ops], ["VSPGYN".index(d["eng"]) for d in ops]
    lag = [d["done"] + rate["lat"] + (d["busy"] + rate["d0"] if d["busy"] else 0) for d in ops]
    order = [d["id"] for d in seq]
    t1, free, key = span(order)[1][0], [0.0] * 6, [0.0] * n
    for i in order:
        key[i] = max([free[eng[i]]] + [t1[e] for e in ops[i]["deps"] + ops[i]["soft"]])
        free[eng[i]] = key[i] + cost[i]
        if ops[i].get("kept"):
            lag[i] = t1[i] - free[eng[i]]
    pre = [[(e, lag[e]) for e in d["deps"] + d["soft"]] + [(e, 0.0) for e in d["order"]] for d in ops]
    suc = [[] for _ in ops]
    for i in range(n):
        for e, g in pre[i]:
            suc[e].append((i, g))

    def rank(key, edges):
        at = [0.0] * n
        for i in (range(n) if edges is pre else range(n - 1, -1, -1)):
            t = key[i]
            for e, g in edges[i]:
                if at[e] >= t:
                    t = at[e] + 1e-3
            at[i] = t
        return sorted(range(n), key=lambda i: at[i])

    def pack(key, edges, first):
        st, en, end = [[] for _ in range(6)], [[] for _ in range(6)], [0.0] * n
        for i in rank(key, edges):
            t, c = first[i], cost[i]
            for e, g in edges[i]:
                if end[e] + g > t:
                    t = end[e] + g
            if c > 0:
                a, b = st[eng[i]], en[eng[i]]
                k = m = len(a)
                while k and b[k - 1] > t:
                    k -= 1
                while k < m and a[k] < t + c - 1e-6:
                    t = b[k]
                    k += 1
                a.insert(k, t)
                b.insert(k, t + c)
            end[i] = t + c
        return end

    def both(key):
        zero, best = [0.0] * n, None
        end = pack(key, pre, zero)
        while True:
            whole = max([e + g for e, g in zip(end, lag)])
            if best is not None and whole >= best[0] - 5:
                return best
            best = (whole, [e - c for e, c in zip(end, cost)])
            end = pack([-e for e in pack([-e for e in end], suc, lag)], pre, zero)

    def swap(calls):
        for i in calls:
            eng[i] = 1 - eng[i]
            put(i, "VS"[eng[i]])
            cost[i] = ops[i]["cost"]
    whole, st = both(key)
    keep, where, free_to_move, late = rank(st, pre), list(eng), [d["id"] for d in ops if "alt" in d], []
    now = best = worth(span(keep)[0])
    for it in range(CFG["SHAKES"]):
        c, w = rnd() * whole, (3000.0, 8000.0, 20000.0)[it % 3]
        pool = free_to_move if it % 3 == 0 else (late or free_to_move)
        moved = {pool[int(rnd() * len(pool))] for _ in range(CFG["FLIPS"][it % len(CFG["FLIPS"])])}
        swap(moved)
        shake = CFG["DEN"] / w if not moved or it % 2 else 0.0
        whole, new = both([x + ((rnd() + rnd() - 1) * CFG["AMP"] if abs(x - c) < w and rnd() < shake else 0) for x in st])
        order = rank(new, pre)
        ends, t1 = span(order)
        s = worth(ends)
        if s <= now + CFG["TH"] * (1 - it / CFG["SHAKES"]) * rnd():
            now, st, late = s, new, [i for i in held(order, t1, True) if "alt" in ops[i]]
            if s < best:
                best, keep, where = s, order, list(eng)
        else:
            swap(moved)
    swap([i for i in free_to_move if eng[i] != where[i]])
    return [ops[i] for i in keep]


def timer(ops):
    built = [build_ops(z) for z in RATES]
    sets = [([d["cost"] for d in o], [d["done"] + z["lat"] for d in o], [d["busy"] for d in o], z["d0"])
            for o, z in zip(built, RATES)]
    hard = [d["deps"] + d["soft"] for d in ops]
    eng, n = ["VSPGYN".index(d["eng"]) for d in ops], len(ops)

    def put(i, e):
        d = ops[i]
        eng[i], d["eng"] = "VS".index(e), e
        d["kind"], d["args"], d["cost"] = d["alt"][e]
        for o, z in zip(built, sets):
            z[0][i] = o[i]["alt"][e][2]
    for d in ops:
        if "alt" in d:
            put(d["id"], d["eng"])

    def span(order, at=0, old=None):
        ends, all_t1 = [], []
        for k, (cost, done, busy, d0) in enumerate(sets):
            free, t1, pipe = [0.0] * 6, (list(old[k]) if at else [0.0] * (2 * len(ops))), 0.0
            seen, j = set(), at - 1
            while j >= 0 and len(seen) < 7:
                i = order[j]
                if eng[i] not in seen:
                    seen.add(eng[i])
                    free[eng[i]] = t1[n + i]
                if busy[i] and 6 not in seen:
                    seen.add(6)
                    pipe = t1[i] - done[i]
                j -= 1
            for i in order[at:]:
                t = free[eng[i]]
                for e in hard[i]:
                    if t1[e] > t:
                        t = t1[e]
                t += cost[i]
                free[eng[i]] = t1[n + i] = t
                if busy[i]:
                    pipe = t = max(pipe, t + d0) + busy[i]
                t1[i] = t + done[i]
            ends.append(max(t1))
            all_t1.append(t1)
        return ends, all_t1

    def held(order, all_t1, both=False):
        before, last, out = {}, {}, []
        for i in order:
            before[i] = last.get(eng[i])
            last[eng[i]] = i
        for (cost, done, busy, d0), t1 in zip(sets, all_t1):
            i = t1.index(max(t1))
            while i is not None:
                e = max(hard[i], key=lambda j: t1[j]) if hard[i] else None
                p = before[i]
                if p is not None and (e is None or t1[n + p] >= t1[e]):
                    out += [i, p] if both else [i]
                    e = p
                i = e
        return out
    return span, held, put


def polish(ops, seq):
    span, held, put = timer(ops)
    pre = [set(d["deps"] + d["soft"] + d["order"]) for d in ops]
    eng = [d["eng"] for d in ops]
    order = [d["id"] for d in seq]
    ends, t1 = span(order)
    now = best = worth(ends)
    keep, where, rnd, moves = order, list(eng), draws(CFG["SEED"]), CFG["MOVES"]
    pick = held(order, t1)
    for it in range(moves):
        d = pick[int(rnd() * len(pick))] if it % 5 else order[int(rnd() * len(order))]
        k = (1, 1, 1, 2, 2, 3)[int(rnd() * 6)]
        i = j = order.index(d)
        if eng[d] == "N" or ops[d].get("kept"):
            continue
        if "alt" in ops[d] and it % 4 == 0:
            put(d, "VS"[eng[d] == "V"])
            ends, new = span(order, i, t1)
            s = worth(ends)
            if s <= now + CFG["HEAT"] * (1 - it / moves) * rnd() ** 2:
                now, t1, pick, eng[d] = s, new, held(order, new), ops[d]["eng"]
                if s < best:
                    best, keep, where = s, order, list(eng)
            else:
                put(d, eng[d])
            continue
        while k and j > 0:
            j -= 1
            k -= 1 if eng[order[j]] == eng[d] else 0
        need, mv = set(pre[d]), set()
        for e in reversed(order[j:i]):
            if e in need:
                mv.add(e)
                need |= pre[e]
        if k or order[j] in mv or ops[order[j]].get("kept"):
            continue
        c = order[:j] + [e for e in order[j:i] if e in mv] + [d] + [e for e in order[j:i] if e not in mv] + order[i + 1:]
        ends, new = span(c, j, t1)
        s = worth(ends)
        if s <= now + CFG["HEAT"] * (1 - it / moves) * rnd() ** 2:
            order, now, t1, pick = c, s, new, held(c, new)
            if s < best:
                best, keep, where = s, c, list(eng)
    for d in ops:
        if "alt" in d:
            put(d["id"], where[d["id"]])
    return [ops[i] for i in keep]


def plan_waits(ops, seq):
    cnt, known, most, nd = {}, {e: {} for e in "VSPGY"}, {}, 0
    place = {d["id"]: i for i, d in enumerate(seq)}
    for d in seq:
        if d["kind"] == "recv":
            d["sig"], d["know"] = ("ya%d_%d" % d["args"], CFG["NENG"]), {}
            continue
        kn, need = known[d["eng"]], {}
        for e in sorted(d["deps"], key=lambda j: -place[j]):
            s, v = ops[e]["sig"]
            if kn.get(s, 0) < v:
                need[s] = max(need.get(s, 0), v)
                kn[s] = v
                for s2, v2 in ops[e]["know"].items():
                    kn[s2] = max(kn.get(s2, 0), v2)
        d["waits"] = sorted(need.items())
        for s, v in d["waits"]:
            most[s] = max(most.get(s, 0), v)
        d["know"] = dict(kn)
        if d["kind"] == "dma":
            s, inc = d["sem"] or "d%d" % nd, 16
            nd += 1
        elif d["kind"] == "send":
            s, inc = "sent", CFG["NENG"]
        else:
            s, inc = "e" + d["eng"], len(d["args"][1]) if d["kind"] == "mm" else 1
        cnt[s] = cnt.get(s, 0) + inc
        d["sig"] = (s, cnt[s])
    final = sorted([(s, v) for s, v in cnt.items() if most.get(s, 0) < v], key=lambda z: z[0] == "out")
    return final, sorted(cnt) + ["ya%d_%d" % (k, b) for k in range(3) for b in range(NB)]


OPS = build_ops(RATES[0])
link(OPS)
SEQ = polish(OPS, justify(OPS, stagger(OPS, RATES[0]), RATES[0]))
FINAL, SEMAPHORES = plan_waits(OPS, SEQ)


def rank_program(g, core, T, topo):
    rank = T.rank_of(core)
    if rank is None:
        return
    nxt = T.cores[(rank + 1) % len(T.cores)]
    rid, pid = topo.addr(nxt, core)
    mask = sum(1 << e for e in topo.engines(core, nxt)[:CFG["NENG"]])
    queue = {"V": g.vector, "S": g.scalar, "P": g.tensor, "G": g, "Y": g.sync}

    def ap(r):
        if not isreg(r):
            return r
        if r[0] == "ind":
            return ap(r[1]).indirect(ap(r[2]))
        if r[0] == "h":
            return T["h"][:]
        return T[r[0]][slice(r[4], r[5], r[6] if r[6] > 1 else None), slice(r[1], r[1] + (ncols(r) - 1) * r[3] + 1, r[3] if r[3] > 1 else None)]

    for d in SEQ:
        k = d["kind"]
        if k == "recv":
            continue
        a = [ap(z) for z in d["args"]]
        q = queue[d["eng"]]
        for s, v in d["waits"]:
            q.wait_ge(T.sem[s], v)
        if k == "send":
            o, h = OFF[a[1]], HS[a[1]]
            g.remote_dma(ap(R("yy%d" % (a[0] + 1), o, o + h)), ap(d["rd"][0]),
                         T.sem["ya%d_%d" % d["args"]], T.sem["sent"], pid, rid, mask)
            continue
        if k == "cp":
            ins = q.tensor_copy(*a)
        elif k == "ts":
            ins = q.tensor_scalar(*(a[:5] if a[5] is None else a))
        elif k == "tt":
            ins = q.tensor_tensor(*a)
        elif k == "ms":
            ins = q.memset(*a)
        elif k == "scan":
            ins = q.tensor_tensor_scan(a[0], a[1], a[2], 0.0, A.add, A.max)
        elif k == "act":
            ins = q.activation(*a[:3]) if a[2] == F.Copy else q.activation(*a[:3], bias=a[3], scale=a[4])
        elif k == "mm":
            for z in a[1]:
                q.matmul(ap(z[4]) if len(z) > 4 else a[0], ap(z[0]), ap(z[1]), z[2], z[3]).then_inc(T.sem["eP"], 1)
            continue
        elif k == "iota":
            ins = q.iota(*a) if SCRATCH[d["args"][0][0]][2] == I32 else q.iota(*a, allow_small_or_imprecise_dtypes=True)
        elif k == "sel":
            ins = q.affine_select(a[0], a[1], a[2], a[3], a[6], a[4], a[5])
        else:
            ins = q.dma_start(*a)
        ins.then_inc(T.sem[d["sig"][0]], 16 if k == "dma" else 1)
    for s, v in FINAL:
        g.wait_ge(T.sem[s], v)
